import numpy as np
import ml_dtypes


def mxq(x, axis, fmt="e4m3"):
    dtype, down = {"e4m3": (ml_dtypes.float8_e4m3fn, 7), "e5m2": (ml_dtypes.float8_e5m2, 14)}[fmt]
    v = np.moveaxis(np.asarray(x, np.float32).astype(ml_dtypes.bfloat16).astype(np.float64), axis, -1)
    blocks = v.reshape(v.shape[:-1] + (-1, 32))
    amax = np.abs(blocks).max(-1, keepdims=True)
    byte = np.maximum(np.where(amax > 0, np.frexp(amax)[1] - 1 + 127, 0) - down, 1)
    scale = np.exp2(byte - 127.0)
    codes = (blocks / scale).astype(np.float32).astype(dtype).astype(np.float64)
    return np.moveaxis((codes * scale).reshape(v.shape), -1, axis)


WIDE = False


def mx_kscale(k):
    if not WIDE:
        return np.ones(k)
    levels = np.array([30, -30])
    if k % 512:
        return np.exp2(np.random.permutation(np.resize(levels, k // 32))).repeat(32)
    a = np.empty((k // 512, 16))
    for p in range(k // 512):
        a[p, :8] = np.random.permutation(np.resize(levels, 8))
        for g in range(8):
            far = levels[np.abs(levels - a[p, g]) >= 10]
            a[p, g + 8] = far[np.random.randint(len(far))]
    return np.exp2(a.ravel()).repeat(32)


def f64(x):
    return np.asarray(x).astype(np.float64)


def striped(idx):
    return np.tile(idx.reshape(-1, 16).T, (8, 1)).astype(np.uint16)


def unstriped(offs):
    return offs[:16].T.reshape(-1).astype(np.int64)


def d_silu(v):
    s = 1.0 / (1.0 + np.exp(-np.maximum(v, -700.0)))
    return s * (1.0 + v * (1.0 - s))


K, T, E, C, H, N = 128, 1536, 2, 512, 1024, 512


def by_expert(wq, xq):
    return np.concatenate([wq[e].T @ xq[:, e * C:(e + 1) * C] for e in range(E)], axis=1)


def setup_inputs():
    n = np.random.standard_normal
    s = mx_kscale(N)[:, None]
    u = mx_kscale(H)
    return {
        "dyT": (n((N, T)) * s).astype(np.float32),
        "a": n((H, E * C)).astype(np.float32),
        "w2": (n((E, N, H)) / np.sqrt(N) / s[None] * u[None, None, :]).astype(np.float32),
        "w1": (n((E, H, K)) / np.sqrt(H) / u[None, :, None]).astype(np.float32),
        "gate": np.tile(np.random.uniform(0.2, 1.0, E * C), (N, 1)).astype(np.float32),
        "offs": striped(np.random.permutation(T)[:E * C]),
    }


def reference(dyT, a, w2, w1, gate, offs):
    idx = unstriped(offs)
    gq = mxq(f64(gate) * f64(dyT)[:, idx], 0, "e5m2")
    dh = by_expert(mxq(f64(w2), 1, "e4m3"), gq)
    da = dh * d_silu(f64(a))
    dx = by_expert(mxq(f64(w1), 1, "e4m3"), mxq(da, 0, "e5m2"))
    out = np.zeros((K, T))
    out[:, idx] = dx
    return out

@@ -1,0 +1,263 @@
+from contextlib import ExitStack
+
+import concourse.mybir as mybir
+
+F32 = mybir.dt.float32
+BF16 = mybir.dt.bfloat16
+U32 = mybir.dt.uint32
+U16 = mybir.dt.uint16
+U8 = mybir.dt.uint8
+E4M3 = mybir.dt.float8_e4m3fn_x4
+E5M2 = mybir.dt.float8_e5m2_x4
+ADD = mybir.AluOpType.add
+MULT = mybir.AluOpType.mult
+COPY = mybir.ActivationFunctionType.Copy
+SIGMOID = mybir.ActivationFunctionType.Sigmoid
+SILU = mybir.ActivationFunctionType.Silu
+
+P = 128
+K, T, E, C, H, N = 128, 1536, 2, 512, 1024, 512
+S = E * C
+PACK = 4
+PASS = P * PACK
+HALVES = H // PASS
+RUN = 4
+
+FLOPS = 2 * S * N * H + 2 * S * H * K
+BYTES = 4 * (N * T + H * S + E * N * H + E * H * K + S + K * T) + 2 * S
+
+
+def tile_moe_bdx_mlp_silu_kernel(tc, dyT, a, w2, w1, gate, offs, out):
+    nc = tc.nc
+    dy_rows = dyT.rearrange("(p t) s -> p t s", t=PACK)
+    a_rows = a.rearrange("(h p t) s -> p h t s", h=HALVES, t=PACK)
+    w2_rows = w2.rearrange("e (p j) i -> p e j i", j=PACK)
+    w1_rows = w1.rearrange("e (h p j) k -> p (e h) j k", h=HALVES, j=PACK)
+    pairs = [(e, h) for h in range(HALVES) for e in range(E)]
+
+    with ExitStack() as ctx:
+        lists = ctx.enter_context(tc.tile_pool(name="lists", bufs=1))
+        keep = ctx.enter_context(tc.tile_pool(name="keep", bufs=1))
+        ring = ctx.enter_context(tc.tile_pool(name="ring", bufs=2))
+        dh_banks = ctx.enter_context(tc.psum_pool(name="dh_banks", bufs=6))
+        dx_banks = ctx.enter_context(tc.psum_pool(name="dx_banks", bufs=2))
+
+        offsets = lists.tile([P, S // 16], U16, name="offsets")
+        gates = keep.tile([P, S], F32, name="gates")
+        dy = [keep.tile([P, T], F32, name=f"dy{t}") for t in range(PACK)]
+        v = [keep.tile([P, PACK, S], F32, name=f"v{h}") for h in range(HALVES)]
+        d = [keep.tile([P, PACK, S], F32, name=f"d{h}") for h in range(HALVES)]
+        w2_raw = {x: keep.tile([P, PACK, PASS], F32, name=f"w2_raw{x[0]}{x[1]}") for x in pairs}
+        w1_raw = keep.tile([P, E * HALVES, PACK, K], F32, name="w1_raw")
+        g_rows = keep.tile([P, PACK, S], F32, name="g_rows")
+
+        g_words = [keep.tile([P, C, PACK], BF16, name=f"g_words{e}", align_bytes=64) for e in range(E)]
+        g_codes = [keep.tile([P, C], U32, name=f"g_codes{e}", align_bytes=64) for e in range(E)]
+        g_scales = [keep.tile([P, C], U8, name=f"g_scales{e}", align_bytes=64) for e in range(E)]
+        w2_words = {x: keep.tile([P, PACK, P, PACK], BF16, name=f"w2_words{x[0]}{x[1]}", align_bytes=64) for x in pairs}
+        w2_codes = {x: keep.tile([P, PASS], U32, name=f"w2_codes{x[0]}{x[1]}", align_bytes=64) for x in pairs}
+        w2_scales = {x: keep.tile([P, PASS], U8, name=f"w2_scales{x[0]}{x[1]}", align_bytes=64) for x in pairs}
+        w1_words = keep.tile([P, E * HALVES, K, PACK], BF16, name="w1_words", align_bytes=64)
+        w1_codes = keep.tile([P, E * HALVES * K], U32, name="w1_codes", align_bytes=64)
+        w1_scales = keep.tile([P, E * HALVES * K], U8, name="w1_scales", align_bytes=64)
+        da_codes = {x: keep.tile([P, C], U32, name=f"da_codes{x[0]}{x[1]}", align_bytes=64) for x in pairs}
+        da_scales = {x: keep.tile([P, C], U8, name=f"da_scales{x[0]}{x[1]}", align_bytes=64) for x in pairs}
+        result = keep.tile([P, T], F32, name="result")
+        warm = keep.tile([P, 1], F32, name="warm")
+        zero = keep.tile([P, 1], F32, name="zero")
+
+
+        def load_a(h, t0, t1):
+            nc.sync.dma_start(v[h][:, t0:t1, :], a_rows[:, h, t0:t1, :])
+
+        def load_w2(e, h):
+            nc.sync.dma_start(w2_raw[e, h][:], w2_rows[:, e, :, h * PASS : (h + 1) * PASS])
+
+        def sigmoid(h, t):
+            nc.scalar.activation(d[h][:, t, :], v[h][:, t, :], SIGMOID, scale=(1.0, -1.0)[h])
+
+        def silu(t):
+            nc.scalar.activation(v[1][:, t, :], v[1][:, t, :], SILU, bias=zero[:])
+
+        def make_u(t):
+            nc.vector.scalar_tensor_tensor(v[0][:, t, :], d[0][:, t, :], -1.0, v[0][:, t, :], ADD, MULT)
+
+        def make_z(h, t):
+            nc.vector.scalar_tensor_tensor(d[h][:, t, :], v[h][:, t, :], -1.0, d[h][:, t, :], ADD, MULT)
+
+        last_step = [(-1.0, MULT), (1.0, ADD)]
+
+        def gather(t):
+            nc.vector.tensor_tensor(g_rows[:, t, :], dy[t][:].indirect(offsets[:]), gates[:], MULT)
+
+        def interleave(copy, words, planes):
+            copy(
+                words.rearrange("p (c i) t -> p c t i", i=RUN),
+                planes.rearrange("p t (c i) -> p c t i", i=RUN),
+            )
+
+        def lay_g(e):
+            interleave(nc.vector.tensor_copy, g_words[e][:], g_rows[:, :, e * C : (e + 1) * C])
+
+        def quantize_g(e):
+            nc.vector.quantize_mx(
+                out=g_codes[e][:].bitcast(E5M2), scales=g_scales[e][:], in_=g_words[e][:].rearrange("p c t -> p (c t)")
+            )
+
+        def lay_w2(e, h):
+            nc.scalar.copy(
+                w2_words[e, h][:].rearrange("p t m j -> p m j t"),
+                w2_raw[e, h][:].rearrange("p j (m t) -> p m j t", t=PACK),
+            )
+
+        def quantize_w2(e, h):
+            nc.vector.quantize_mx(
+                out=w2_codes[e, h][:].bitcast(E4M3),
+                scales=w2_scales[e, h][:],
+                in_=w2_words[e, h][:].rearrange("p t m j -> p (t m j)"),
+            )
+
+        def lay_w1():
+            for x in range(E * HALVES):
+                interleave(nc.scalar.copy, w1_words[:, x], w1_raw[:, x])
+
+        def quantize_w1():
+            nc.vector.quantize_mx(
+                out=w1_codes[:].bitcast(E4M3), scales=w1_scales[:], in_=w1_words[:].rearrange("p x k j -> p (x k j)")
+            )
+
+        da_planes = {}
+        da_words = {}
+
+        def make_da(e, h):
+            da_planes[e, h] = ring.tile([P, PACK, C], BF16, name="da_planes")
+            da_words[e, h] = ring.tile([P, C, PACK], BF16, name="da_words", align_bytes=64)
+            scalar, op = last_step[h]
+            for t in range(PACK):
+                dh = dh_banks.tile([P, C], F32, name="dh")
+                columns = slice(t * P, (t + 1) * P)
+                nc.tensor.matmul_mx(
+                    out=dh[:],
+                    lhsT=w2_codes[e, h][:, columns].bitcast(E4M3),
+                    lhsT_scale=w2_scales[e, h][:, columns],
+                    rhs=g_codes[e][:].bitcast(E5M2),
+                    rhs_scale=g_scales[e][:],
+                    start=True,
+                    stop=True,
+                )
+                nc.vector.scalar_tensor_tensor(
+                    da_planes[e, h][:, t, :], d[h][:, t, e * C : (e + 1) * C], scalar, dh[:], op, MULT
+                )
+
+        def lay_da(e, h, copy=nc.scalar.copy, c0=0, c1=C):
+            interleave(copy, da_words[e, h][:, c0:c1, :], da_planes[e, h][:, :, c0:c1])
+
+        def quantize_da(e, h):
+            nc.vector.quantize_mx(
+                out=da_codes[e, h][:].bitcast(E5M2),
+                scales=da_scales[e, h][:],
+                in_=da_words[e, h][:].rearrange("p c t -> p (c t)"),
+            )
+
+        dx = [dx_banks.tile([P, C], F32, name="dx") for e in range(E)]
+
+        def add_to_dx(e, h):
+            columns = slice((e * HALVES + h) * K, (e * HALVES + h + 1) * K)
+            nc.tensor.matmul_mx(
+                out=dx[e][:],
+                lhsT=w1_codes[:, columns].bitcast(E4M3),
+                lhsT_scale=w1_scales[:, columns],
+                rhs=da_codes[e, h][:].bitcast(E5M2),
+                rhs_scale=da_scales[e, h][:],
+                start=(h == 0),
+                stop=(h == HALVES - 1),
+            )
+
+        def put_back(e):
+            slots = ring.tile([P, C], F32, name="slots")
+            nc.scalar.copy(slots[:], dx[e][:])
+            nc.vector.tensor_copy(result[:].indirect(offsets[:, e * (C // 16) : (e + 1) * (C // 16)]), slots[:])
+
+
+        nc.sync.dma_start(offsets[:], offs)
+        load_a(0, 0, 1)
+        load_a(0, 1, 2)
+        load_a(0, 2, 4)
+        load_a(1, 0, 2)
+        nc.sync.dma_start(gates[:], gate[0:P, :])
+        nc.sync.dma_start(dy[0][:], dy_rows[:, 0, :])
+        load_a(1, 2, 4)
+        for t in range(1, PACK):
+            nc.sync.dma_start(dy[t][:], dy_rows[:, t, :])
+        for e, h in pairs:
+            load_w2(e, h)
+        nc.sync.dma_start(w1_raw[:], w1_rows)
+
+
+        nc.vector.memset(warm[:], 1.0)
+        nc.scalar.activation(warm[:], warm[:], SIGMOID)
+        nc.vector.memset(result[:], 0.0)
+
+        for t0 in (0, 2):
+            planes = range(t0, t0 + 2)
+            for t in planes:
+                sigmoid(0, t)
+            for t in planes:
+                make_u(t)
+            for t in planes:
+                make_z(0, t)
+
+        sigmoid(1, 0)
+        sigmoid(1, 1)
+        gather(0)
+        gather(1)
+        sigmoid(1, 2)
+        sigmoid(1, 3)
+        nc.scalar.activation(zero[:], d[1][:, PACK - 1, S - 1 : S], COPY, scale=0.0)
+        silu(0)
+        silu(1)
+        gather(2)
+        gather(3)
+        silu(2)
+        lay_w2(0, 0)
+        make_z(1, 0)
+        lay_g(0)
+        quantize_w2(0, 0)
+        lay_w2(1, 0)
+        lay_g(1)
+        quantize_g(0)
+        quantize_g(1)
+        quantize_w2(1, 0)
+
+        make_da(0, 0)
+        lay_w2(0, 1)
+        quantize_w2(0, 1)
+        make_da(1, 0)
+        lay_w2(1, 1)
+        quantize_w2(1, 1)
+        make_z(1, 1)
+        lay_da(0, 0)
+        lay_da(1, 0)
+        quantize_da(0, 0)
+        quantize_da(1, 0)
+        silu(3)
+        lay_w1()
+        make_z(1, 2)
+        make_z(1, 3)
+
+        make_da(0, 1)
+        make_da(1, 1)
+        quantize_w1()
+        add_to_dx(0, 0)
+        add_to_dx(1, 0)
+        lay_da(0, 1)
+        quantize_da(0, 1)
+        add_to_dx(0, 1)
+        lay_da(1, 1, nc.scalar.copy, 0, C // 2)
+        lay_da(1, 1, nc.vector.tensor_copy, C // 2, C)
+        quantize_da(1, 1)
+        add_to_dx(1, 1)
+        put_back(0)
+        put_back(1)
+
+        nc.sync.dma_start(out, result[:])

@@ -1,6 +1,7 @@
 from contextlib import ExitStack
 
 import concourse.mybir as mybir
+from concourse.masks import make_identity
 
 F32 = mybir.dt.float32
 BF16 = mybir.dt.bfloat16
@@ -47,61 +48,78 @@ def tile_moe_bdx_mlp_silu_kernel(tc, dyT, a, w2, w1, gate, offs, out):
         dy = [keep.tile([P, T], F32, name=f"dy{t}") for t in range(PACK)]
         v = [keep.tile([P, PACK, S], F32, name=f"v{h}") for h in range(HALVES)]
         d = [keep.tile([P, PACK, S], F32, name=f"d{h}") for h in range(HALVES)]
+        s_of = [d[0], v[1]]
+        m_of = [v[0], d[1]]
         w2_raw = {x: keep.tile([P, PACK, PASS], F32, name=f"w2_raw{x[0]}{x[1]}") for x in pairs}
         w1_raw = keep.tile([P, E * HALVES, PACK, K], F32, name="w1_raw")
         g_rows = keep.tile([P, PACK, S], F32, name="g_rows")
 
-        g_words = [keep.tile([P, C, PACK], BF16, name=f"g_words{e}", align_bytes=64) for e in range(E)]
         g_codes = [keep.tile([P, C], U32, name=f"g_codes{e}", align_bytes=64) for e in range(E)]
         g_scales = [keep.tile([P, C], U8, name=f"g_scales{e}", align_bytes=64) for e in range(E)]
         w2_words = {x: keep.tile([P, PACK, P, PACK], BF16, name=f"w2_words{x[0]}{x[1]}", align_bytes=64) for x in pairs}
         w2_codes = {x: keep.tile([P, PASS], U32, name=f"w2_codes{x[0]}{x[1]}", align_bytes=64) for x in pairs}
         w2_scales = {x: keep.tile([P, PASS], U8, name=f"w2_scales{x[0]}{x[1]}", align_bytes=64) for x in pairs}
         w1_words = keep.tile([P, E * HALVES, K, PACK], BF16, name="w1_words", align_bytes=64)
+        w2_flat = [w2_words[x][:].rearrange("p t m j -> p (t m) j") for x in pairs]
+        g_first = keep.tile([P, C, PACK], BF16, name="g_first", align_bytes=64)
+        g_words = [g_first[:], w2_flat[0]]
+        da_words = dict(zip(pairs, w2_flat[1:3] + [g_first[:], w1_words[:].rearrange("p x k j -> p (x k) j")]))
         w1_codes = keep.tile([P, E * HALVES * K], U32, name="w1_codes", align_bytes=64)
         w1_scales = keep.tile([P, E * HALVES * K], U8, name="w1_scales", align_bytes=64)
         da_codes = {x: keep.tile([P, C], U32, name=f"da_codes{x[0]}{x[1]}", align_bytes=64) for x in pairs}
         da_scales = {x: keep.tile([P, C], U8, name=f"da_scales{x[0]}{x[1]}", align_bytes=64) for x in pairs}
         result = keep.tile([P, T], F32, name="result")
+        gate_columns = keep.tile([P, S // P], F32, name="gate_columns")
+        identity = keep.tile([P, P], F32, name="identity")
         warm = keep.tile([P, 1], F32, name="warm")
-        zero = keep.tile([P, 1], F32, name="zero")
 
+        def slots_of(e):
+            return slice(e * C, (e + 1) * C)
 
         def load_a(h, t0, t1):
             nc.sync.dma_start(v[h][:, t0:t1, :], a_rows[:, h, t0:t1, :])
 
+        def load_dy(t):
+            nc.sync.dma_start(dy[t][:], dy_rows[:, t, :])
+
         def load_w2(e, h):
             nc.sync.dma_start(w2_raw[e, h][:], w2_rows[:, e, :, h * PASS : (h + 1) * PASS])
 
-        def sigmoid(h, t):
-            nc.scalar.activation(d[h][:, t, :], v[h][:, t, :], SIGMOID, scale=(1.0, -1.0)[h])
+        def spread_gates():
+            per_bank = C // P
+            for b in range(S // C):
+                bank = dh_banks.tile([P, per_bank, P], F32, name="dh")
+                for j in range(per_bank):
+                    column = b * per_bank + j
+                    nc.tensor.transpose(
+                        bank[:, j, :], gate_columns[:, column : column + 1].to_broadcast([P, P]), identity[:]
+                    )
+                nc.vector.tensor_copy(
+                    gates[:].rearrange("q (p b j) -> q b p j", b=S // C, j=per_bank)[:, b],
+                    bank[:].rearrange("q j p -> q p j"),
+                )
 
-        def silu(t):
-            nc.scalar.activation(v[1][:, t, :], v[1][:, t, :], SILU, bias=zero[:])
+        def sigmoid(h, planes, columns):
+            nc.scalar.activation(s_of[h][:, planes, columns], v[h][:, planes, columns], SIGMOID)
 
-        def make_u(t):
-            nc.vector.scalar_tensor_tensor(v[0][:, t, :], d[0][:, t, :], -1.0, v[0][:, t, :], ADD, MULT)
-
-        def make_z(h, t):
-            nc.vector.scalar_tensor_tensor(d[h][:, t, :], v[h][:, t, :], -1.0, d[h][:, t, :], ADD, MULT)
-
-        last_step = [(-1.0, MULT), (1.0, ADD)]
+        def silu(h, planes, columns):
+            nc.scalar.activation(m_of[h][:, planes, columns], v[h][:, planes, columns], SILU, scale=-1.0)
 
         def gather(t):
             nc.vector.tensor_tensor(g_rows[:, t, :], dy[t][:].indirect(offsets[:]), gates[:], MULT)
 
-        def interleave(copy, words, planes):
-            copy(
-                words.rearrange("p (c i) t -> p c t i", i=RUN),
-                planes.rearrange("p t (c i) -> p c t i", i=RUN),
-            )
+        def as_words(words):
+            return words.rearrange("p (c i) t -> p c t i", i=RUN)
 
-        def lay_g(e):
-            interleave(nc.vector.tensor_copy, g_words[e][:], g_rows[:, :, e * C : (e + 1) * C])
+        def as_planes(planes):
+            return planes.rearrange("p t (c i) -> p c t i", i=RUN)
+
+        def lay_g(e, copy):
+            copy(as_words(g_words[e]), as_planes(g_rows[:, :, slots_of(e)]))
 
         def quantize_g(e):
             nc.vector.quantize_mx(
-                out=g_codes[e][:].bitcast(E5M2), scales=g_scales[e][:], in_=g_words[e][:].rearrange("p c t -> p (c t)")
+                out=g_codes[e][:].bitcast(E5M2), scales=g_scales[e][:], in_=g_words[e].rearrange("p c t -> p (c t)")
             )
 
         def lay_w2(e, h):
@@ -119,20 +137,14 @@ def tile_moe_bdx_mlp_silu_kernel(tc, dyT, a, w2, w1, gate, offs, out):
 
         def lay_w1():
             for x in range(E * HALVES):
-                interleave(nc.scalar.copy, w1_words[:, x], w1_raw[:, x])
+                nc.scalar.copy(as_words(w1_words[:, x]), as_planes(w1_raw[:, x]))
 
         def quantize_w1():
             nc.vector.quantize_mx(
                 out=w1_codes[:].bitcast(E4M3), scales=w1_scales[:], in_=w1_words[:].rearrange("p x k j -> p (x k j)")
             )
 
-        da_planes = {}
-        da_words = {}
-
-        def make_da(e, h):
-            da_planes[e, h] = ring.tile([P, PACK, C], BF16, name="da_planes")
-            da_words[e, h] = ring.tile([P, C, PACK], BF16, name="da_words", align_bytes=64)
-            scalar, op = last_step[h]
+        def make_x(e, h):
             for t in range(PACK):
                 dh = dh_banks.tile([P, C], F32, name="dh")
                 columns = slice(t * P, (t + 1) * P)
@@ -145,18 +157,22 @@ def tile_moe_bdx_mlp_silu_kernel(tc, dyT, a, w2, w1, gate, offs, out):
                     start=True,
                     stop=True,
                 )
-                nc.vector.scalar_tensor_tensor(
-                    da_planes[e, h][:, t, :], d[h][:, t, e * C : (e + 1) * C], scalar, dh[:], op, MULT
-                )
+                m = m_of[h][:, t, slots_of(e)]
+                nc.vector.scalar_tensor_tensor(m, m, -1.0, dh[:], ADD, MULT)
 
-        def lay_da(e, h, copy=nc.scalar.copy, c0=0, c1=C):
-            interleave(copy, da_words[e, h][:, c0:c1, :], da_planes[e, h][:, :, c0:c1])
+        def make_da(e, h):
+            nc.vector.tensor_tensor(
+                as_words(da_words[e, h]),
+                as_planes(m_of[h][:, :, slots_of(e)]),
+                as_planes(s_of[h][:, :, slots_of(e)]),
+                MULT,
+            )
 
         def quantize_da(e, h):
             nc.vector.quantize_mx(
                 out=da_codes[e, h][:].bitcast(E5M2),
                 scales=da_scales[e, h][:],
-                in_=da_words[e, h][:].rearrange("p c t -> p (c t)"),
+                in_=da_words[e, h].rearrange("p c t -> p (c t)"),
             )
 
         dx = [dx_banks.tile([P, C], F32, name="dx") for e in range(E)]
@@ -175,86 +191,74 @@ def tile_moe_bdx_mlp_silu_kernel(tc, dyT, a, w2, w1, gate, offs, out):
 
         def put_back(e):
             slots = ring.tile([P, C], F32, name="slots")
-            nc.scalar.copy(slots[:], dx[e][:])
+            nc.scalar.activation(slots[:], dx[e][:], COPY, scale=-1.0)
             nc.vector.tensor_copy(result[:].indirect(offsets[:, e * (C // 16) : (e + 1) * (C // 16)]), slots[:])
 
+        every_plane = slice(0, PACK)
+        every_slot = slice(0, S)
 
-        nc.sync.dma_start(offsets[:], offs)
+        nc.sync.dma_start(gate_columns[:], gate[0, :].rearrange("(p j) -> p j", p=P))
         load_a(0, 0, 1)
+        nc.sync.dma_start(offsets[:], offs)
+        load_dy(0)
         load_a(0, 1, 2)
-        load_a(0, 2, 4)
+        load_dy(1)
+        load_a(0, 2, 3)
+        load_dy(2)
+        load_a(0, 3, 4)
+        load_dy(3)
+        load_w2(0, 0)
+        load_w2(1, 0)
         load_a(1, 0, 2)
-        nc.sync.dma_start(gates[:], gate[0:P, :])
-        nc.sync.dma_start(dy[0][:], dy_rows[:, 0, :])
         load_a(1, 2, 4)
-        for t in range(1, PACK):
-            nc.sync.dma_start(dy[t][:], dy_rows[:, t, :])
-        for e, h in pairs:
-            load_w2(e, h)
+        load_w2(0, 1)
+        load_w2(1, 1)
         nc.sync.dma_start(w1_raw[:], w1_rows)
-
 
         nc.vector.memset(warm[:], 1.0)
         nc.scalar.activation(warm[:], warm[:], SIGMOID)
-        nc.vector.memset(result[:], 0.0)
+        make_identity(nc, identity[:])
+        spread_gates()
+        nc.gpsimd.memset(result[:], 0.0)
 
-        for t0 in (0, 2):
-            planes = range(t0, t0 + 2)
-            for t in planes:
-                sigmoid(0, t)
-            for t in planes:
-                make_u(t)
-            for t in planes:
-                make_z(0, t)
-
-        sigmoid(1, 0)
-        sigmoid(1, 1)
-        gather(0)
-        gather(1)
-        sigmoid(1, 2)
-        sigmoid(1, 3)
-        nc.scalar.activation(zero[:], d[1][:, PACK - 1, S - 1 : S], COPY, scale=0.0)
-        silu(0)
-        silu(1)
-        gather(2)
-        gather(3)
-        silu(2)
+        for t in range(PACK):
+            gather(t)
+            sigmoid(0, slice(t, t + 1), every_slot)
+        silu(0, every_plane, slice(0, C // 2))
+        lay_g(0, nc.vector.tensor_copy)
         lay_w2(0, 0)
-        make_z(1, 0)
-        lay_g(0)
-        quantize_w2(0, 0)
-        lay_w2(1, 0)
-        lay_g(1)
+        silu(0, every_plane, slice(C // 2, C))
         quantize_g(0)
+        quantize_w2(0, 0)
+        lay_g(1, nc.vector.tensor_copy)
         quantize_g(1)
+        lay_w2(1, 0)
+        silu(0, every_plane, slots_of(1))
+        make_x(0, 0)
         quantize_w2(1, 0)
-
         make_da(0, 0)
+        silu(1, every_plane, slots_of(0))
         lay_w2(0, 1)
+        silu(1, every_plane, slots_of(1))
+        make_x(1, 0)
         quantize_w2(0, 1)
-        make_da(1, 0)
-        lay_w2(1, 1)
-        quantize_w2(1, 1)
-        make_z(1, 1)
-        lay_da(0, 0)
-        lay_da(1, 0)
         quantize_da(0, 0)
+        make_da(1, 0)
+        sigmoid(1, every_plane, slots_of(0))
+        lay_w2(1, 1)
+        make_x(0, 1)
         quantize_da(1, 0)
-        silu(3)
-        lay_w1()
-        make_z(1, 2)
-        make_z(1, 3)
-
         make_da(0, 1)
-        make_da(1, 1)
+        quantize_w2(1, 1)
+        lay_w1()
+        sigmoid(1, every_plane, slots_of(1))
+        quantize_da(0, 1)
+        make_x(1, 1)
         quantize_w1()
+        make_da(1, 1)
         add_to_dx(0, 0)
         add_to_dx(1, 0)
-        lay_da(0, 1)
-        quantize_da(0, 1)
         add_to_dx(0, 1)
-        lay_da(1, 1, nc.scalar.copy, 0, C // 2)
-        lay_da(1, 1, nc.vector.tensor_copy, C // 2, C)
         quantize_da(1, 1)
         add_to_dx(1, 1)
         put_back(0)

@@ -46,11 +46,18 @@ def tile_moe_bdx_mlp_silu_kernel(tc, dyT, a, w2, w1, gate, offs, out):
         offsets = lists.tile([P, S // 16], U16, name="offsets")
         gates = keep.tile([P, S], F32, name="gates")
         dy = [keep.tile([P, T], F32, name=f"dy{t}") for t in range(PACK)]
-        v = [keep.tile([P, PACK, S], F32, name=f"v{h}") for h in range(HALVES)]
-        d = [keep.tile([P, PACK, S], F32, name=f"d{h}") for h in range(HALVES)]
-        s_of = [d[0], v[1]]
-        m_of = [v[0], d[1]]
         w2_raw = {x: keep.tile([P, PACK, PASS], F32, name=f"w2_raw{x[0]}{x[1]}") for x in pairs}
+        v = {x: keep.tile([P, PACK, C], F32, name=f"v{x[0]}{x[1]}") for x in pairs}
+        first, second, third, last = pairs
+        spare = {x: keep.tile([P, PACK, C], F32, name=f"spare{x[0]}{x[1]}") for x in pairs[:-1]}
+        tail = keep.tile([P, C // 2 + PACK * C], F32, name="tail")
+        m_of = {
+            first: v[first][:],
+            second: spare[second][:],
+            third: spare[third][:],
+            last: tail[:, C // 2 :].rearrange("p (t c) -> p t c", t=PACK),
+        }
+        s_of = {first: spare[first][:], second: w2_raw[third][:], third: v[second][:], last: v[third][:]}
         w1_raw = keep.tile([P, E * HALVES, PACK, K], F32, name="w1_raw")
         g_rows = keep.tile([P, PACK, S], F32, name="g_rows")
 
@@ -69,15 +76,15 @@ def tile_moe_bdx_mlp_silu_kernel(tc, dyT, a, w2, w1, gate, offs, out):
         da_codes = {x: keep.tile([P, C], U32, name=f"da_codes{x[0]}{x[1]}", align_bytes=64) for x in pairs}
         da_scales = {x: keep.tile([P, C], U8, name=f"da_scales{x[0]}{x[1]}", align_bytes=64) for x in pairs}
         result = keep.tile([P, T], F32, name="result")
-        gate_columns = keep.tile([P, S // P], F32, name="gate_columns")
+        gate_columns = keep.tile([P, E, C // P], F32, name="gate_columns")
         identity = keep.tile([P, P], F32, name="identity")
         warm = keep.tile([P, 1], F32, name="warm")
 
         def slots_of(e):
             return slice(e * C, (e + 1) * C)
 
-        def load_a(h, t0, t1):
-            nc.sync.dma_start(v[h][:, t0:t1, :], a_rows[:, h, t0:t1, :])
+        def load_a(e, h, t0=0, t1=PACK):
+            nc.sync.dma_start(v[e, h][:, t0:t1, :], a_rows[:, h, t0:t1, slots_of(e)])
 
         def load_dy(t):
             nc.sync.dma_start(dy[t][:], dy_rows[:, t, :])
@@ -85,28 +92,22 @@ def tile_moe_bdx_mlp_silu_kernel(tc, dyT, a, w2, w1, gate, offs, out):
         def load_w2(e, h):
             nc.sync.dma_start(w2_raw[e, h][:], w2_rows[:, e, :, h * PASS : (h + 1) * PASS])
 
-        def spread_gates():
-            per_bank = C // P
-            for b in range(S // C):
-                bank = dh_banks.tile([P, per_bank, P], F32, name="dh")
-                for j in range(per_bank):
-                    column = b * per_bank + j
-                    nc.tensor.transpose(
-                        bank[:, j, :], gate_columns[:, column : column + 1].to_broadcast([P, P]), identity[:]
-                    )
-                nc.vector.tensor_copy(
-                    gates[:].rearrange("q (p b j) -> q b p j", b=S // C, j=per_bank)[:, b],
-                    bank[:].rearrange("q j p -> q p j"),
-                )
+        def spread_gates(e, copy):
+            bank = dh_banks.tile([P, C // P, P], F32, name="dh")
+            for j in range(C // P):
+                nc.tensor.transpose(bank[:, j, :], gate_columns[:, e, j : j + 1].to_broadcast([P, P]), identity[:])
+            copy(gates[:, slots_of(e)].rearrange("q (p j) -> q p j", j=C // P), bank[:].rearrange("q j p -> q p j"))
 
-        def sigmoid(h, planes, columns):
-            nc.scalar.activation(s_of[h][:, planes, columns], v[h][:, planes, columns], SIGMOID)
+        def sigmoid(e, h, t0=0, t1=PACK):
+            nc.scalar.activation(s_of[e, h][:, t0:t1, :], v[e, h][:, t0:t1, :], SIGMOID)
 
-        def silu(h, planes, columns):
-            nc.scalar.activation(m_of[h][:, planes, columns], v[h][:, planes, columns], SILU, scale=-1.0)
+        def silu(e, h):
+            nc.scalar.activation(m_of[e, h], v[e, h][:], SILU, scale=-1.0)
 
-        def gather(t):
-            nc.vector.tensor_tensor(g_rows[:, t, :], dy[t][:].indirect(offsets[:]), gates[:], MULT)
+        def gather(t, c0=0, c1=S):
+            nc.vector.tensor_tensor(
+                g_rows[:, t, c0:c1], dy[t][:].indirect(offsets[:, c0 // 16 : c1 // 16]), gates[:, c0:c1], MULT
+            )
 
         def as_words(words):
             return words.rearrange("p (c i) t -> p c t i", i=RUN)
@@ -157,22 +158,22 @@ def tile_moe_bdx_mlp_silu_kernel(tc, dyT, a, w2, w1, gate, offs, out):
                     start=True,
                     stop=True,
                 )
-                m = m_of[h][:, t, slots_of(e)]
+                m = m_of[e, h][:, t, :]
                 nc.vector.scalar_tensor_tensor(m, m, -1.0, dh[:], ADD, MULT)
 
-        def make_da(e, h):
+        def make_da(e, h, c0=0, c1=C):
             nc.vector.tensor_tensor(
-                as_words(da_words[e, h]),
-                as_planes(m_of[h][:, :, slots_of(e)]),
-                as_planes(s_of[h][:, :, slots_of(e)]),
+                as_words(da_words[e, h][:, c0:c1, :]),
+                as_planes(m_of[e, h][:, :, c0:c1]),
+                as_planes(s_of[e, h][:, :, c0:c1]),
                 MULT,
             )
 
-        def quantize_da(e, h):
+        def quantize_da(e, h, c0=0, c1=C):
             nc.vector.quantize_mx(
-                out=da_codes[e, h][:].bitcast(E5M2),
-                scales=da_scales[e, h][:],
-                in_=da_words[e, h].rearrange("p c t -> p (c t)"),
+                out=da_codes[e, h][:, c0:c1].bitcast(E5M2),
+                scales=da_scales[e, h][:, c0:c1],
+                in_=da_words[e, h][:, c0:c1, :].rearrange("p c t -> p (c t)"),
             )
 
         dx = [dx_banks.tile([P, C], F32, name="dx") for e in range(E)]
@@ -189,79 +190,80 @@ def tile_moe_bdx_mlp_silu_kernel(tc, dyT, a, w2, w1, gate, offs, out):
                 stop=(h == HALVES - 1),
             )
 
-        def put_back(e):
-            slots = ring.tile([P, C], F32, name="slots")
-            nc.scalar.activation(slots[:], dx[e][:], COPY, scale=-1.0)
-            nc.vector.tensor_copy(result[:].indirect(offsets[:, e * (C // 16) : (e + 1) * (C // 16)]), slots[:])
+        def put_back(e, slots):
+            nc.scalar.activation(slots, dx[e][:], COPY, scale=-1.0)
+            nc.vector.tensor_copy(result[:].indirect(offsets[:, e * (C // 16) : (e + 1) * (C // 16)]), slots)
 
-        every_plane = slice(0, PACK)
-        every_slot = slice(0, S)
-
-        nc.sync.dma_start(gate_columns[:], gate[0, :].rearrange("(p j) -> p j", p=P))
-        load_a(0, 0, 1)
-        nc.sync.dma_start(offsets[:], offs)
+        nc.sync.dma_start(gate_columns[:], gate[0, :].rearrange("(e p j) -> p e j", e=E, p=P))
         load_dy(0)
-        load_a(0, 1, 2)
+        nc.sync.dma_start(offsets[:], offs)
+        load_a(0, 0, 0, 2)
         load_dy(1)
-        load_a(0, 2, 3)
+        load_a(0, 0, 2, 4)
         load_dy(2)
-        load_a(0, 3, 4)
         load_dy(3)
         load_w2(0, 0)
+        load_a(1, 0)
         load_w2(1, 0)
-        load_a(1, 0, 2)
-        load_a(1, 2, 4)
+        load_a(0, 1)
+        load_a(1, 1)
         load_w2(0, 1)
-        load_w2(1, 1)
         nc.sync.dma_start(w1_raw[:], w1_rows)
+        load_w2(1, 1)
 
         nc.vector.memset(warm[:], 1.0)
         nc.scalar.activation(warm[:], warm[:], SIGMOID)
         make_identity(nc, identity[:])
-        spread_gates()
+        spread_gates(0, nc.vector.tensor_copy)
+        spread_gates(1, nc.vector.tensor_copy)
         nc.gpsimd.memset(result[:], 0.0)
 
-        for t in range(PACK):
+        gather(0, 0, C)
+        gather(0, C, S)
+        for t in range(1, PACK):
             gather(t)
-            sigmoid(0, slice(t, t + 1), every_slot)
-        silu(0, every_plane, slice(0, C // 2))
-        lay_g(0, nc.vector.tensor_copy)
+        sigmoid(0, 0, 0, 2)
+        sigmoid(0, 0, 2, 4)
+        silu(0, 0)
         lay_w2(0, 0)
-        silu(0, every_plane, slice(C // 2, C))
+        lay_g(0, nc.vector.tensor_copy)
         quantize_g(0)
         quantize_w2(0, 0)
         lay_g(1, nc.vector.tensor_copy)
         quantize_g(1)
+        silu(1, 0)
         lay_w2(1, 0)
-        silu(0, every_plane, slots_of(1))
         make_x(0, 0)
         quantize_w2(1, 0)
         make_da(0, 0)
-        silu(1, every_plane, slots_of(0))
+        silu(0, 1)
+        silu(1, 1)
         lay_w2(0, 1)
-        silu(1, every_plane, slots_of(1))
         make_x(1, 0)
         quantize_w2(0, 1)
         quantize_da(0, 0)
-        make_da(1, 0)
-        sigmoid(1, every_plane, slots_of(0))
-        lay_w2(1, 1)
+        sigmoid(1, 0)
+        sigmoid(0, 1)
         make_x(0, 1)
+        make_da(1, 0)
         quantize_da(1, 0)
+        lay_w2(1, 1)
         make_da(0, 1)
         quantize_w2(1, 1)
+        sigmoid(1, 1)
         lay_w1()
-        sigmoid(1, every_plane, slots_of(1))
         quantize_da(0, 1)
         make_x(1, 1)
         quantize_w1()
-        make_da(1, 1)
+        make_da(1, 1, 0, C // 2)
+        make_da(1, 1, C // 2, C)
         add_to_dx(0, 0)
         add_to_dx(1, 0)
         add_to_dx(0, 1)
-        quantize_da(1, 1)
+        quantize_da(1, 1, 0, C // 2)
+        quantize_da(1, 1, C // 2, C)
         add_to_dx(1, 1)
-        put_back(0)
-        put_back(1)
+        put_back(0, tail[:, 0:C])
+        put_back(1, g_rows[:, 0, 0:C])
 
         nc.sync.dma_start(out, result[:])

@@ -57,7 +57,7 @@ def tile_moe_bdx_mlp_silu_kernel(tc, dyT, a, w2, w1, gate, offs, out):
             third: spare[third][:],
             last: tail[:, C // 2 :].rearrange("p (t c) -> p t c", t=PACK),
         }
-        s_of = {first: spare[first][:], second: w2_raw[third][:], third: v[second][:], last: v[third][:]}
+        s_of = {first: spare[first][:], second: w2_raw[last][:], third: v[second][:], last: v[third][:]}
         w1_raw = keep.tile([P, E * HALVES, PACK, K], F32, name="w1_raw")
         g_rows = keep.tile([P, PACK, S], F32, name="g_rows")
 
@@ -70,7 +70,8 @@ def tile_moe_bdx_mlp_silu_kernel(tc, dyT, a, w2, w1, gate, offs, out):
         w2_flat = [w2_words[x][:].rearrange("p t m j -> p (t m) j") for x in pairs]
         g_first = keep.tile([P, C, PACK], BF16, name="g_first", align_bytes=64)
         g_words = [g_first[:], w2_flat[0]]
-        da_words = dict(zip(pairs, w2_flat[1:3] + [g_first[:], w1_words[:].rearrange("p x k j -> p (x k) j")]))
+        da_first = [(0, C // 2, w2_flat[1]), (C // 2, 3 * C // 4, w2_flat[2]), (3 * C // 4, C, w2_flat[3])]
+        da_words = {second: w2_flat[0], third: g_first[:], last: w1_words[:].rearrange("p x k j -> p (x k) j")}
         w1_codes = keep.tile([P, E * HALVES * K], U32, name="w1_codes", align_bytes=64)
         w1_scales = keep.tile([P, E * HALVES * K], U8, name="w1_scales", align_bytes=64)
         da_codes = {x: keep.tile([P, C], U32, name=f"da_codes{x[0]}{x[1]}", align_bytes=64) for x in pairs}
@@ -161,19 +162,21 @@ def tile_moe_bdx_mlp_silu_kernel(tc, dyT, a, w2, w1, gate, offs, out):
                 m = m_of[e, h][:, t, :]
                 nc.vector.scalar_tensor_tensor(m, m, -1.0, dh[:], ADD, MULT)
 
-        def make_da(e, h, c0=0, c1=C):
+        def make_da(e, h, c0=0, c1=C, words=None):
+            words = da_words[e, h] if words is None else words
             nc.vector.tensor_tensor(
-                as_words(da_words[e, h][:, c0:c1, :]),
+                as_words(words[:, c0:c1, :]),
                 as_planes(m_of[e, h][:, :, c0:c1]),
                 as_planes(s_of[e, h][:, :, c0:c1]),
                 MULT,
             )
 
-        def quantize_da(e, h, c0=0, c1=C):
+        def quantize_da(e, h, c0=0, c1=C, words=None):
+            words = da_words[e, h] if words is None else words
             nc.vector.quantize_mx(
                 out=da_codes[e, h][:, c0:c1].bitcast(E5M2),
                 scales=da_scales[e, h][:, c0:c1],
-                in_=da_words[e, h][:, c0:c1, :].rearrange("p c t -> p (c t)"),
+                in_=words[:, c0:c1, :].rearrange("p c t -> p (c t)"),
             )
 
         dx = [dx_banks.tile([P, C], F32, name="dx") for e in range(E)]
@@ -206,21 +209,19 @@ def tile_moe_bdx_mlp_silu_kernel(tc, dyT, a, w2, w1, gate, offs, out):
         load_a(1, 0)
         load_w2(1, 0)
         load_a(0, 1)
-        load_a(1, 1)
         load_w2(0, 1)
-        nc.sync.dma_start(w1_raw[:], w1_rows)
+        load_a(1, 1)
         load_w2(1, 1)
+        nc.sync.dma_start(w1_raw[:], w1_rows)
 
         nc.vector.memset(warm[:], 1.0)
         nc.scalar.activation(warm[:], warm[:], SIGMOID)
         make_identity(nc, identity[:])
         spread_gates(0, nc.vector.tensor_copy)
         spread_gates(1, nc.vector.tensor_copy)
-        nc.gpsimd.memset(result[:], 0.0)
+        nc.vector.memset(result[:], 0.0)
 
-        gather(0, 0, C)
-        gather(0, C, S)
-        for t in range(1, PACK):
+        for t in range(PACK):
             gather(t)
         sigmoid(0, 0, 0, 2)
         sigmoid(0, 0, 2, 4)
@@ -231,29 +232,20 @@ def tile_moe_bdx_mlp_silu_kernel(tc, dyT, a, w2, w1, gate, offs, out):
         quantize_w2(0, 0)
         lay_g(1, nc.vector.tensor_copy)
         quantize_g(1)
-        silu(1, 0)
-        lay_w2(1, 0)
         make_x(0, 0)
-        quantize_w2(1, 0)
-        make_da(0, 0)
-        silu(0, 1)
-        silu(1, 1)
-        lay_w2(0, 1)
-        make_x(1, 0)
-        quantize_w2(0, 1)
-        quantize_da(0, 0)
-        sigmoid(1, 0)
-        sigmoid(0, 1)
-        make_x(0, 1)
-        make_da(1, 0)
-        quantize_da(1, 0)
-        lay_w2(1, 1)
-        make_da(0, 1)
-        quantize_w2(1, 1)
+        for (e, h), part in zip(pairs[1:], da_first):
+            silu(e, h)
+            lay_w2(e, h)
+            quantize_w2(e, h)
+            make_da(0, 0, *part)
+            quantize_da(0, 0, *part)
+            make_x(e, h)
+        for e, h in pairs[1:-1]:
+            sigmoid(e, h)
+            make_da(e, h)
+            quantize_da(e, h)
         sigmoid(1, 1)
         lay_w1()
-        quantize_da(0, 1)
-        make_x(1, 1)
         quantize_w1()
         make_da(1, 1, 0, C // 2)
         make_da(1, 1, C // 2, C)

@@ -57,7 +57,7 @@ def tile_moe_bdx_mlp_silu_kernel(tc, dyT, a, w2, w1, gate, offs, out):
             third: spare[third][:],
             last: tail[:, C // 2 :].rearrange("p (t c) -> p t c", t=PACK),
         }
-        s_of = {first: spare[first][:], second: w2_raw[last][:], third: v[second][:], last: v[third][:]}
+        s_of = {first: spare[first][:], second: w2_raw[first][:], third: v[second][:], last: v[third][:]}
         w1_raw = keep.tile([P, E * HALVES, PACK, K], F32, name="w1_raw")
         g_rows = keep.tile([P, PACK, S], F32, name="g_rows")
 
@@ -70,8 +70,8 @@ def tile_moe_bdx_mlp_silu_kernel(tc, dyT, a, w2, w1, gate, offs, out):
         w2_flat = [w2_words[x][:].rearrange("p t m j -> p (t m) j") for x in pairs]
         g_first = keep.tile([P, C, PACK], BF16, name="g_first", align_bytes=64)
         g_words = [g_first[:], w2_flat[0]]
-        da_first = [(0, C // 2, w2_flat[1]), (C // 2, 3 * C // 4, w2_flat[2]), (3 * C // 4, C, w2_flat[3])]
-        da_words = {second: w2_flat[0], third: g_first[:], last: w1_words[:].rearrange("p x k j -> p (x k) j")}
+        da_first = [(0, C // 2, w2_flat[1]), (C // 2, C, w2_flat[2])]
+        da_words = {second: w2_flat[0], third: w2_flat[3], last: w1_words[:].rearrange("p x k j -> p (x k) j")}
         w1_codes = keep.tile([P, E * HALVES * K], U32, name="w1_codes", align_bytes=64)
         w1_scales = keep.tile([P, E * HALVES * K], U8, name="w1_scales", align_bytes=64)
         da_codes = {x: keep.tile([P, C], U32, name=f"da_codes{x[0]}{x[1]}", align_bytes=64) for x in pairs}
@@ -79,6 +79,7 @@ def tile_moe_bdx_mlp_silu_kernel(tc, dyT, a, w2, w1, gate, offs, out):
         result = keep.tile([P, T], F32, name="result")
         gate_columns = keep.tile([P, E, C // P], F32, name="gate_columns")
         identity = keep.tile([P, P], F32, name="identity")
+        zero = keep.tile([P, 1], F32, name="zero")
         warm = keep.tile([P, 1], F32, name="warm")
 
         def slots_of(e):
@@ -99,8 +100,8 @@ def tile_moe_bdx_mlp_silu_kernel(tc, dyT, a, w2, w1, gate, offs, out):
                 nc.tensor.transpose(bank[:, j, :], gate_columns[:, e, j : j + 1].to_broadcast([P, P]), identity[:])
             copy(gates[:, slots_of(e)].rearrange("q (p j) -> q p j", j=C // P), bank[:].rearrange("q j p -> q p j"))
 
-        def sigmoid(e, h, t0=0, t1=PACK):
-            nc.scalar.activation(s_of[e, h][:, t0:t1, :], v[e, h][:, t0:t1, :], SIGMOID)
+        def sigmoid(e, h, t0=0, t1=PACK, bias=0.0):
+            nc.scalar.activation(s_of[e, h][:, t0:t1, :], v[e, h][:, t0:t1, :], SIGMOID, bias=bias)
 
         def silu(e, h):
             nc.scalar.activation(m_of[e, h], v[e, h][:], SILU, scale=-1.0)
@@ -124,8 +125,8 @@ def tile_moe_bdx_mlp_silu_kernel(tc, dyT, a, w2, w1, gate, offs, out):
                 out=g_codes[e][:].bitcast(E5M2), scales=g_scales[e][:], in_=g_words[e].rearrange("p c t -> p (c t)")
             )
 
-        def lay_w2(e, h):
-            nc.scalar.copy(
+        def lay_w2(e, h, copy=nc.scalar.copy):
+            copy(
                 w2_words[e, h][:].rearrange("p t m j -> p m j t"),
                 w2_raw[e, h][:].rearrange("p j (m t) -> p m j t", t=PACK),
             )
@@ -209,8 +210,8 @@ def tile_moe_bdx_mlp_silu_kernel(tc, dyT, a, w2, w1, gate, offs, out):
         load_a(1, 0)
         load_w2(1, 0)
         load_a(0, 1)
-        load_w2(0, 1)
         load_a(1, 1)
+        load_w2(0, 1)
         load_w2(1, 1)
         nc.sync.dma_start(w1_raw[:], w1_rows)
 
@@ -233,17 +234,29 @@ def tile_moe_bdx_mlp_silu_kernel(tc, dyT, a, w2, w1, gate, offs, out):
         lay_g(1, nc.vector.tensor_copy)
         quantize_g(1)
         make_x(0, 0)
-        for (e, h), part in zip(pairs[1:], da_first):
-            silu(e, h)
-            lay_w2(e, h)
-            quantize_w2(e, h)
-            make_da(0, 0, *part)
-            quantize_da(0, 0, *part)
-            make_x(e, h)
-        for e, h in pairs[1:-1]:
-            sigmoid(e, h)
-            make_da(e, h)
-            quantize_da(e, h)
+        silu(1, 0)
+        lay_w2(1, 0)
+        quantize_w2(1, 0)
+        make_da(0, 0, *da_first[0])
+        quantize_da(0, 0, *da_first[0])
+        make_x(1, 0)
+        silu(0, 1)
+        silu(1, 1)
+        nc.scalar.activation(zero[:], m_of[last][:, 0, 0:1], COPY, scale=0.0)
+        lay_w2(0, 1, nc.vector.tensor_copy)
+        quantize_w2(0, 1)
+        make_da(0, 0, *da_first[1])
+        quantize_da(0, 0, *da_first[1])
+        make_x(0, 1)
+        sigmoid(1, 0, bias=zero[:])
+        make_da(1, 0)
+        quantize_da(1, 0)
+        lay_w2(1, 1)
+        sigmoid(0, 1)
+        quantize_w2(1, 1)
+        make_da(0, 1)
+        quantize_da(0, 1)
+        make_x(1, 1)
         sigmoid(1, 1)
         lay_w1()
         quantize_w1()

@@ -70,7 +70,7 @@ def tile_moe_bdx_mlp_silu_kernel(tc, dyT, a, w2, w1, gate, offs, out):
         w2_flat = [w2_words[x][:].rearrange("p t m j -> p (t m) j") for x in pairs]
         g_first = keep.tile([P, C, PACK], BF16, name="g_first", align_bytes=64)
         g_words = [g_first[:], w2_flat[0]]
-        da_first = [(0, C // 2, w2_flat[1]), (C // 2, C, w2_flat[2])]
+        da_first = [(0, C // 2, w2_flat[1], 0), (C // 2, C, w2_flat[2], 0)]
         da_words = {second: w2_flat[0], third: w2_flat[3], last: w1_words[:].rearrange("p x k j -> p (x k) j")}
         w1_codes = keep.tile([P, E * HALVES * K], U32, name="w1_codes", align_bytes=64)
         w1_scales = keep.tile([P, E * HALVES * K], U8, name="w1_scales", align_bytes=64)
@@ -117,35 +117,41 @@ def tile_moe_bdx_mlp_silu_kernel(tc, dyT, a, w2, w1, gate, offs, out):
         def as_planes(planes):
             return planes.rearrange("p t (c i) -> p c t i", i=RUN)
 
-        def lay_g(e, copy):
-            copy(as_words(g_words[e]), as_planes(g_rows[:, :, slots_of(e)]))
+        def lay_g(e, c0=0, c1=C):
+            nc.vector.tensor_copy(as_words(g_words[e][:, c0:c1, :]), as_planes(g_rows[:, :, e * C + c0 : e * C + c1]))
 
         def quantize_g(e):
             nc.vector.quantize_mx(
                 out=g_codes[e][:].bitcast(E5M2), scales=g_scales[e][:], in_=g_words[e].rearrange("p c t -> p (c t)")
             )
 
-        def lay_w2(e, h, copy=nc.scalar.copy):
+        def lay_w2(e, h, copy=nc.scalar.copy, t0=0, t1=PACK):
             copy(
-                w2_words[e, h][:].rearrange("p t m j -> p m j t"),
-                w2_raw[e, h][:].rearrange("p j (m t) -> p m j t", t=PACK),
+                w2_words[e, h][:, t0:t1].rearrange("p t m j -> p m j t"),
+                w2_raw[e, h][:].rearrange("p j (m t) -> p m j t", t=PACK)[:, :, :, t0:t1],
             )
 
         def quantize_w2(e, h):
-            nc.vector.quantize_mx(
-                out=w2_codes[e, h][:].bitcast(E4M3),
-                scales=w2_scales[e, h][:],
-                in_=w2_words[e, h][:].rearrange("p t m j -> p (t m j)"),
-            )
+            for t0 in (0, 2):
+                columns = slice(t0 * P, (t0 + 2) * P)
+                nc.vector.quantize_mx(
+                    out=w2_codes[e, h][:, columns].bitcast(E4M3),
+                    scales=w2_scales[e, h][:, columns],
+                    in_=w2_words[e, h][:, t0 : t0 + 2].rearrange("p t m j -> p (t m j)"),
+                )
 
         def lay_w1():
             for x in range(E * HALVES):
                 nc.scalar.copy(as_words(w1_words[:, x]), as_planes(w1_raw[:, x]))
 
         def quantize_w1():
-            nc.vector.quantize_mx(
-                out=w1_codes[:].bitcast(E4M3), scales=w1_scales[:], in_=w1_words[:].rearrange("p x k j -> p (x k j)")
-            )
+            for e in range(E):
+                columns = slice(e * HALVES * K, (e + 1) * HALVES * K)
+                nc.vector.quantize_mx(
+                    out=w1_codes[:, columns].bitcast(E4M3),
+                    scales=w1_scales[:, columns],
+                    in_=w1_words[:, e * HALVES : (e + 1) * HALVES].rearrange("p x k j -> p (x k j)"),
+                )
 
         def make_x(e, h):
             for t in range(PACK):
@@ -163,21 +169,23 @@ def tile_moe_bdx_mlp_silu_kernel(tc, dyT, a, w2, w1, gate, offs, out):
                 m = m_of[e, h][:, t, :]
                 nc.vector.scalar_tensor_tensor(m, m, -1.0, dh[:], ADD, MULT)
 
-        def make_da(e, h, c0=0, c1=C, words=None):
+        def make_da(e, h, c0=0, c1=C, words=None, at=None):
             words = da_words[e, h] if words is None else words
+            at = c0 if at is None else at
             nc.vector.tensor_tensor(
-                as_words(words[:, c0:c1, :]),
+                as_words(words[:, at : at + c1 - c0, :]),
                 as_planes(m_of[e, h][:, :, c0:c1]),
                 as_planes(s_of[e, h][:, :, c0:c1]),
                 MULT,
             )
 
-        def quantize_da(e, h, c0=0, c1=C, words=None):
+        def quantize_da(e, h, c0=0, c1=C, words=None, at=None):
             words = da_words[e, h] if words is None else words
+            at = c0 if at is None else at
             nc.vector.quantize_mx(
                 out=da_codes[e, h][:, c0:c1].bitcast(E5M2),
                 scales=da_scales[e, h][:, c0:c1],
-                in_=words[:, c0:c1, :].rearrange("p c t -> p (c t)"),
+                in_=words[:, at : at + c1 - c0, :].rearrange("p c t -> p (c t)"),
             )
 
         dx = [dx_banks.tile([P, C], F32, name="dx") for e in range(E)]
@@ -222,16 +230,19 @@ def tile_moe_bdx_mlp_silu_kernel(tc, dyT, a, w2, w1, gate, offs, out):
         spread_gates(1, nc.vector.tensor_copy)
         nc.vector.memset(result[:], 0.0)
 
-        for t in range(PACK):
+        for t in range(PACK - 1):
             gather(t)
+        gather(PACK - 1, 0, C)
+        gather(PACK - 1, C, S)
         sigmoid(0, 0, 0, 2)
         sigmoid(0, 0, 2, 4)
         silu(0, 0)
         lay_w2(0, 0)
-        lay_g(0, nc.vector.tensor_copy)
+        lay_g(0)
         quantize_g(0)
         quantize_w2(0, 0)
-        lay_g(1, nc.vector.tensor_copy)
+        lay_g(1, 0, C // 2)
+        lay_g(1, C // 2, C)
         quantize_g(1)
         make_x(0, 0)
         silu(1, 0)
@@ -243,7 +254,8 @@ def tile_moe_bdx_mlp_silu_kernel(tc, dyT, a, w2, w1, gate, offs, out):
         silu(0, 1)
         silu(1, 1)
         nc.scalar.activation(zero[:], m_of[last][:, 0, 0:1], COPY, scale=0.0)
-        lay_w2(0, 1, nc.vector.tensor_copy)
+        lay_w2(0, 1, nc.vector.tensor_copy, 0, 2)
+        lay_w2(0, 1, nc.vector.tensor_copy, 2, 4)
         quantize_w2(0, 1)
         make_da(0, 0, *da_first[1])
         quantize_da(0, 0, *da_first[1])

@@ -101,7 +101,9 @@ def tile_moe_bdx_mlp_silu_kernel(tc, dyT, a, w2, w1, gate, offs, out):
             copy(gates[:, slots_of(e)].rearrange("q (p j) -> q p j", j=C // P), bank[:].rearrange("q j p -> q p j"))
 
         def sigmoid(e, h, t0=0, t1=PACK, bias=0.0):
-            nc.scalar.activation(s_of[e, h][:, t0:t1, :], v[e, h][:, t0:t1, :], SIGMOID, bias=bias)
+            nc.scalar.activation(
+                in_runs(s_of[e, h])[:, :, t0:t1, :], as_planes(v[e, h][:])[:, :, t0:t1, :], SIGMOID, bias=bias
+            )
 
         def silu(e, h):
             nc.scalar.activation(m_of[e, h], v[e, h][:], SILU, scale=-1.0)
@@ -117,12 +119,17 @@ def tile_moe_bdx_mlp_silu_kernel(tc, dyT, a, w2, w1, gate, offs, out):
         def as_planes(planes):
             return planes.rearrange("p t (c i) -> p c t i", i=RUN)
 
+        def in_runs(block):
+            return block.rearrange("p t c -> p (t c)").rearrange("p (c t i) -> p c t i", t=PACK, i=RUN)
+
         def lay_g(e, c0=0, c1=C):
             nc.vector.tensor_copy(as_words(g_words[e][:, c0:c1, :]), as_planes(g_rows[:, :, e * C + c0 : e * C + c1]))
 
-        def quantize_g(e):
+        def quantize_g(e, c0=0, c1=C):
             nc.vector.quantize_mx(
-                out=g_codes[e][:].bitcast(E5M2), scales=g_scales[e][:], in_=g_words[e].rearrange("p c t -> p (c t)")
+                out=g_codes[e][:, c0:c1].bitcast(E5M2),
+                scales=g_scales[e][:, c0:c1],
+                in_=g_words[e][:, c0:c1, :].rearrange("p c t -> p (c t)"),
             )
 
         def lay_w2(e, h, copy=nc.scalar.copy, t0=0, t1=PACK):
@@ -175,7 +182,7 @@ def tile_moe_bdx_mlp_silu_kernel(tc, dyT, a, w2, w1, gate, offs, out):
             nc.vector.tensor_tensor(
                 as_words(words[:, at : at + c1 - c0, :]),
                 as_planes(m_of[e, h][:, :, c0:c1]),
-                as_planes(s_of[e, h][:, :, c0:c1]),
+                in_runs(s_of[e, h])[:, c0 // RUN : c1 // RUN],
                 MULT,
             )
 
@@ -230,7 +237,9 @@ def tile_moe_bdx_mlp_silu_kernel(tc, dyT, a, w2, w1, gate, offs, out):
         spread_gates(1, nc.vector.tensor_copy)
         nc.vector.memset(result[:], 0.0)
 
-        for t in range(PACK - 1):
+        gather(0, 0, C)
+        gather(0, C, S)
+        for t in range(1, PACK - 1):
             gather(t)
         gather(PACK - 1, 0, C)
         gather(PACK - 1, C, S)
@@ -238,8 +247,10 @@ def tile_moe_bdx_mlp_silu_kernel(tc, dyT, a, w2, w1, gate, offs, out):
         sigmoid(0, 0, 2, 4)
         silu(0, 0)
         lay_w2(0, 0)
-        lay_g(0)
-        quantize_g(0)
+        lay_g(0, 0, C // 2)
+        lay_g(0, C // 2, C)
+        quantize_g(0, 0, C // 2)
+        quantize_g(0, C // 2, C)
         quantize_w2(0, 0)
         lay_g(1, 0, C // 2)
         lay_g(1, C // 2, C)

@@ -277,7 +277,8 @@ def tile_moe_bdx_mlp_silu_kernel(tc, dyT, a, w2, w1, gate, offs, out):
         lay_w2(1, 1)
         sigmoid(0, 1)
         quantize_w2(1, 1)
-        make_da(0, 1)
+        make_da(0, 1, 0, C // 2)
+        make_da(0, 1, C // 2, C)
         quantize_da(0, 1)
         make_x(1, 1)
         sigmoid(1, 1)
@@ -294,4 +295,5 @@ def tile_moe_bdx_mlp_silu_kernel(tc, dyT, a, w2, w1, gate, offs, out):
         put_back(0, tail[:, 0:C])
         put_back(1, g_rows[:, 0, 0:C])
 
-        nc.sync.dma_start(out, result[:])
+        nc.sync.dma_start(out[:, 0 : T // 2], result[:, 0 : T // 2])
+        nc.scalar.dma_start(out[:, T // 2 : T], result[:, T // 2 : T])

@@ -295,5 +295,5 @@ def tile_moe_bdx_mlp_silu_kernel(tc, dyT, a, w2, w1, gate, offs, out):
         put_back(0, tail[:, 0:C])
         put_back(1, g_rows[:, 0, 0:C])
 
-        nc.sync.dma_start(out[:, 0 : T // 2], result[:, 0 : T // 2])
-        nc.scalar.dma_start(out[:, T // 2 : T], result[:, T // 2 : T])
+        for q, queue in enumerate((nc.sync, nc.scalar, nc.sync, nc.scalar)):
+            queue.dma_start(out[:, q * T // 4 : (q + 1) * T // 4], result[:, q * T // 4 : (q + 1) * T // 4])

@@ -23,6 +23,12 @@ PACK = 4
 PASS = P * PACK
 HALVES = H // PASS
 RUN = 4
+LIST_ROWS = 16
+STORES = 4
+
+SLOT_PARTS = ((0, C // 2), (C // 2, C))
+EXPERT_PARTS = ((0, C), (C, S))
+PLANE_PARTS = ((0, PACK // 2), (PACK // 2, PACK))
 
 FLOPS = 2 * S * N * H + 2 * S * H * K
 BYTES = 4 * (N * T + H * S + E * N * H + E * H * K + S + K * T) + 2 * S
@@ -30,26 +36,25 @@ BYTES = 4 * (N * T + H * S + E * N * H + E * H * K + S + K * T) + 2 * S
 
 def tile_moe_bdx_mlp_silu_kernel(tc, dyT, a, w2, w1, gate, offs, out):
     nc = tc.nc
-    dy_rows = dyT.rearrange("(p t) s -> p t s", t=PACK)
-    a_rows = a.rearrange("(h p t) s -> p h t s", h=HALVES, t=PACK)
-    w2_rows = w2.rearrange("e (p j) i -> p e j i", j=PACK)
-    w1_rows = w1.rearrange("e (h p j) k -> p (e h) j k", h=HALVES, j=PACK)
-    pairs = [(e, h) for h in range(HALVES) for e in range(E)]
+    dy_planes = dyT.rearrange("(p t) s -> p t s", t=PACK)
+    a_planes = a.rearrange("(h p t) s -> p h t s", h=HALVES, t=PACK)
+    w2_planes = w2.rearrange("e (p j) i -> p e j i", j=PACK)
+    w1_planes = w1.rearrange("e (h p j) k -> p (e h) j k", h=HALVES, j=PACK)
+    units = [(e, h) for h in range(HALVES) for e in range(E)]
+    first, second, third, last = units
 
     with ExitStack() as ctx:
         lists = ctx.enter_context(tc.tile_pool(name="lists", bufs=1))
         keep = ctx.enter_context(tc.tile_pool(name="keep", bufs=1))
-        ring = ctx.enter_context(tc.tile_pool(name="ring", bufs=2))
         dh_banks = ctx.enter_context(tc.psum_pool(name="dh_banks", bufs=6))
         dx_banks = ctx.enter_context(tc.psum_pool(name="dx_banks", bufs=2))
 
-        offsets = lists.tile([P, S // 16], U16, name="offsets")
+        offsets = lists.tile([P, S // LIST_ROWS], U16, name="offsets")
         gates = keep.tile([P, S], F32, name="gates")
         dy = [keep.tile([P, T], F32, name=f"dy{t}") for t in range(PACK)]
-        w2_raw = {x: keep.tile([P, PACK, PASS], F32, name=f"w2_raw{x[0]}{x[1]}") for x in pairs}
-        v = {x: keep.tile([P, PACK, C], F32, name=f"v{x[0]}{x[1]}") for x in pairs}
-        first, second, third, last = pairs
-        spare = {x: keep.tile([P, PACK, C], F32, name=f"spare{x[0]}{x[1]}") for x in pairs[:-1]}
+        w2_raw = {u: keep.tile([P, PACK, PASS], F32, name=f"w2_raw{u[0]}{u[1]}") for u in units}
+        v = {u: keep.tile([P, PACK, C], F32, name=f"v{u[0]}{u[1]}") for u in units}
+        spare = {u: keep.tile([P, PACK, C], F32, name=f"spare{u[0]}{u[1]}") for u in units[:-1]}
         tail = keep.tile([P, C // 2 + PACK * C], F32, name="tail")
         m_of = {
             first: v[first][:],
@@ -59,59 +64,33 @@ def tile_moe_bdx_mlp_silu_kernel(tc, dyT, a, w2, w1, gate, offs, out):
         }
         s_of = {first: spare[first][:], second: w2_raw[first][:], third: v[second][:], last: v[third][:]}
         w1_raw = keep.tile([P, E * HALVES, PACK, K], F32, name="w1_raw")
-        g_rows = keep.tile([P, PACK, S], F32, name="g_rows")
+        g_planes = keep.tile([P, PACK, S], F32, name="g_planes")
 
         g_codes = [keep.tile([P, C], U32, name=f"g_codes{e}", align_bytes=64) for e in range(E)]
         g_scales = [keep.tile([P, C], U8, name=f"g_scales{e}", align_bytes=64) for e in range(E)]
-        w2_words = {x: keep.tile([P, PACK, P, PACK], BF16, name=f"w2_words{x[0]}{x[1]}", align_bytes=64) for x in pairs}
-        w2_codes = {x: keep.tile([P, PASS], U32, name=f"w2_codes{x[0]}{x[1]}", align_bytes=64) for x in pairs}
-        w2_scales = {x: keep.tile([P, PASS], U8, name=f"w2_scales{x[0]}{x[1]}", align_bytes=64) for x in pairs}
+        w2_words = {u: keep.tile([P, PACK, P, PACK], BF16, name=f"w2_words{u[0]}{u[1]}", align_bytes=64) for u in units}
+        w2_codes = {u: keep.tile([P, PASS], U32, name=f"w2_codes{u[0]}{u[1]}", align_bytes=64) for u in units}
+        w2_scales = {u: keep.tile([P, PASS], U8, name=f"w2_scales{u[0]}{u[1]}", align_bytes=64) for u in units}
         w1_words = keep.tile([P, E * HALVES, K, PACK], BF16, name="w1_words", align_bytes=64)
-        w2_flat = [w2_words[x][:].rearrange("p t m j -> p (t m) j") for x in pairs]
         g_first = keep.tile([P, C, PACK], BF16, name="g_first", align_bytes=64)
-        g_words = [g_first[:], w2_flat[0]]
-        da_first = [(0, C // 2, w2_flat[1], 0), (C // 2, C, w2_flat[2], 0)]
-        da_words = {second: w2_flat[0], third: w2_flat[3], last: w1_words[:].rearrange("p x k j -> p (x k) j")}
+        freed = {u: w2_words[u][:].rearrange("p t m j -> p (t m) j") for u in units}
+        g_words = [g_first[:], freed[first]]
+        da_words = {second: freed[first], third: freed[last], last: w1_words[:].rearrange("p b k j -> p (b k) j")}
+        da_parts = {u: {(c0, c1): da_words[u][:, c0:c1, :] for c0, c1 in SLOT_PARTS + ((0, C),)} for u in units[1:]}
+        da_parts[first] = {part: freed[u][:, 0 : C // 2, :] for part, u in zip(SLOT_PARTS, (second, third))}
         w1_codes = keep.tile([P, E * HALVES * K], U32, name="w1_codes", align_bytes=64)
         w1_scales = keep.tile([P, E * HALVES * K], U8, name="w1_scales", align_bytes=64)
-        da_codes = {x: keep.tile([P, C], U32, name=f"da_codes{x[0]}{x[1]}", align_bytes=64) for x in pairs}
-        da_scales = {x: keep.tile([P, C], U8, name=f"da_scales{x[0]}{x[1]}", align_bytes=64) for x in pairs}
+        da_codes = {u: keep.tile([P, C], U32, name=f"da_codes{u[0]}{u[1]}", align_bytes=64) for u in units}
+        da_scales = {u: keep.tile([P, C], U8, name=f"da_scales{u[0]}{u[1]}", align_bytes=64) for u in units}
         result = keep.tile([P, T], F32, name="result")
         gate_columns = keep.tile([P, E, C // P], F32, name="gate_columns")
         identity = keep.tile([P, P], F32, name="identity")
         zero = keep.tile([P, 1], F32, name="zero")
-        warm = keep.tile([P, 1], F32, name="warm")
+        dx_slots = [tail[:, 0:C], g_planes[:, 0, 0:C]]
+
 
         def slots_of(e):
             return slice(e * C, (e + 1) * C)
-
-        def load_a(e, h, t0=0, t1=PACK):
-            nc.sync.dma_start(v[e, h][:, t0:t1, :], a_rows[:, h, t0:t1, slots_of(e)])
-
-        def load_dy(t):
-            nc.sync.dma_start(dy[t][:], dy_rows[:, t, :])
-
-        def load_w2(e, h):
-            nc.sync.dma_start(w2_raw[e, h][:], w2_rows[:, e, :, h * PASS : (h + 1) * PASS])
-
-        def spread_gates(e, copy):
-            bank = dh_banks.tile([P, C // P, P], F32, name="dh")
-            for j in range(C // P):
-                nc.tensor.transpose(bank[:, j, :], gate_columns[:, e, j : j + 1].to_broadcast([P, P]), identity[:])
-            copy(gates[:, slots_of(e)].rearrange("q (p j) -> q p j", j=C // P), bank[:].rearrange("q j p -> q p j"))
-
-        def sigmoid(e, h, t0=0, t1=PACK, bias=0.0):
-            nc.scalar.activation(
-                in_runs(s_of[e, h])[:, :, t0:t1, :], as_planes(v[e, h][:])[:, :, t0:t1, :], SIGMOID, bias=bias
-            )
-
-        def silu(e, h):
-            nc.scalar.activation(m_of[e, h], v[e, h][:], SILU, scale=-1.0)
-
-        def gather(t, c0=0, c1=S):
-            nc.vector.tensor_tensor(
-                g_rows[:, t, c0:c1], dy[t][:].indirect(offsets[:, c0 // 16 : c1 // 16]), gates[:, c0:c1], MULT
-            )
 
         def as_words(words):
             return words.rearrange("p (c i) t -> p c t i", i=RUN)
@@ -122,8 +101,41 @@ def tile_moe_bdx_mlp_silu_kernel(tc, dyT, a, w2, w1, gate, offs, out):
         def in_runs(block):
             return block.rearrange("p t c -> p (t c)").rearrange("p (c t i) -> p c t i", t=PACK, i=RUN)
 
-        def lay_g(e, c0=0, c1=C):
-            nc.vector.tensor_copy(as_words(g_words[e][:, c0:c1, :]), as_planes(g_rows[:, :, e * C + c0 : e * C + c1]))
+
+        def load_a(u, t0=0, t1=PACK):
+            nc.sync.dma_start(v[u][:, t0:t1, :], a_planes[:, u[1], t0:t1, slots_of(u[0])])
+
+        def load_dy(t):
+            nc.sync.dma_start(dy[t][:], dy_planes[:, t, :])
+
+        def load_w2(u):
+            nc.sync.dma_start(w2_raw[u][:], w2_planes[:, u[0], :, u[1] * PASS : (u[1] + 1) * PASS])
+
+        def spread_gates(e):
+            bank = dh_banks.tile([P, C // P, P], F32, name="dh")
+            for j in range(C // P):
+                nc.tensor.transpose(bank[:, j, :], gate_columns[:, e, j : j + 1].to_broadcast([P, P]), identity[:])
+            nc.vector.tensor_copy(
+                gates[:, slots_of(e)].rearrange("r (p j) -> r p j", j=C // P), bank[:].rearrange("r j p -> r p j")
+            )
+
+        def sigmoid(u, t0=0, t1=PACK, bias=0.0):
+            nc.scalar.activation(
+                in_runs(s_of[u])[:, :, t0:t1, :], as_planes(v[u][:])[:, :, t0:t1, :], SIGMOID, bias=bias
+            )
+
+        def silu(u):
+            nc.scalar.activation(m_of[u], v[u][:], SILU, scale=-1.0)
+
+        def gather(t, c0=0, c1=S):
+            window = dy[t][:].indirect(offsets[:, c0 // LIST_ROWS : c1 // LIST_ROWS])
+            nc.vector.tensor_tensor(g_planes[:, t, c0:c1], window, gates[:, c0:c1], MULT)
+
+        def lay_g(e):
+            for c0, c1 in SLOT_PARTS:
+                nc.vector.tensor_copy(
+                    as_words(g_words[e][:, c0:c1, :]), as_planes(g_planes[:, :, e * C + c0 : e * C + c1])
+                )
 
         def quantize_g(e, c0=0, c1=C):
             nc.vector.quantize_mx(
@@ -132,24 +144,24 @@ def tile_moe_bdx_mlp_silu_kernel(tc, dyT, a, w2, w1, gate, offs, out):
                 in_=g_words[e][:, c0:c1, :].rearrange("p c t -> p (c t)"),
             )
 
-        def lay_w2(e, h, copy=nc.scalar.copy, t0=0, t1=PACK):
+        def lay_w2(u, copy=nc.scalar.copy, t0=0, t1=PACK):
             copy(
-                w2_words[e, h][:, t0:t1].rearrange("p t m j -> p m j t"),
-                w2_raw[e, h][:].rearrange("p j (m t) -> p m j t", t=PACK)[:, :, :, t0:t1],
+                w2_words[u][:, t0:t1].rearrange("p t q j -> p q j t"),
+                w2_raw[u][:].rearrange("p j (q t) -> p q j t", t=PACK)[:, :, :, t0:t1],
             )
 
-        def quantize_w2(e, h):
-            for t0 in (0, 2):
-                columns = slice(t0 * P, (t0 + 2) * P)
+        def quantize_w2(u):
+            for t0, t1 in PLANE_PARTS:
+                columns = slice(t0 * P, t1 * P)
                 nc.vector.quantize_mx(
-                    out=w2_codes[e, h][:, columns].bitcast(E4M3),
-                    scales=w2_scales[e, h][:, columns],
-                    in_=w2_words[e, h][:, t0 : t0 + 2].rearrange("p t m j -> p (t m j)"),
+                    out=w2_codes[u][:, columns].bitcast(E4M3),
+                    scales=w2_scales[u][:, columns],
+                    in_=w2_words[u][:, t0:t1].rearrange("p t q j -> p (t q j)"),
                 )
 
         def lay_w1():
-            for x in range(E * HALVES):
-                nc.scalar.copy(as_words(w1_words[:, x]), as_planes(w1_raw[:, x]))
+            for matrix in range(E * HALVES):
+                nc.scalar.copy(as_words(w1_words[:, matrix]), as_planes(w1_raw[:, matrix]))
 
         def quantize_w1():
             for e in range(E):
@@ -157,143 +169,140 @@ def tile_moe_bdx_mlp_silu_kernel(tc, dyT, a, w2, w1, gate, offs, out):
                 nc.vector.quantize_mx(
                     out=w1_codes[:, columns].bitcast(E4M3),
                     scales=w1_scales[:, columns],
-                    in_=w1_words[:, e * HALVES : (e + 1) * HALVES].rearrange("p x k j -> p (x k j)"),
+                    in_=w1_words[:, e * HALVES : (e + 1) * HALVES].rearrange("p b k j -> p (b k j)"),
                 )
 
-        def make_x(e, h):
+        def make_x(u):
             for t in range(PACK):
                 dh = dh_banks.tile([P, C], F32, name="dh")
                 columns = slice(t * P, (t + 1) * P)
                 nc.tensor.matmul_mx(
                     out=dh[:],
-                    lhsT=w2_codes[e, h][:, columns].bitcast(E4M3),
-                    lhsT_scale=w2_scales[e, h][:, columns],
-                    rhs=g_codes[e][:].bitcast(E5M2),
-                    rhs_scale=g_scales[e][:],
+                    lhsT=w2_codes[u][:, columns].bitcast(E4M3),
+                    lhsT_scale=w2_scales[u][:, columns],
+                    rhs=g_codes[u[0]][:].bitcast(E5M2),
+                    rhs_scale=g_scales[u[0]][:],
                     start=True,
                     stop=True,
                 )
-                m = m_of[e, h][:, t, :]
+                m = m_of[u][:, t, :]
                 nc.vector.scalar_tensor_tensor(m, m, -1.0, dh[:], ADD, MULT)
 
-        def make_da(e, h, c0=0, c1=C, words=None, at=None):
-            words = da_words[e, h] if words is None else words
-            at = c0 if at is None else at
+        def make_da(u, c0=0, c1=C):
             nc.vector.tensor_tensor(
-                as_words(words[:, at : at + c1 - c0, :]),
-                as_planes(m_of[e, h][:, :, c0:c1]),
-                in_runs(s_of[e, h])[:, c0 // RUN : c1 // RUN],
+                as_words(da_parts[u][c0, c1]),
+                as_planes(m_of[u][:, :, c0:c1]),
+                in_runs(s_of[u])[:, c0 // RUN : c1 // RUN],
                 MULT,
             )
 
-        def quantize_da(e, h, c0=0, c1=C, words=None, at=None):
-            words = da_words[e, h] if words is None else words
-            at = c0 if at is None else at
+        def quantize_da(u, c0=0, c1=C):
             nc.vector.quantize_mx(
-                out=da_codes[e, h][:, c0:c1].bitcast(E5M2),
-                scales=da_scales[e, h][:, c0:c1],
-                in_=words[:, at : at + c1 - c0, :].rearrange("p c t -> p (c t)"),
+                out=da_codes[u][:, c0:c1].bitcast(E5M2),
+                scales=da_scales[u][:, c0:c1],
+                in_=da_parts[u][c0, c1].rearrange("p c t -> p (c t)"),
             )
 
         dx = [dx_banks.tile([P, C], F32, name="dx") for e in range(E)]
 
-        def add_to_dx(e, h):
+        def add_to_dx(u):
+            e, h = u
             columns = slice((e * HALVES + h) * K, (e * HALVES + h + 1) * K)
             nc.tensor.matmul_mx(
                 out=dx[e][:],
                 lhsT=w1_codes[:, columns].bitcast(E4M3),
                 lhsT_scale=w1_scales[:, columns],
-                rhs=da_codes[e, h][:].bitcast(E5M2),
-                rhs_scale=da_scales[e, h][:],
+                rhs=da_codes[u][:].bitcast(E5M2),
+                rhs_scale=da_scales[u][:],
                 start=(h == 0),
                 stop=(h == HALVES - 1),
             )
 
-        def put_back(e, slots):
-            nc.scalar.activation(slots, dx[e][:], COPY, scale=-1.0)
-            nc.vector.tensor_copy(result[:].indirect(offsets[:, e * (C // 16) : (e + 1) * (C // 16)]), slots)
+        def put_back(e):
+            nc.scalar.activation(dx_slots[e], dx[e][:], COPY, scale=-1.0)
+            window = result[:].indirect(offsets[:, e * C // LIST_ROWS : (e + 1) * C // LIST_ROWS])
+            nc.vector.tensor_copy(window, dx_slots[e])
+
 
         nc.sync.dma_start(gate_columns[:], gate[0, :].rearrange("(e p j) -> p e j", e=E, p=P))
         load_dy(0)
         nc.sync.dma_start(offsets[:], offs)
-        load_a(0, 0, 0, 2)
-        load_dy(1)
-        load_a(0, 0, 2, 4)
-        load_dy(2)
-        load_dy(3)
-        load_w2(0, 0)
-        load_a(1, 0)
-        load_w2(1, 0)
-        load_a(0, 1)
-        load_a(1, 1)
-        load_w2(0, 1)
-        load_w2(1, 1)
-        nc.sync.dma_start(w1_raw[:], w1_rows)
+        for t, planes in enumerate(PLANE_PARTS):
+            load_a(first, *planes)
+            load_dy(t + 1)
+        load_dy(PACK - 1)
+        load_w2(first)
+        load_a(second)
+        load_w2(second)
+        load_a(third)
+        load_a(last)
+        load_w2(third)
+        load_w2(last)
+        nc.sync.dma_start(w1_raw[:], w1_planes)
 
-        nc.vector.memset(warm[:], 1.0)
-        nc.scalar.activation(warm[:], warm[:], SIGMOID)
+
         make_identity(nc, identity[:])
-        spread_gates(0, nc.vector.tensor_copy)
-        spread_gates(1, nc.vector.tensor_copy)
+        for e in range(E):
+            spread_gates(e)
         nc.vector.memset(result[:], 0.0)
 
-        gather(0, 0, C)
-        gather(0, C, S)
-        for t in range(1, PACK - 1):
-            gather(t)
-        gather(PACK - 1, 0, C)
-        gather(PACK - 1, C, S)
-        sigmoid(0, 0, 0, 2)
-        sigmoid(0, 0, 2, 4)
-        silu(0, 0)
-        lay_w2(0, 0)
-        lay_g(0, 0, C // 2)
-        lay_g(0, C // 2, C)
-        quantize_g(0, 0, C // 2)
-        quantize_g(0, C // 2, C)
-        quantize_w2(0, 0)
-        lay_g(1, 0, C // 2)
-        lay_g(1, C // 2, C)
+        for t in range(PACK):
+            for slots in EXPERT_PARTS if t in (0, PACK - 1) else ((0, S),):
+                gather(t, *slots)
+        for planes in PLANE_PARTS:
+            sigmoid(first, *planes)
+        silu(first)
+        lay_w2(first)
+        lay_g(0)
+        for slots in SLOT_PARTS:
+            quantize_g(0, *slots)
+        quantize_w2(first)
+        lay_g(1)
         quantize_g(1)
-        make_x(0, 0)
-        silu(1, 0)
-        lay_w2(1, 0)
-        quantize_w2(1, 0)
-        make_da(0, 0, *da_first[0])
-        quantize_da(0, 0, *da_first[0])
-        make_x(1, 0)
-        silu(0, 1)
-        silu(1, 1)
+        make_x(first)
+
+
+        silu(second)
+        lay_w2(second)
+        quantize_w2(second)
+        make_da(first, *SLOT_PARTS[0])
+        quantize_da(first, *SLOT_PARTS[0])
+        make_x(second)
+
+        silu(third)
+        silu(last)
         nc.scalar.activation(zero[:], m_of[last][:, 0, 0:1], COPY, scale=0.0)
-        lay_w2(0, 1, nc.vector.tensor_copy, 0, 2)
-        lay_w2(0, 1, nc.vector.tensor_copy, 2, 4)
-        quantize_w2(0, 1)
-        make_da(0, 0, *da_first[1])
-        quantize_da(0, 0, *da_first[1])
-        make_x(0, 1)
-        sigmoid(1, 0, bias=zero[:])
-        make_da(1, 0)
-        quantize_da(1, 0)
-        lay_w2(1, 1)
-        sigmoid(0, 1)
-        quantize_w2(1, 1)
-        make_da(0, 1, 0, C // 2)
-        make_da(0, 1, C // 2, C)
-        quantize_da(0, 1)
-        make_x(1, 1)
-        sigmoid(1, 1)
+        for tiles in PLANE_PARTS:
+            lay_w2(third, nc.vector.tensor_copy, *tiles)
+        quantize_w2(third)
+        make_da(first, *SLOT_PARTS[1])
+        quantize_da(first, *SLOT_PARTS[1])
+        make_x(third)
+
+
+        sigmoid(second, bias=zero[:])
+        make_da(second)
+        quantize_da(second)
+        lay_w2(last)
+        sigmoid(third)
+        quantize_w2(last)
+        for slots in SLOT_PARTS:
+            make_da(third, *slots)
+        quantize_da(third)
+        make_x(last)
+        sigmoid(last)
         lay_w1()
         quantize_w1()
-        make_da(1, 1, 0, C // 2)
-        make_da(1, 1, C // 2, C)
-        add_to_dx(0, 0)
-        add_to_dx(1, 0)
-        add_to_dx(0, 1)
-        quantize_da(1, 1, 0, C // 2)
-        quantize_da(1, 1, C // 2, C)
-        add_to_dx(1, 1)
-        put_back(0, tail[:, 0:C])
-        put_back(1, g_rows[:, 0, 0:C])
+        for slots in SLOT_PARTS:
+            make_da(last, *slots)
+        for u in units[:-1]:
+            add_to_dx(u)
+        for slots in SLOT_PARTS:
+            quantize_da(last, *slots)
+        add_to_dx(last)
+        for e in range(E):
+            put_back(e)
 
-        for q, queue in enumerate((nc.sync, nc.scalar, nc.sync, nc.scalar)):
-            queue.dma_start(out[:, q * T // 4 : (q + 1) * T // 4], result[:, q * T // 4 : (q + 1) * T // 4])
+        for part in range(STORES):
+            columns = slice(part * T // STORES, (part + 1) * T // STORES)
+            (nc.sync, nc.scalar)[part % 2].dma_start(out[:, columns], result[:, columns])

@@ -13,7 +13,7 @@ E5M2 = mybir.dt.float8_e5m2_x4
 ADD = mybir.AluOpType.add
 MULT = mybir.AluOpType.mult
 COPY = mybir.ActivationFunctionType.Copy
-SIGMOID = mybir.ActivationFunctionType.Sigmoid
+TANH = mybir.ActivationFunctionType.Tanh
 SILU = mybir.ActivationFunctionType.Silu
 
 P = 128
@@ -39,8 +39,8 @@ def tile_moe_bdx_mlp_silu_kernel(tc, dyT, a, w2, w1, gate, offs, out):
     dy_planes = dyT.rearrange("(p t) s -> p t s", t=PACK)
     a_planes = a.rearrange("(h p t) s -> p h t s", h=HALVES, t=PACK)
     w2_planes = w2.rearrange("e (p j) i -> p e j i", j=PACK)
-    w1_planes = w1.rearrange("e (h p j) k -> p (e h) j k", h=HALVES, j=PACK)
-    units = [(e, h) for h in range(HALVES) for e in range(E)]
+    w1_planes = w1.rearrange("e (h p j) k -> p e h j k", h=HALVES, j=PACK)
+    units = [(e, h) for e in range(E) for h in range(HALVES)]
     first, second, third, last = units
 
     with ExitStack() as ctx:
@@ -50,43 +50,51 @@ def tile_moe_bdx_mlp_silu_kernel(tc, dyT, a, w2, w1, gate, offs, out):
         dx_banks = ctx.enter_context(tc.psum_pool(name="dx_banks", bufs=2))
 
         offsets = lists.tile([P, S // LIST_ROWS], U16, name="offsets")
-        gates = keep.tile([P, S], F32, name="gates")
         dy = [keep.tile([P, T], F32, name=f"dy{t}") for t in range(PACK)]
+        pitch = C + C // 2
+        g_first = keep.tile([P, PACK * pitch], F32, name="g_first")
+        g_second = keep.tile([P, PACK * C + 3 * C // 2], F32, name="g_second", align_bytes=64)
+        g_planes = [
+            g_first[:].rearrange("p (t c) -> p t c", t=PACK)[:, :, 0:C],
+            g_second[:, 0 : PACK * C].rearrange("p (t c) -> p t c", t=PACK),
+        ]
+        gates_first = keep.tile([P, C], F32, name="gates_first")
+        gates = [gates_first[:], g_first[:, 2 * pitch + C // 2 : 2 * pitch + C // 2 + C]]
         w2_raw = {u: keep.tile([P, PACK, PASS], F32, name=f"w2_raw{u[0]}{u[1]}") for u in units}
         v = {u: keep.tile([P, PACK, C], F32, name=f"v{u[0]}{u[1]}") for u in units}
-        spare = {u: keep.tile([P, PACK, C], F32, name=f"spare{u[0]}{u[1]}") for u in units[:-1]}
-        tail = keep.tile([P, C // 2 + PACK * C], F32, name="tail")
-        m_of = {
-            first: v[first][:],
-            second: spare[second][:],
-            third: spare[third][:],
-            last: tail[:, C // 2 :].rearrange("p (t c) -> p t c", t=PACK),
-        }
-        s_of = {first: spare[first][:], second: w2_raw[first][:], third: v[second][:], last: v[third][:]}
-        w1_raw = keep.tile([P, E * HALVES, PACK, K], F32, name="w1_raw")
-        g_planes = keep.tile([P, PACK, S], F32, name="g_planes")
+        m_first = keep.tile([P, PACK, C], F32, name="m_first")
+        th_first = keep.tile([P, PACK, C], F32, name="th_first")
+        m_of = {first: m_first[:], second: v[first][:], third: v[second][:], last: v[third][:]}
+        th_of = {u: th_first[:] if u == first else w2_raw[u][:] for u in units}
+        w1_raw = [keep.tile([P, HALVES, PACK, K], F32, name=f"w1_raw{e}") for e in range(E)]
 
-        g_codes = [keep.tile([P, C], U32, name=f"g_codes{e}", align_bytes=64) for e in range(E)]
-        g_scales = [keep.tile([P, C], U8, name=f"g_scales{e}", align_bytes=64) for e in range(E)]
-        w2_words = {u: keep.tile([P, PACK, P, PACK], BF16, name=f"w2_words{u[0]}{u[1]}", align_bytes=64) for u in units}
+        w2_words = {u: keep.tile([P, PACK, P, PACK], BF16, name=f"w2_words{u[0]}{u[1]}", align_bytes=64)[:] for u in units[1:]}
+        w2_words[first] = (
+            g_second[:, PACK * C - C // 2 :]
+            .bitcast(BF16)
+            .rearrange("p (t q j) -> p t q j", t=PACK, j=PACK)
+        )
         w2_codes = {u: keep.tile([P, PASS], U32, name=f"w2_codes{u[0]}{u[1]}", align_bytes=64) for u in units}
         w2_scales = {u: keep.tile([P, PASS], U8, name=f"w2_scales{u[0]}{u[1]}", align_bytes=64) for u in units}
-        w1_words = keep.tile([P, E * HALVES, K, PACK], BF16, name="w1_words", align_bytes=64)
-        g_first = keep.tile([P, C, PACK], BF16, name="g_first", align_bytes=64)
-        freed = {u: w2_words[u][:].rearrange("p t m j -> p (t m) j") for u in units}
-        g_words = [g_first[:], freed[first]]
-        da_words = {second: freed[first], third: freed[last], last: w1_words[:].rearrange("p b k j -> p (b k) j")}
-        da_parts = {u: {(c0, c1): da_words[u][:, c0:c1, :] for c0, c1 in SLOT_PARTS + ((0, C),)} for u in units[1:]}
-        da_parts[first] = {part: freed[u][:, 0 : C // 2, :] for part, u in zip(SLOT_PARTS, (second, third))}
-        w1_codes = keep.tile([P, E * HALVES * K], U32, name="w1_codes", align_bytes=64)
-        w1_scales = keep.tile([P, E * HALVES * K], U8, name="w1_scales", align_bytes=64)
+        w1_words = [keep.tile([P, HALVES, K, PACK], BF16, name=f"w1_words{e}", align_bytes=64) for e in range(E)]
+        g_words = [keep.tile([P, C, PACK], BF16, name=f"g_words{e}", align_bytes=64) for e in range(E)]
+        g_codes = [keep.tile([P, C], U32, name=f"g_codes{e}", align_bytes=64)[:] for e in range(E)]
+        g_scales = [keep.tile([P, C], U8, name=f"g_scales{e}", align_bytes=64) for e in range(E)]
+        freed = {u: w2_words[u].rearrange("p t m j -> p (t m) j") for u in units}
+        da_words = {first: freed[second], second: freed[third], third: freed[last], last: g_words[1][:]}
+        w1_codes = [keep.tile([P, HALVES * K], U32, name=f"w1_codes{e}", align_bytes=64) for e in range(E)]
+        w1_scales = [keep.tile([P, HALVES * K], U8, name=f"w1_scales{e}", align_bytes=64) for e in range(E)]
         da_codes = {u: keep.tile([P, C], U32, name=f"da_codes{u[0]}{u[1]}", align_bytes=64) for u in units}
         da_scales = {u: keep.tile([P, C], U8, name=f"da_scales{u[0]}{u[1]}", align_bytes=64) for u in units}
         result = keep.tile([P, T], F32, name="result")
         gate_columns = keep.tile([P, E, C // P], F32, name="gate_columns")
         identity = keep.tile([P, P], F32, name="identity")
-        zero = keep.tile([P, 1], F32, name="zero")
-        dx_slots = [tail[:, 0:C], g_planes[:, 0, 0:C]]
+        held = m_of[last].rearrange("p t c -> p (t c)")[:, 0 : C // 2]
+        dx_slots = {
+            (0, 0, C // 2): g_planes[0][:, 0, 0 : C // 2],
+            (0, C // 2, C): held,
+            (1, 0, C): g_planes[1][:, 0, :],
+        }
 
 
         def slots_of(e):
@@ -111,31 +119,27 @@ def tile_moe_bdx_mlp_silu_kernel(tc, dyT, a, w2, w1, gate, offs, out):
         def load_w2(u):
             nc.sync.dma_start(w2_raw[u][:], w2_planes[:, u[0], :, u[1] * PASS : (u[1] + 1) * PASS])
 
+        def load_w1(e):
+            nc.sync.dma_start(w1_raw[e][:], w1_planes[:, e])
+
         def spread_gates(e):
             bank = dh_banks.tile([P, C // P, P], F32, name="dh")
             for j in range(C // P):
                 nc.tensor.transpose(bank[:, j, :], gate_columns[:, e, j : j + 1].to_broadcast([P, P]), identity[:])
-            nc.vector.tensor_copy(
-                gates[:, slots_of(e)].rearrange("r (p j) -> r p j", j=C // P), bank[:].rearrange("r j p -> r p j")
-            )
+            nc.vector.tensor_copy(gates[e].rearrange("r (p j) -> r p j", j=C // P), bank[:].rearrange("r j p -> r p j"))
 
-        def sigmoid(u, t0=0, t1=PACK, bias=0.0):
-            nc.scalar.activation(
-                in_runs(s_of[u])[:, :, t0:t1, :], as_planes(v[u][:])[:, :, t0:t1, :], SIGMOID, bias=bias
-            )
+        def silu(u, t0=0, t1=PACK):
+            nc.scalar.activation(in_runs(m_of[u])[:, :, t0:t1, :], as_planes(v[u][:])[:, :, t0:t1, :], SILU, scale=-1.0)
 
-        def silu(u):
-            nc.scalar.activation(m_of[u], v[u][:], SILU, scale=-1.0)
+        def tanh(u, t0=0, t1=PACK):
+            nc.scalar.activation(in_runs(th_of[u])[:, :, t0:t1, :], as_planes(v[u][:])[:, :, t0:t1, :], TANH, scale=0.5)
 
-        def gather(t, c0=0, c1=S):
-            window = dy[t][:].indirect(offsets[:, c0 // LIST_ROWS : c1 // LIST_ROWS])
-            nc.vector.tensor_tensor(g_planes[:, t, c0:c1], window, gates[:, c0:c1], MULT)
+        def gather(t, e, c0=0, c1=C):
+            window = dy[t][:].indirect(offsets[:, (e * C + c0) // LIST_ROWS : (e * C + c1) // LIST_ROWS])
+            nc.vector.tensor_tensor(g_planes[e][:, t, c0:c1], window, gates[e][:, c0:c1], MULT)
 
-        def lay_g(e):
-            for c0, c1 in SLOT_PARTS:
-                nc.vector.tensor_copy(
-                    as_words(g_words[e][:, c0:c1, :]), as_planes(g_planes[:, :, e * C + c0 : e * C + c1])
-                )
+        def lay_g(e, copy, c0=0, c1=C):
+            copy(as_words(g_words[e][:, c0:c1, :]), as_planes(g_planes[e][:, :, c0:c1]))
 
         def quantize_g(e, c0=0, c1=C):
             nc.vector.quantize_mx(
@@ -144,14 +148,14 @@ def tile_moe_bdx_mlp_silu_kernel(tc, dyT, a, w2, w1, gate, offs, out):
                 in_=g_words[e][:, c0:c1, :].rearrange("p c t -> p (c t)"),
             )
 
-        def lay_w2(u, copy=nc.scalar.copy, t0=0, t1=PACK):
-            copy(
+        def lay_w2(u, t0=0, t1=PACK):
+            nc.scalar.copy(
                 w2_words[u][:, t0:t1].rearrange("p t q j -> p q j t"),
                 w2_raw[u][:].rearrange("p j (q t) -> p q j t", t=PACK)[:, :, :, t0:t1],
             )
 
-        def quantize_w2(u):
-            for t0, t1 in PLANE_PARTS:
+        def quantize_w2(u, parts=PLANE_PARTS):
+            for t0, t1 in parts:
                 columns = slice(t0 * P, t1 * P)
                 nc.vector.quantize_mx(
                     out=w2_codes[u][:, columns].bitcast(E4M3),
@@ -159,18 +163,16 @@ def tile_moe_bdx_mlp_silu_kernel(tc, dyT, a, w2, w1, gate, offs, out):
                     in_=w2_words[u][:, t0:t1].rearrange("p t q j -> p (t q j)"),
                 )
 
-        def lay_w1():
-            for matrix in range(E * HALVES):
-                nc.scalar.copy(as_words(w1_words[:, matrix]), as_planes(w1_raw[:, matrix]))
+        def lay_w1(e):
+            for h in range(HALVES):
+                nc.scalar.copy(as_words(w1_words[e][:, h]), as_planes(w1_raw[e][:, h]))
 
-        def quantize_w1():
-            for e in range(E):
-                columns = slice(e * HALVES * K, (e + 1) * HALVES * K)
-                nc.vector.quantize_mx(
-                    out=w1_codes[:, columns].bitcast(E4M3),
-                    scales=w1_scales[:, columns],
-                    in_=w1_words[:, e * HALVES : (e + 1) * HALVES].rearrange("p b k j -> p (b k j)"),
-                )
+        def quantize_w1(e):
+            nc.vector.quantize_mx(
+                out=w1_codes[e][:].bitcast(E4M3),
+                scales=w1_scales[e][:],
+                in_=w1_words[e][:].rearrange("p h k j -> p (h k j)"),
+            )
 
         def make_x(u):
             for t in range(PACK):
@@ -180,65 +182,81 @@ def tile_moe_bdx_mlp_silu_kernel(tc, dyT, a, w2, w1, gate, offs, out):
                     out=dh[:],
                     lhsT=w2_codes[u][:, columns].bitcast(E4M3),
                     lhsT_scale=w2_scales[u][:, columns],
-                    rhs=g_codes[u[0]][:].bitcast(E5M2),
+                    rhs=g_codes[u[0]].bitcast(E5M2),
                     rhs_scale=g_scales[u[0]][:],
                     start=True,
                     stop=True,
                 )
-                m = m_of[u][:, t, :]
-                nc.vector.scalar_tensor_tensor(m, m, -1.0, dh[:], ADD, MULT)
+                for c0, c1 in SLOT_PARTS if t == PACK - 1 else ((0, C),):
+                    m = in_runs(m_of[u])[:, c0 // RUN : c1 // RUN, t, :]
+                    nc.vector.scalar_tensor_tensor(
+                        m, m, -1.0, dh[:, c0:c1].rearrange("p (c i) -> p c i", i=RUN), ADD, MULT
+                    )
 
-        def make_da(u, c0=0, c1=C):
-            nc.vector.tensor_tensor(
-                as_words(da_parts[u][c0, c1]),
-                as_planes(m_of[u][:, :, c0:c1]),
-                in_runs(s_of[u])[:, c0 // RUN : c1 // RUN],
-                MULT,
-            )
+        def make_da(u):
+            for c0, c1 in SLOT_PARTS:
+                stream = slice(c0 * PACK, c1 * PACK)
+                nc.vector.scalar_tensor_tensor(
+                    da_words[u][:, c0:c1, :].rearrange("p (i c) t -> p (c t) i", i=RUN),
+                    th_of[u].rearrange("p t c -> p (t c)")[:, stream].rearrange("p (n i) -> p n i", i=RUN),
+                    1.0,
+                    m_of[u].rearrange("p t c -> p (t c)")[:, stream].rearrange("p (n i) -> p n i", i=RUN),
+                    ADD,
+                    MULT,
+                )
 
-        def quantize_da(u, c0=0, c1=C):
-            nc.vector.quantize_mx(
-                out=da_codes[u][:, c0:c1].bitcast(E5M2),
-                scales=da_scales[u][:, c0:c1],
-                in_=da_parts[u][c0, c1].rearrange("p c t -> p (c t)"),
-            )
+        def quantize_da(u):
+            for c0, c1 in SLOT_PARTS:
+                nc.vector.quantize_mx(
+                    out=da_codes[u][:, c0:c1].bitcast(E5M2),
+                    scales=da_scales[u][:, c0:c1],
+                    in_=da_words[u][:, c0:c1, :].rearrange("p c t -> p (c t)"),
+                )
 
         dx = [dx_banks.tile([P, C], F32, name="dx") for e in range(E)]
 
         def add_to_dx(u):
             e, h = u
-            columns = slice((e * HALVES + h) * K, (e * HALVES + h + 1) * K)
+            columns = slice(h * K, (h + 1) * K)
             nc.tensor.matmul_mx(
                 out=dx[e][:],
-                lhsT=w1_codes[:, columns].bitcast(E4M3),
-                lhsT_scale=w1_scales[:, columns],
+                lhsT=w1_codes[e][:, columns].bitcast(E4M3),
+                lhsT_scale=w1_scales[e][:, columns],
                 rhs=da_codes[u][:].bitcast(E5M2),
                 rhs_scale=da_scales[u][:],
                 start=(h == 0),
                 stop=(h == HALVES - 1),
             )
 
-        def put_back(e):
-            nc.scalar.activation(dx_slots[e], dx[e][:], COPY, scale=-1.0)
-            window = result[:].indirect(offsets[:, e * C // LIST_ROWS : (e + 1) * C // LIST_ROWS])
-            nc.vector.tensor_copy(window, dx_slots[e])
+        def put_back(e, c0, c1):
+            slots = dx_slots[e, c0, c1]
+            nc.scalar.activation(
+                slots.rearrange("p (k c i) -> p k c i", c=C // 2 // RUN, i=RUN),
+                dx[e][:, c0:c1].rearrange("p (k i c) -> p k c i", c=C // 2 // RUN, i=RUN),
+                COPY,
+                scale=-0.5,
+            )
+            window = result[:].indirect(offsets[:, (e * C + c0) // LIST_ROWS : (e * C + c1) // LIST_ROWS])
+            nc.vector.tensor_copy(window, slots)
 
 
         nc.sync.dma_start(gate_columns[:], gate[0, :].rearrange("(e p j) -> p e j", e=E, p=P))
         load_dy(0)
         nc.sync.dma_start(offsets[:], offs)
-        for t, planes in enumerate(PLANE_PARTS):
-            load_a(first, *planes)
-            load_dy(t + 1)
-        load_dy(PACK - 1)
+        load_a(first, 0, 2)
+        load_dy(1)
+        load_a(first, 2, 4)
+        load_dy(2)
+        load_dy(3)
         load_w2(first)
-        load_a(second)
         load_w2(second)
-        load_a(third)
-        load_a(last)
+        load_a(second)
         load_w2(third)
+        load_a(third)
+        load_w1(0)
         load_w2(last)
-        nc.sync.dma_start(w1_raw[:], w1_planes)
+        load_a(last)
+        load_w1(1)
 
 
         make_identity(nc, identity[:])
@@ -246,62 +264,69 @@ def tile_moe_bdx_mlp_silu_kernel(tc, dyT, a, w2, w1, gate, offs, out):
             spread_gates(e)
         nc.vector.memset(result[:], 0.0)
 
-        for t in range(PACK):
-            for slots in EXPERT_PARTS if t in (0, PACK - 1) else ((0, S),):
-                gather(t, *slots)
+        for t in range(2):
+            for e in range(E):
+                gather(t, e)
+        low, high = SLOT_PARTS
+        gather(2, 1)
+        gather(2, 0, *low)
+        gather(3, 1, *low)
+        gather(3, 0, *low)
+        gather(2, 0, *high)
+        gather(3, 0, *high)
         for planes in PLANE_PARTS:
-            sigmoid(first, *planes)
-        silu(first)
+            silu(first, *planes)
+            tanh(first, *planes)
+        lay_g(1, nc.scalar.copy, *low)
         lay_w2(first)
-        lay_g(0)
+        for slots in SLOT_PARTS:
+            lay_g(0, nc.vector.tensor_copy, *slots)
         for slots in SLOT_PARTS:
             quantize_g(0, *slots)
-        quantize_w2(first)
-        lay_g(1)
-        quantize_g(1)
+        quantize_g(1, *low)
+        quantize_w2(first, ((0, 1), (1, 2), (2, 4)))
+        gather(3, 1, *high)
         make_x(first)
 
-
-        silu(second)
         lay_w2(second)
         quantize_w2(second)
-        make_da(first, *SLOT_PARTS[0])
-        quantize_da(first, *SLOT_PARTS[0])
+        lay_g(1, nc.scalar.copy, *high)
+        make_da(first)
+        quantize_da(first)
+        quantize_g(1, *high)
+        silu(second)
         make_x(second)
+        tanh(second)
 
-        silu(third)
-        silu(last)
-        nc.scalar.activation(zero[:], m_of[last][:, 0, 0:1], COPY, scale=0.0)
-        for tiles in PLANE_PARTS:
-            lay_w2(third, nc.vector.tensor_copy, *tiles)
+        lay_w2(third)
         quantize_w2(third)
-        make_da(first, *SLOT_PARTS[1])
-        quantize_da(first, *SLOT_PARTS[1])
-        make_x(third)
-
-
-        sigmoid(second, bias=zero[:])
         make_da(second)
         quantize_da(second)
+        silu(third)
+        lay_w1(0)
+        quantize_w1(0)
+        make_x(third)
+
         lay_w2(last)
-        sigmoid(third)
         quantize_w2(last)
-        for slots in SLOT_PARTS:
-            make_da(third, *slots)
+        add_to_dx(first)
+        add_to_dx(second)
+        put_back(0, *low)
+        tanh(third)
+        make_da(third)
         quantize_da(third)
+        silu(last)
+        lay_w1(1)
         make_x(last)
-        sigmoid(last)
-        lay_w1()
-        quantize_w1()
-        for slots in SLOT_PARTS:
-            make_da(last, *slots)
-        for u in units[:-1]:
-            add_to_dx(u)
-        for slots in SLOT_PARTS:
-            quantize_da(last, *slots)
+        quantize_w1(1)
+        tanh(last)
+
+        make_da(last)
+        add_to_dx(third)
+        quantize_da(last)
         add_to_dx(last)
-        for e in range(E):
-            put_back(e)
+        put_back(0, *SLOT_PARTS[1])
+        put_back(1, 0, C)
 
         for part in range(STORES):
             columns = slice(part * T // STORES, (part + 1) * T // STORES)

@@ -24,6 +24,7 @@ PASS = P * PACK
 HALVES = H // PASS
 RUN = 4
 LIST_ROWS = 16
+EARLY = 320
 STORES = 4
 
 SLOT_PARTS = ((0, C // 2), (C // 2, C))
@@ -74,25 +75,26 @@ def tile_moe_bdx_mlp_silu_kernel(tc, dyT, a, w2, w1, gate, offs, out):
             .bitcast(BF16)
             .rearrange("p (t q j) -> p t q j", t=PACK, j=PACK)
         )
-        w2_codes = {u: keep.tile([P, PASS], U32, name=f"w2_codes{u[0]}{u[1]}", align_bytes=64) for u in units}
-        w2_scales = {u: keep.tile([P, PASS], U8, name=f"w2_scales{u[0]}{u[1]}", align_bytes=64) for u in units}
+        w2_codes = keep.tile([P, PASS], U32, name="w2_codes", align_bytes=64)
+        w2_scales = keep.tile([P, PASS], U8, name="w2_scales", align_bytes=64)
         w1_words = [keep.tile([P, HALVES, K, PACK], BF16, name=f"w1_words{e}", align_bytes=64) for e in range(E)]
         g_words = [keep.tile([P, C, PACK], BF16, name=f"g_words{e}", align_bytes=64) for e in range(E)]
         g_codes = [keep.tile([P, C], U32, name=f"g_codes{e}", align_bytes=64)[:] for e in range(E)]
         g_scales = [keep.tile([P, C], U8, name=f"g_scales{e}", align_bytes=64) for e in range(E)]
         freed = {u: w2_words[u].rearrange("p t m j -> p (t m) j") for u in units}
         da_words = {first: freed[second], second: freed[third], third: freed[last], last: g_words[1][:]}
-        w1_codes = [keep.tile([P, HALVES * K], U32, name=f"w1_codes{e}", align_bytes=64) for e in range(E)]
-        w1_scales = [keep.tile([P, HALVES * K], U8, name=f"w1_scales{e}", align_bytes=64) for e in range(E)]
+        w1_codes_first = keep.tile([P, HALVES * K], U32, name="w1_codes_first", align_bytes=64)
+        w1_scales_first = keep.tile([P, HALVES * K], U8, name="w1_scales_first", align_bytes=64)
+        w1_codes = [w1_codes_first[:], w2_codes[:, 0 : HALVES * K]]
+        w1_scales = [w1_scales_first[:], w2_scales[:, 0 : HALVES * K]]
         da_codes = {u: keep.tile([P, C], U32, name=f"da_codes{u[0]}{u[1]}", align_bytes=64) for u in units}
         da_scales = {u: keep.tile([P, C], U8, name=f"da_scales{u[0]}{u[1]}", align_bytes=64) for u in units}
         result = keep.tile([P, T], F32, name="result")
         gate_columns = keep.tile([P, E, C // P], F32, name="gate_columns")
         identity = keep.tile([P, P], F32, name="identity")
-        held = m_of[last].rearrange("p t c -> p (t c)")[:, 0 : C // 2]
         dx_slots = {
-            (0, 0, C // 2): g_planes[0][:, 0, 0 : C // 2],
-            (0, C // 2, C): held,
+            (0, 0, EARLY): g_planes[0][:, 0, 0:EARLY],
+            (0, EARLY, C): v[last][:, 0, EARLY:C],
             (1, 0, C): g_planes[1][:, 0, :],
         }
 
@@ -158,8 +160,8 @@ def tile_moe_bdx_mlp_silu_kernel(tc, dyT, a, w2, w1, gate, offs, out):
             for t0, t1 in parts:
                 columns = slice(t0 * P, t1 * P)
                 nc.vector.quantize_mx(
-                    out=w2_codes[u][:, columns].bitcast(E4M3),
-                    scales=w2_scales[u][:, columns],
+                    out=w2_codes[:, columns].bitcast(E4M3),
+                    scales=w2_scales[:, columns],
                     in_=w2_words[u][:, t0:t1].rearrange("p t q j -> p (t q j)"),
                 )
 
@@ -169,8 +171,8 @@ def tile_moe_bdx_mlp_silu_kernel(tc, dyT, a, w2, w1, gate, offs, out):
 
         def quantize_w1(e):
             nc.vector.quantize_mx(
-                out=w1_codes[e][:].bitcast(E4M3),
-                scales=w1_scales[e][:],
+                out=w1_codes[e].bitcast(E4M3),
+                scales=w1_scales[e],
                 in_=w1_words[e][:].rearrange("p h k j -> p (h k j)"),
             )
 
@@ -180,27 +182,23 @@ def tile_moe_bdx_mlp_silu_kernel(tc, dyT, a, w2, w1, gate, offs, out):
                 columns = slice(t * P, (t + 1) * P)
                 nc.tensor.matmul_mx(
                     out=dh[:],
-                    lhsT=w2_codes[u][:, columns].bitcast(E4M3),
-                    lhsT_scale=w2_scales[u][:, columns],
+                    lhsT=w2_codes[:, columns].bitcast(E4M3),
+                    lhsT_scale=w2_scales[:, columns],
                     rhs=g_codes[u[0]].bitcast(E5M2),
                     rhs_scale=g_scales[u[0]][:],
                     start=True,
                     stop=True,
                 )
-                for c0, c1 in SLOT_PARTS if t == PACK - 1 else ((0, C),):
-                    m = in_runs(m_of[u])[:, c0 // RUN : c1 // RUN, t, :]
-                    nc.vector.scalar_tensor_tensor(
-                        m, m, -1.0, dh[:, c0:c1].rearrange("p (c i) -> p c i", i=RUN), ADD, MULT
-                    )
+                m = in_runs(m_of[u])[:, :, t, :]
+                nc.vector.scalar_tensor_tensor(m, m, -1.0, dh[:].rearrange("p (c i) -> p c i", i=RUN), ADD, MULT)
 
         def make_da(u):
-            for c0, c1 in SLOT_PARTS:
-                stream = slice(c0 * PACK, c1 * PACK)
+            for i0, i1 in ((0, RUN // 2), (RUN // 2, RUN)):
                 nc.vector.scalar_tensor_tensor(
-                    da_words[u][:, c0:c1, :].rearrange("p (i c) t -> p (c t) i", i=RUN),
-                    th_of[u].rearrange("p t c -> p (t c)")[:, stream].rearrange("p (n i) -> p n i", i=RUN),
+                    da_words[u].rearrange("p (i c) t -> p (c t) i", i=RUN)[:, :, i0:i1],
+                    th_of[u].rearrange("p t c -> p (t c)").rearrange("p (n i) -> p n i", i=RUN)[:, :, i0:i1],
                     1.0,
-                    m_of[u].rearrange("p t c -> p (t c)")[:, stream].rearrange("p (n i) -> p n i", i=RUN),
+                    m_of[u].rearrange("p t c -> p (t c)").rearrange("p (n i) -> p n i", i=RUN)[:, :, i0:i1],
                     ADD,
                     MULT,
                 )
@@ -231,8 +229,8 @@ def tile_moe_bdx_mlp_silu_kernel(tc, dyT, a, w2, w1, gate, offs, out):
         def put_back(e, c0, c1):
             slots = dx_slots[e, c0, c1]
             nc.scalar.activation(
-                slots.rearrange("p (k c i) -> p k c i", c=C // 2 // RUN, i=RUN),
-                dx[e][:, c0:c1].rearrange("p (k i c) -> p k c i", c=C // 2 // RUN, i=RUN),
+                slots.rearrange("p (c i) -> p c i", i=RUN),
+                dx[e][:].rearrange("p (i c) -> p c i", i=RUN)[:, c0 // RUN : c1 // RUN],
                 COPY,
                 scale=-0.5,
             )
@@ -290,16 +288,16 @@ def tile_moe_bdx_mlp_silu_kernel(tc, dyT, a, w2, w1, gate, offs, out):
 
         lay_w2(second)
         quantize_w2(second)
-        lay_g(1, nc.scalar.copy, *high)
         make_da(first)
         quantize_da(first)
-        quantize_g(1, *high)
         silu(second)
         make_x(second)
-        tanh(second)
 
         lay_w2(third)
         quantize_w2(third)
+        tanh(second)
+        lay_g(1, nc.scalar.copy, *high)
+        quantize_g(1, *high)
         make_da(second)
         quantize_da(second)
         silu(third)
@@ -311,7 +309,7 @@ def tile_moe_bdx_mlp_silu_kernel(tc, dyT, a, w2, w1, gate, offs, out):
         quantize_w2(last)
         add_to_dx(first)
         add_to_dx(second)
-        put_back(0, *low)
+        put_back(0, 0, EARLY)
         tanh(third)
         make_da(third)
         quantize_da(third)
@@ -325,7 +323,7 @@ def tile_moe_bdx_mlp_silu_kernel(tc, dyT, a, w2, w1, gate, offs, out):
         add_to_dx(third)
         quantize_da(last)
         add_to_dx(last)
-        put_back(0, *SLOT_PARTS[1])
+        put_back(0, EARLY, C)
         put_back(1, 0, C)
 
         for part in range(STORES):

@@ -13,6 +13,7 @@ E5M2 = mybir.dt.float8_e5m2_x4
 ADD = mybir.AluOpType.add
 MULT = mybir.AluOpType.mult
 COPY = mybir.ActivationFunctionType.Copy
+IDENTITY = mybir.ActivationFunctionType.Identity
 TANH = mybir.ActivationFunctionType.Tanh
 SILU = mybir.ActivationFunctionType.Silu
 
@@ -24,7 +25,7 @@ PASS = P * PACK
 HALVES = H // PASS
 RUN = 4
 LIST_ROWS = 16
-EARLY = 320
+EARLY = 256
 STORES = 4
 
 SLOT_PARTS = ((0, C // 2), (C // 2, C))
@@ -52,15 +53,9 @@ def tile_moe_bdx_mlp_silu_kernel(tc, dyT, a, w2, w1, gate, offs, out):
 
         offsets = lists.tile([P, S // LIST_ROWS], U16, name="offsets")
         dy = [keep.tile([P, T], F32, name=f"dy{t}") for t in range(PACK)]
-        pitch = C + C // 2
-        g_first = keep.tile([P, PACK * pitch], F32, name="g_first")
-        g_second = keep.tile([P, PACK * C + 3 * C // 2], F32, name="g_second", align_bytes=64)
-        g_planes = [
-            g_first[:].rearrange("p (t c) -> p t c", t=PACK)[:, :, 0:C],
-            g_second[:, 0 : PACK * C].rearrange("p (t c) -> p t c", t=PACK),
-        ]
-        gates_first = keep.tile([P, C], F32, name="gates_first")
-        gates = [gates_first[:], g_first[:, 2 * pitch + C // 2 : 2 * pitch + C // 2 + C]]
+        g_room = keep.tile([P, PACK * S + 3 * C // 2], F32, name="g_room", align_bytes=64)
+        g_planes = g_room[:, 0 : PACK * S].rearrange("p (t s) -> p t s", t=PACK)
+        gates = keep.tile([P, S], F32, name="gates")
         w2_raw = {u: keep.tile([P, PACK, PASS], F32, name=f"w2_raw{u[0]}{u[1]}") for u in units}
         v = {u: keep.tile([P, PACK, C], F32, name=f"v{u[0]}{u[1]}") for u in units}
         m_first = keep.tile([P, PACK, C], F32, name="m_first")
@@ -71,7 +66,7 @@ def tile_moe_bdx_mlp_silu_kernel(tc, dyT, a, w2, w1, gate, offs, out):
 
         w2_words = {u: keep.tile([P, PACK, P, PACK], BF16, name=f"w2_words{u[0]}{u[1]}", align_bytes=64)[:] for u in units[1:]}
         w2_words[first] = (
-            g_second[:, PACK * C - C // 2 :]
+            g_room[:, PACK * S - C // 2 :]
             .bitcast(BF16)
             .rearrange("p (t q j) -> p t q j", t=PACK, j=PACK)
         )
@@ -91,11 +86,13 @@ def tile_moe_bdx_mlp_silu_kernel(tc, dyT, a, w2, w1, gate, offs, out):
         da_scales = {u: keep.tile([P, C], U8, name=f"da_scales{u[0]}{u[1]}", align_bytes=64) for u in units}
         result = keep.tile([P, T], F32, name="result")
         gate_columns = keep.tile([P, E, C // P], F32, name="gate_columns")
+        zero = keep.tile([P, 1], F32, name="zero")
+        after_gates = keep.tile([P, 1], F32, name="after_gates")
         identity = keep.tile([P, P], F32, name="identity")
         dx_slots = {
-            (0, 0, EARLY): g_planes[0][:, 0, 0:EARLY],
+            (0, 0, EARLY): g_planes[:, 0, 0:EARLY],
             (0, EARLY, C): v[last][:, 0, EARLY:C],
-            (1, 0, C): g_planes[1][:, 0, :],
+            (1, 0, C): g_planes[:, 0, C:S],
         }
 
 
@@ -128,20 +125,29 @@ def tile_moe_bdx_mlp_silu_kernel(tc, dyT, a, w2, w1, gate, offs, out):
             bank = dh_banks.tile([P, C // P, P], F32, name="dh")
             for j in range(C // P):
                 nc.tensor.transpose(bank[:, j, :], gate_columns[:, e, j : j + 1].to_broadcast([P, P]), identity[:])
-            nc.vector.tensor_copy(gates[e].rearrange("r (p j) -> r p j", j=C // P), bank[:].rearrange("r j p -> r p j"))
+            nc.scalar.activation(
+                gates[:, slots_of(e)].rearrange("r (p j) -> r p j", j=C // P),
+                bank[:].rearrange("r j p -> r p j"),
+                IDENTITY,
+                bias=zero[:],
+            )
 
-        def silu(u, t0=0, t1=PACK):
-            nc.scalar.activation(in_runs(m_of[u])[:, :, t0:t1, :], as_planes(v[u][:])[:, :, t0:t1, :], SILU, scale=-1.0)
+        def silu(u, t0=0, t1=PACK, bias=0.0):
+            nc.scalar.activation(
+                in_runs(m_of[u])[:, :, t0:t1, :], as_planes(v[u][:])[:, :, t0:t1, :], SILU, scale=-1.0, bias=bias
+            )
 
-        def tanh(u, t0=0, t1=PACK):
-            nc.scalar.activation(in_runs(th_of[u])[:, :, t0:t1, :], as_planes(v[u][:])[:, :, t0:t1, :], TANH, scale=0.5)
+        def tanh(u, t0=0, t1=PACK, bias=0.0):
+            nc.scalar.activation(
+                in_runs(th_of[u])[:, :, t0:t1, :], as_planes(v[u][:])[:, :, t0:t1, :], TANH, scale=0.5, bias=bias
+            )
 
-        def gather(t, e, c0=0, c1=C):
-            window = dy[t][:].indirect(offsets[:, (e * C + c0) // LIST_ROWS : (e * C + c1) // LIST_ROWS])
-            nc.vector.tensor_tensor(g_planes[e][:, t, c0:c1], window, gates[e][:, c0:c1], MULT)
+        def gather(t, s0=0, s1=S):
+            window = dy[t][:].indirect(offsets[:, s0 // LIST_ROWS : s1 // LIST_ROWS])
+            nc.vector.tensor_tensor(g_planes[:, t, s0:s1], window, gates[:, s0:s1], MULT)
 
         def lay_g(e, copy, c0=0, c1=C):
-            copy(as_words(g_words[e][:, c0:c1, :]), as_planes(g_planes[e][:, :, c0:c1]))
+            copy(as_words(g_words[e][:, c0:c1, :]), as_planes(g_planes[:, :, e * C + c0 : e * C + c1]))
 
         def quantize_g(e, c0=0, c1=C):
             nc.vector.quantize_mx(
@@ -239,13 +245,13 @@ def tile_moe_bdx_mlp_silu_kernel(tc, dyT, a, w2, w1, gate, offs, out):
 
 
         nc.sync.dma_start(gate_columns[:], gate[0, :].rearrange("(e p j) -> p e j", e=E, p=P))
-        load_dy(0)
+        load_dy(1)
         nc.sync.dma_start(offsets[:], offs)
         load_a(first, 0, 2)
-        load_dy(1)
-        load_a(first, 2, 4)
         load_dy(2)
+        load_a(first, 2, 4)
         load_dy(3)
+        load_dy(0)
         load_w2(first)
         load_w2(second)
         load_a(second)
@@ -258,23 +264,23 @@ def tile_moe_bdx_mlp_silu_kernel(tc, dyT, a, w2, w1, gate, offs, out):
 
 
         make_identity(nc, identity[:])
+        nc.scalar.activation(zero[:], identity[:, 0:1], SILU, scale=0.0)
         for e in range(E):
             spread_gates(e)
+        nc.scalar.activation(after_gates[:], gates[:, S - 1 : S], SILU, scale=0.0)
         nc.vector.memset(result[:], 0.0)
 
-        for t in range(2):
-            for e in range(E):
-                gather(t, e)
         low, high = SLOT_PARTS
-        gather(2, 1)
-        gather(2, 0, *low)
-        gather(3, 1, *low)
-        gather(3, 0, *low)
-        gather(2, 0, *high)
-        gather(3, 0, *high)
+        for slots in EXPERT_PARTS:
+            gather(1, *slots)
+        gather(2)
+        gather(3, 0, C + C // 2)
+        gather(0, C, C + C // 2)
+        gather(0, *low)
+        gather(0, *high)
         for planes in PLANE_PARTS:
-            silu(first, *planes)
-            tanh(first, *planes)
+            silu(first, *planes, bias=after_gates[:])
+            tanh(first, *planes, bias=after_gates[:])
         lay_g(1, nc.scalar.copy, *low)
         lay_w2(first)
         for slots in SLOT_PARTS:
@@ -282,8 +288,9 @@ def tile_moe_bdx_mlp_silu_kernel(tc, dyT, a, w2, w1, gate, offs, out):
         for slots in SLOT_PARTS:
             quantize_g(0, *slots)
         quantize_g(1, *low)
+        gather(0, C + C // 2, S)
         quantize_w2(first, ((0, 1), (1, 2), (2, 4)))
-        gather(3, 1, *high)
+        gather(3, C + C // 2, S)
         make_x(first)
 
         lay_w2(second)

@@ -25,7 +25,7 @@ PASS = P * PACK
 HALVES = H // PASS
 RUN = 4
 LIST_ROWS = 16
-EARLY = 256
+EARLY = 288
 STORES = 4
 
 SLOT_PARTS = ((0, C // 2), (C // 2, C))
@@ -56,12 +56,18 @@ def tile_moe_bdx_mlp_silu_kernel(tc, dyT, a, w2, w1, gate, offs, out):
         g_room = keep.tile([P, PACK * S + 3 * C // 2], F32, name="g_room", align_bytes=64)
         g_planes = g_room[:, 0 : PACK * S].rearrange("p (t s) -> p t s", t=PACK)
         gates = keep.tile([P, S], F32, name="gates")
-        w2_raw = {u: keep.tile([P, PACK, PASS], F32, name=f"w2_raw{u[0]}{u[1]}") for u in units}
-        v = {u: keep.tile([P, PACK, C], F32, name=f"v{u[0]}{u[1]}") for u in units}
+        w2_raw = {u: keep.tile([P, PACK, PASS], F32, name=f"w2_raw{u[0]}{u[1]}")[:] for u in units}
+        v = {u: keep.tile([P, PACK, C], F32, name=f"v{u[0]}{u[1]}", align_bytes=64) for u in units}
         m_first = keep.tile([P, PACK, C], F32, name="m_first")
+        m_last = keep.tile([P, PACK, C], F32, name="m_last")
         th_first = keep.tile([P, PACK, C], F32, name="th_first")
-        m_of = {first: m_first[:], second: v[first][:], third: v[second][:], last: v[third][:]}
-        th_of = {u: th_first[:] if u == first else w2_raw[u][:] for u in units}
+        m_of = {first: m_first[:], second: v[first][:], third: v[second][:], last: m_last[:]}
+        th_of = {
+            first: th_first[:],
+            second: w2_raw[third],
+            third: w2_raw[last],
+            last: w2_raw[first],
+        }
         w1_raw = [keep.tile([P, HALVES, PACK, K], F32, name=f"w1_raw{e}") for e in range(E)]
 
         w2_words = {u: keep.tile([P, PACK, P, PACK], BF16, name=f"w2_words{u[0]}{u[1]}", align_bytes=64)[:] for u in units[1:]}
@@ -72,7 +78,11 @@ def tile_moe_bdx_mlp_silu_kernel(tc, dyT, a, w2, w1, gate, offs, out):
         )
         w2_codes = keep.tile([P, PASS], U32, name="w2_codes", align_bytes=64)
         w2_scales = keep.tile([P, PASS], U8, name="w2_scales", align_bytes=64)
-        w1_words = [keep.tile([P, HALVES, K, PACK], BF16, name=f"w1_words{e}", align_bytes=64) for e in range(E)]
+        w1_words_first = keep.tile([P, HALVES, K, PACK], BF16, name="w1_words_first", align_bytes=64)
+        w1_words = [
+            w1_words_first[:],
+            v[last][:, 0, :].bitcast(BF16).rearrange("p (h k j) -> p h k j", h=HALVES, j=PACK),
+        ]
         g_words = [keep.tile([P, C, PACK], BF16, name=f"g_words{e}", align_bytes=64) for e in range(E)]
         g_codes = [keep.tile([P, C], U32, name=f"g_codes{e}", align_bytes=64)[:] for e in range(E)]
         g_scales = [keep.tile([P, C], U8, name=f"g_scales{e}", align_bytes=64) for e in range(E)]
@@ -91,7 +101,7 @@ def tile_moe_bdx_mlp_silu_kernel(tc, dyT, a, w2, w1, gate, offs, out):
         identity = keep.tile([P, P], F32, name="identity")
         dx_slots = {
             (0, 0, EARLY): g_planes[:, 0, 0:EARLY],
-            (0, EARLY, C): v[last][:, 0, EARLY:C],
+            (0, EARLY, C): m_of[last][:, 0, EARLY:C],
             (1, 0, C): g_planes[:, 0, C:S],
         }
 
@@ -116,7 +126,7 @@ def tile_moe_bdx_mlp_silu_kernel(tc, dyT, a, w2, w1, gate, offs, out):
             nc.sync.dma_start(dy[t][:], dy_planes[:, t, :])
 
         def load_w2(u):
-            nc.sync.dma_start(w2_raw[u][:], w2_planes[:, u[0], :, u[1] * PASS : (u[1] + 1) * PASS])
+            nc.sync.dma_start(w2_raw[u], w2_planes[:, u[0], :, u[1] * PASS : (u[1] + 1) * PASS])
 
         def load_w1(e):
             nc.sync.dma_start(w1_raw[e][:], w1_planes[:, e])
@@ -159,7 +169,7 @@ def tile_moe_bdx_mlp_silu_kernel(tc, dyT, a, w2, w1, gate, offs, out):
         def lay_w2(u, t0=0, t1=PACK):
             nc.scalar.copy(
                 w2_words[u][:, t0:t1].rearrange("p t q j -> p q j t"),
-                w2_raw[u][:].rearrange("p j (q t) -> p q j t", t=PACK)[:, :, :, t0:t1],
+                w2_raw[u].rearrange("p j (q t) -> p q j t", t=PACK)[:, :, :, t0:t1],
             )
 
         def quantize_w2(u, parts=PLANE_PARTS):
@@ -172,14 +182,16 @@ def tile_moe_bdx_mlp_silu_kernel(tc, dyT, a, w2, w1, gate, offs, out):
                 )
 
         def lay_w1(e):
-            for h in range(HALVES):
-                nc.scalar.copy(as_words(w1_words[e][:, h]), as_planes(w1_raw[e][:, h]))
+            nc.scalar.copy(
+                w1_words[e].rearrange("p h (c i) t -> p h c t i", i=RUN),
+                w1_raw[e][:].rearrange("p h t (c i) -> p h c t i", i=RUN),
+            )
 
         def quantize_w1(e):
             nc.vector.quantize_mx(
                 out=w1_codes[e].bitcast(E4M3),
                 scales=w1_scales[e],
-                in_=w1_words[e][:].rearrange("p h k j -> p (h k j)"),
+                in_=w1_words[e].rearrange("p h k j -> p (h k j)"),
             )
 
         def make_x(u):
@@ -209,8 +221,8 @@ def tile_moe_bdx_mlp_silu_kernel(tc, dyT, a, w2, w1, gate, offs, out):
                     MULT,
                 )
 
-        def quantize_da(u):
-            for c0, c1 in SLOT_PARTS:
+        def quantize_da(u, parts=SLOT_PARTS):
+            for c0, c1 in parts:
                 nc.vector.quantize_mx(
                     out=da_codes[u][:, c0:c1].bitcast(E5M2),
                     scales=da_scales[u][:, c0:c1],
@@ -232,13 +244,13 @@ def tile_moe_bdx_mlp_silu_kernel(tc, dyT, a, w2, w1, gate, offs, out):
                 stop=(h == HALVES - 1),
             )
 
-        def put_back(e, c0, c1):
+        def put_back(e, c0, c1, scale=-0.5):
             slots = dx_slots[e, c0, c1]
             nc.scalar.activation(
                 slots.rearrange("p (c i) -> p c i", i=RUN),
                 dx[e][:].rearrange("p (i c) -> p c i", i=RUN)[:, c0 // RUN : c1 // RUN],
                 COPY,
-                scale=-0.5,
+                scale=scale,
             )
             window = result[:].indirect(offsets[:, (e * C + c0) // LIST_ROWS : (e * C + c1) // LIST_ROWS])
             nc.vector.tensor_copy(window, slots)
@@ -256,11 +268,11 @@ def tile_moe_bdx_mlp_silu_kernel(tc, dyT, a, w2, w1, gate, offs, out):
         load_w2(second)
         load_a(second)
         load_w2(third)
-        load_a(third)
         load_w1(0)
+        load_a(third)
         load_w2(last)
-        load_a(last)
         load_w1(1)
+        load_a(last)
 
 
         make_identity(nc, identity[:])
@@ -269,6 +281,7 @@ def tile_moe_bdx_mlp_silu_kernel(tc, dyT, a, w2, w1, gate, offs, out):
             spread_gates(e)
         nc.scalar.activation(after_gates[:], gates[:, S - 1 : S], SILU, scale=0.0)
         nc.vector.memset(result[:], 0.0)
+        nc.vector.memset(m_last[:, 0, 0:1], -0.5)
 
         low, high = SLOT_PARTS
         for slots in EXPERT_PARTS:
@@ -296,37 +309,38 @@ def tile_moe_bdx_mlp_silu_kernel(tc, dyT, a, w2, w1, gate, offs, out):
         lay_w2(second)
         quantize_w2(second)
         make_da(first)
+        lay_g(1, nc.vector.tensor_copy, *high)
         quantize_da(first)
+        quantize_g(1, *high)
         silu(second)
         make_x(second)
 
         lay_w2(third)
         quantize_w2(third)
         tanh(second)
-        lay_g(1, nc.scalar.copy, *high)
-        quantize_g(1, *high)
-        make_da(second)
-        quantize_da(second)
-        silu(third)
         lay_w1(0)
         quantize_w1(0)
+        add_to_dx(first)
+        make_da(second)
+        quantize_da(second)
+        add_to_dx(second)
+        silu(third)
         make_x(third)
 
         lay_w2(last)
         quantize_w2(last)
-        add_to_dx(first)
-        add_to_dx(second)
-        put_back(0, 0, EARLY)
         tanh(third)
         make_da(third)
-        quantize_da(third)
+        quantize_da(third, [low])
+        put_back(0, 0, EARLY, m_last[:, 0, 0:1])
         silu(last)
-        lay_w1(1)
         make_x(last)
-        quantize_w1(1)
+        quantize_da(third, [high])
         tanh(last)
+        lay_w1(1)
 
         make_da(last)
+        quantize_w1(1)
         add_to_dx(third)
         quantize_da(last)
         add_to_dx(last)

@@ -78,11 +78,7 @@ def tile_moe_bdx_mlp_silu_kernel(tc, dyT, a, w2, w1, gate, offs, out):
         )
         w2_codes = keep.tile([P, PASS], U32, name="w2_codes", align_bytes=64)
         w2_scales = keep.tile([P, PASS], U8, name="w2_scales", align_bytes=64)
-        w1_words_first = keep.tile([P, HALVES, K, PACK], BF16, name="w1_words_first", align_bytes=64)
-        w1_words = [
-            w1_words_first[:],
-            v[last][:, 0, :].bitcast(BF16).rearrange("p (h k j) -> p h k j", h=HALVES, j=PACK),
-        ]
+        w1_words = [w2_words[u][:, 2:4] for u in (second, third)]
         g_words = [keep.tile([P, C, PACK], BF16, name=f"g_words{e}", align_bytes=64) for e in range(E)]
         g_codes = [keep.tile([P, C], U32, name=f"g_codes{e}", align_bytes=64)[:] for e in range(E)]
         g_scales = [keep.tile([P, C], U8, name=f"g_scales{e}", align_bytes=64) for e in range(E)]
@@ -101,7 +97,7 @@ def tile_moe_bdx_mlp_silu_kernel(tc, dyT, a, w2, w1, gate, offs, out):
         identity = keep.tile([P, P], F32, name="identity")
         dx_slots = {
             (0, 0, EARLY): g_planes[:, 0, 0:EARLY],
-            (0, EARLY, C): m_of[last][:, 0, EARLY:C],
+            (0, EARLY, C): w1_words[1].rearrange("p h k j -> p (h k j)").bitcast(F32)[:, EARLY:C],
             (1, 0, C): g_planes[:, 0, C:S],
         }
 
@@ -156,6 +152,9 @@ def tile_moe_bdx_mlp_silu_kernel(tc, dyT, a, w2, w1, gate, offs, out):
             window = dy[t][:].indirect(offsets[:, s0 // LIST_ROWS : s1 // LIST_ROWS])
             nc.vector.tensor_tensor(g_planes[:, t, s0:s1], window, gates[:, s0:s1], MULT)
 
+        def round_on_gpsimd(words, planes):
+            nc.gpsimd.tensor_scalar(words, planes, 1.0, 0.0, MULT, ADD)
+
         def lay_g(e, copy, c0=0, c1=C):
             copy(as_words(g_words[e][:, c0:c1, :]), as_planes(g_planes[:, :, e * C + c0 : e * C + c1]))
 
@@ -182,10 +181,8 @@ def tile_moe_bdx_mlp_silu_kernel(tc, dyT, a, w2, w1, gate, offs, out):
                 )
 
         def lay_w1(e):
-            nc.scalar.copy(
-                w1_words[e].rearrange("p h (c i) t -> p h c t i", i=RUN),
-                w1_raw[e][:].rearrange("p h t (c i) -> p h c t i", i=RUN),
-            )
+            for h in range(HALVES):
+                round_on_gpsimd(as_words(w1_words[e][:, h]), as_planes(w1_raw[e][:, h]))
 
         def quantize_w1(e):
             nc.vector.quantize_mx(
@@ -304,25 +301,27 @@ def tile_moe_bdx_mlp_silu_kernel(tc, dyT, a, w2, w1, gate, offs, out):
         gather(0, C + C // 2, S)
         quantize_w2(first, ((0, 1), (1, 2), (2, 4)))
         gather(3, C + C // 2, S)
+        for c0 in range(C // 2, C, C // 4):
+            lay_g(1, round_on_gpsimd, c0, c0 + C // 4)
         make_x(first)
 
         lay_w2(second)
         quantize_w2(second)
         make_da(first)
-        lay_g(1, nc.vector.tensor_copy, *high)
-        quantize_da(first)
         quantize_g(1, *high)
+        quantize_da(first)
+        lay_w1(0)
         silu(second)
         make_x(second)
 
         lay_w2(third)
         quantize_w2(third)
         tanh(second)
-        lay_w1(0)
+        make_da(second)
         quantize_w1(0)
         add_to_dx(first)
-        make_da(second)
         quantize_da(second)
+        lay_w1(1)
         add_to_dx(second)
         silu(third)
         make_x(third)
@@ -336,11 +335,10 @@ def tile_moe_bdx_mlp_silu_kernel(tc, dyT, a, w2, w1, gate, offs, out):
         silu(last)
         make_x(last)
         quantize_da(third, [high])
+        quantize_w1(1)
         tanh(last)
-        lay_w1(1)
 
         make_da(last)
-        quantize_w1(1)
         add_to_dx(third)
         quantize_da(last)
         add_to_dx(last)

@@ -25,7 +25,7 @@ PASS = P * PACK
 HALVES = H // PASS
 RUN = 4
 LIST_ROWS = 16
-EARLY = 288
+EARLY = 256
 STORES = 4
 
 SLOT_PARTS = ((0, C // 2), (C // 2, C))
@@ -83,7 +83,7 @@ def tile_moe_bdx_mlp_silu_kernel(tc, dyT, a, w2, w1, gate, offs, out):
         g_codes = [keep.tile([P, C], U32, name=f"g_codes{e}", align_bytes=64)[:] for e in range(E)]
         g_scales = [keep.tile([P, C], U8, name=f"g_scales{e}", align_bytes=64) for e in range(E)]
         freed = {u: w2_words[u].rearrange("p t m j -> p (t m) j") for u in units}
-        da_words = {first: freed[second], second: freed[third], third: freed[last], last: g_words[1][:]}
+        da_words = {first: freed[second], second: freed[third], third: freed[second], last: g_words[1][:]}
         w1_codes_first = keep.tile([P, HALVES * K], U32, name="w1_codes_first", align_bytes=64)
         w1_scales_first = keep.tile([P, HALVES * K], U8, name="w1_scales_first", align_bytes=64)
         w1_codes = [w1_codes_first[:], w2_codes[:, 0 : HALVES * K]]
@@ -94,9 +94,11 @@ def tile_moe_bdx_mlp_silu_kernel(tc, dyT, a, w2, w1, gate, offs, out):
         gate_columns = keep.tile([P, E, C // P], F32, name="gate_columns")
         zero = keep.tile([P, 1], F32, name="zero")
         after_gates = keep.tile([P, 1], F32, name="after_gates")
+        lifted = keep.tile([P, C], F32, name="lifted")
+        one = keep.tile([P, 1], F32, name="one")
         identity = keep.tile([P, P], F32, name="identity")
         dx_slots = {
-            (0, 0, EARLY): g_planes[:, 0, 0:EARLY],
+            (0, 0, EARLY): da_words[third][:, C - C // RUN :, :].rearrange("p c t -> p (c t)").bitcast(F32),
             (0, EARLY, C): w1_words[1].rearrange("p h k j -> p (h k j)").bitcast(F32)[:, EARLY:C],
             (1, 0, C): g_planes[:, 0, C:S],
         }
@@ -113,6 +115,9 @@ def tile_moe_bdx_mlp_silu_kernel(tc, dyT, a, w2, w1, gate, offs, out):
 
         def in_runs(block):
             return block.rearrange("p t c -> p (t c)").rearrange("p (c t i) -> p c t i", t=PACK, i=RUN)
+
+        def last_of_runs(block):
+            return block.rearrange("p t c -> p (t c)").rearrange("p (n i) -> p n i", i=RUN)[:, :, RUN - 1]
 
 
         def load_a(u, t0=0, t1=PACK):
@@ -207,8 +212,8 @@ def tile_moe_bdx_mlp_silu_kernel(tc, dyT, a, w2, w1, gate, offs, out):
                 m = in_runs(m_of[u])[:, :, t, :]
                 nc.vector.scalar_tensor_tensor(m, m, -1.0, dh[:].rearrange("p (c i) -> p c i", i=RUN), ADD, MULT)
 
-        def make_da(u):
-            for i0, i1 in ((0, RUN // 2), (RUN // 2, RUN)):
+        def make_da(u, parts=((0, RUN // 2), (RUN // 2, RUN))):
+            for i0, i1 in parts:
                 nc.vector.scalar_tensor_tensor(
                     da_words[u].rearrange("p (i c) t -> p (c t) i", i=RUN)[:, :, i0:i1],
                     th_of[u].rearrange("p t c -> p (t c)").rearrange("p (n i) -> p n i", i=RUN)[:, :, i0:i1],
@@ -278,6 +283,7 @@ def tile_moe_bdx_mlp_silu_kernel(tc, dyT, a, w2, w1, gate, offs, out):
             spread_gates(e)
         nc.scalar.activation(after_gates[:], gates[:, S - 1 : S], SILU, scale=0.0)
         nc.vector.memset(result[:], 0.0)
+        nc.vector.memset(one[:], 1.0)
         nc.vector.memset(m_last[:, 0, 0:1], -0.5)
 
         low, high = SLOT_PARTS
@@ -329,12 +335,15 @@ def tile_moe_bdx_mlp_silu_kernel(tc, dyT, a, w2, w1, gate, offs, out):
         lay_w2(last)
         quantize_w2(last)
         tanh(third)
-        make_da(third)
-        quantize_da(third, [low])
+        make_da(third, [(0, RUN - 1)])
         put_back(0, 0, EARLY, m_last[:, 0, 0:1])
         silu(last)
+        nc.scalar.activation(lifted[:], last_of_runs(th_of[third]), IDENTITY, bias=one[:])
+        nc.gpsimd.tensor_tensor(
+            da_words[third][:, C - C // RUN :, :].rearrange("p c t -> p (c t)"), lifted[:], last_of_runs(m_of[third]), MULT
+        )
         make_x(last)
-        quantize_da(third, [high])
+        quantize_da(third, [(0, C)])
         quantize_w1(1)
         tanh(last)
 

@@ -311,7 +311,8 @@ def tile_moe_bdx_mlp_silu_kernel(tc, dyT, a, w2, w1, gate, offs, out):
             lay_g(1, round_on_gpsimd, c0, c0 + C // 4)
         make_x(first)
 
-        lay_w2(second)
+        for tiles in PLANE_PARTS:
+            lay_w2(second, *tiles)
         quantize_w2(second)
         make_da(first)
         quantize_g(1, *high)
@@ -320,7 +321,8 @@ def tile_moe_bdx_mlp_silu_kernel(tc, dyT, a, w2, w1, gate, offs, out):
         silu(second)
         make_x(second)
 
-        lay_w2(third)
+        for tiles in PLANE_PARTS:
+            lay_w2(third, *tiles)
         quantize_w2(third)
         tanh(second)
         make_da(second)
@@ -332,7 +334,8 @@ def tile_moe_bdx_mlp_silu_kernel(tc, dyT, a, w2, w1, gate, offs, out):
         silu(third)
         make_x(third)
 
-        lay_w2(last)
+        for tiles in PLANE_PARTS:
+            lay_w2(last, *tiles)
         quantize_w2(last)
         tanh(third)
         make_da(third, [(0, RUN - 1)])

@@ -160,6 +160,9 @@ def tile_moe_bdx_mlp_silu_kernel(tc, dyT, a, w2, w1, gate, offs, out):
         def round_on_gpsimd(words, planes):
             nc.gpsimd.tensor_scalar(words, planes, 1.0, 0.0, MULT, ADD)
 
+        def lay_on_gpsimd(words, planes):
+            round_on_gpsimd(words, planes.rearrange("p t c -> p c t"))
+
         def lay_g(e, copy, c0=0, c1=C):
             copy(as_words(g_words[e][:, c0:c1, :]), as_planes(g_planes[:, :, e * C + c0 : e * C + c1]))
 
@@ -187,7 +190,7 @@ def tile_moe_bdx_mlp_silu_kernel(tc, dyT, a, w2, w1, gate, offs, out):
 
         def lay_w1(e):
             for h in range(HALVES):
-                round_on_gpsimd(as_words(w1_words[e][:, h]), as_planes(w1_raw[e][:, h]))
+                lay_on_gpsimd(w1_words[e][:, h], w1_raw[e][:, h])
 
         def quantize_w1(e):
             nc.vector.quantize_mx(
@@ -308,7 +311,7 @@ def tile_moe_bdx_mlp_silu_kernel(tc, dyT, a, w2, w1, gate, offs, out):
         quantize_w2(first, ((0, 1), (1, 2), (2, 4)))
         gather(3, C + C // 2, S)
         for c0 in range(C // 2, C, C // 4):
-            lay_g(1, round_on_gpsimd, c0, c0 + C // 4)
+            lay_on_gpsimd(g_words[1][:, c0 : c0 + C // 4, :], g_planes[:, :, C + c0 : C + c0 + C // 4])
         make_x(first)
 
         for tiles in PLANE_PARTS:

@@ -13,7 +13,6 @@ E5M2 = mybir.dt.float8_e5m2_x4
 ADD = mybir.AluOpType.add
 MULT = mybir.AluOpType.mult
 COPY = mybir.ActivationFunctionType.Copy
-IDENTITY = mybir.ActivationFunctionType.Identity
 TANH = mybir.ActivationFunctionType.Tanh
 SILU = mybir.ActivationFunctionType.Silu
 
@@ -25,12 +24,9 @@ PASS = P * PACK
 HALVES = H // PASS
 RUN = 4
 LIST_ROWS = 16
-EARLY = 256
+B = C // 2
+BLOCKS = S // B
 STORES = 4
-
-SLOT_PARTS = ((0, C // 2), (C // 2, C))
-EXPERT_PARTS = ((0, C), (C, S))
-PLANE_PARTS = ((0, PACK // 2), (PACK // 2, PACK))
 
 FLOPS = 2 * S * N * H + 2 * S * H * K
 BYTES = 4 * (N * T + H * S + E * N * H + E * H * K + S + K * T) + 2 * S
@@ -43,69 +39,53 @@ def tile_moe_bdx_mlp_silu_kernel(tc, dyT, a, w2, w1, gate, offs, out):
     w2_planes = w2.rearrange("e (p j) i -> p e j i", j=PACK)
     w1_planes = w1.rearrange("e (h p j) k -> p e h j k", h=HALVES, j=PACK)
     units = [(e, h) for e in range(E) for h in range(HALVES)]
-    first, second, third, last = units
 
     with ExitStack() as ctx:
         lists = ctx.enter_context(tc.tile_pool(name="lists", bufs=1))
         keep = ctx.enter_context(tc.tile_pool(name="keep", bufs=1))
-        dh_banks = ctx.enter_context(tc.psum_pool(name="dh_banks", bufs=6))
-        dx_banks = ctx.enter_context(tc.psum_pool(name="dx_banks", bufs=2))
+        dh_banks = ctx.enter_context(tc.psum_pool(name="dh_banks", bufs=5))
+        side_banks = ctx.enter_context(tc.psum_pool(name="side_banks", bufs=2))
+        dx_bank = ctx.enter_context(tc.psum_pool(name="dx_bank", bufs=1))
 
         offsets = lists.tile([P, S // LIST_ROWS], U16, name="offsets")
         dy = [keep.tile([P, T], F32, name=f"dy{t}") for t in range(PACK)]
-        g_room = keep.tile([P, PACK * S + 3 * C // 2], F32, name="g_room", align_bytes=64)
-        g_planes = g_room[:, 0 : PACK * S].rearrange("p (t s) -> p t s", t=PACK)
-        gates = keep.tile([P, S], F32, name="gates")
-        w2_raw = {u: keep.tile([P, PACK, PASS], F32, name=f"w2_raw{u[0]}{u[1]}")[:] for u in units}
-        v = {u: keep.tile([P, PACK, C], F32, name=f"v{u[0]}{u[1]}", align_bytes=64) for u in units}
-        m_first = keep.tile([P, PACK, C], F32, name="m_first")
-        m_last = keep.tile([P, PACK, C], F32, name="m_last")
-        th_first = keep.tile([P, PACK, C], F32, name="th_first")
-        m_of = {first: m_first[:], second: v[first][:], third: v[second][:], last: m_last[:]}
-        th_of = {
-            first: th_first[:],
-            second: w2_raw[third],
-            third: w2_raw[last],
-            last: w2_raw[first],
-        }
+        g_first = keep.tile([P, PACK, B], F32, name="g_first")
+        g_fourth = keep.tile([P, PACK, B], F32, name="g_fourth")
+        room_m = keep.tile([P, 2 * PACK * C + 2 * B], F32, name="room_m")
+        room_w2 = keep.tile([P, (2 * PACK - 1) * B], F32, name="room_w2", align_bytes=64)
+
+        def planes_at(room, start):
+            return room[:, start : start + PACK * B].rearrange("p (t s) -> p t s", t=PACK)
+
+        g_planes = [g_first[:], planes_at(room_m, PACK * C - B), planes_at(room_w2, (PACK - 1) * B), g_fourth[:]]
+        gates = {b: keep.tile([P, B], F32, name=f"gates{b}") for b in (1, 2)}
+        w2_first = [keep.tile([P, PACK, PASS // 2], F32, name=f"w2_first{c}") for c in range(2)]
+        w2_raw = {u: keep.tile([P, PACK, PASS], F32, name=f"w2_raw{u}") for u in (1, 2, 3)}
+        v = [keep.tile([P, PACK, C], F32, name=f"v{u}", align_bytes=64) for u in range(4)]
+        m_of = [room_m[:, 0 : PACK * C], keep.tile([P, PACK * C], F32, name="m_odd")[:]]
+        th_of = [room_m[:, PACK * C + 2 * B :], keep.tile([P, PACK * C], F32, name="th_odd")[:]]
         w1_raw = [keep.tile([P, HALVES, PACK, K], F32, name=f"w1_raw{e}") for e in range(E)]
 
-        w2_words = {u: keep.tile([P, PACK, P, PACK], BF16, name=f"w2_words{u[0]}{u[1]}", align_bytes=64)[:] for u in units[1:]}
-        w2_words[first] = (
-            g_room[:, PACK * S - C // 2 :]
-            .bitcast(BF16)
-            .rearrange("p (t q j) -> p t q j", t=PACK, j=PACK)
-        )
-        w2_codes = keep.tile([P, PASS], U32, name="w2_codes", align_bytes=64)
-        w2_scales = keep.tile([P, PASS], U8, name="w2_scales", align_bytes=64)
-        w1_words = [w2_words[u][:, 2:4] for u in (second, third)]
-        g_words = [keep.tile([P, C, PACK], BF16, name=f"g_words{e}", align_bytes=64) for e in range(E)]
-        g_codes = [keep.tile([P, C], U32, name=f"g_codes{e}", align_bytes=64)[:] for e in range(E)]
+        w2_words = {u: keep.tile([P, PACK, P, PACK], BF16, name=f"w2_words{u}", align_bytes=64)[:] for u in (1, 2, 3)}
+        w2_words[0] = room_w2[:, 0 : PACK * B].bitcast(BF16).rearrange("p (t q j) -> p t q j", t=PACK, j=PACK)
+        w2_codes = [keep.tile([P, PASS], U32, name=f"w2_codes{u}", align_bytes=64) for u in range(4)]
+        w2_scales = [keep.tile([P, PASS], U8, name=f"w2_scales{u}", align_bytes=64) for u in range(4)]
+        g_words = [keep.tile([P, B, PACK], BF16, name=f"g_words{b}", align_bytes=64)[:] for b in range(3)]
+        g_last = [w2_words[0][:, 0], w2_words[1][:, 3]]
+        g_codes = [keep.tile([P, C], U32, name=f"g_codes{e}", align_bytes=64) for e in range(E)]
         g_scales = [keep.tile([P, C], U8, name=f"g_scales{e}", align_bytes=64) for e in range(E)]
-        freed = {u: w2_words[u].rearrange("p t m j -> p (t m) j") for u in units}
-        da_words = {first: freed[second], second: freed[third], third: freed[second], last: g_words[1][:]}
-        w1_codes_first = keep.tile([P, HALVES * K], U32, name="w1_codes_first", align_bytes=64)
-        w1_scales_first = keep.tile([P, HALVES * K], U8, name="w1_scales_first", align_bytes=64)
-        w1_codes = [w1_codes_first[:], w2_codes[:, 0 : HALVES * K]]
-        w1_scales = [w1_scales_first[:], w2_scales[:, 0 : HALVES * K]]
-        da_codes = {u: keep.tile([P, C], U32, name=f"da_codes{u[0]}{u[1]}", align_bytes=64) for u in units}
-        da_scales = {u: keep.tile([P, C], U8, name=f"da_scales{u[0]}{u[1]}", align_bytes=64) for u in units}
+        da_words = [keep.tile([P, C, PACK], BF16, name=f"da_words{u}", align_bytes=64) for u in range(4)]
+        da_codes = [keep.tile([P, C], U32, name=f"da_codes{u}", align_bytes=64) for u in range(4)]
+        da_scales = [keep.tile([P, C], U8, name=f"da_scales{u}", align_bytes=64) for u in range(4)]
+        w1_words = [da_words[e][:, B:C, :].rearrange("p (h k) j -> p h k j", h=HALVES) for e in range(E)]
+        w1_codes = [keep.tile([P, HALVES * K], U32, name=f"w1_codes{e}", align_bytes=64) for e in range(E)]
+        w1_scales = [keep.tile([P, HALVES * K], U8, name=f"w1_scales{e}", align_bytes=64) for e in range(E)]
+        dx_first = keep.tile([P, C], F32, name="dx_first")
+        dx_slots = [dx_first[:, 0:B], dx_first[:, B:C]] + [keep.tile([P, B], F32, name=f"dx_slots{b}")[:] for b in (2, 3)]
         result = keep.tile([P, T], F32, name="result")
         gate_columns = keep.tile([P, E, C // P], F32, name="gate_columns")
         zero = keep.tile([P, 1], F32, name="zero")
-        after_gates = keep.tile([P, 1], F32, name="after_gates")
-        lifted = keep.tile([P, C], F32, name="lifted")
-        one = keep.tile([P, 1], F32, name="one")
         identity = keep.tile([P, P], F32, name="identity")
-        dx_slots = {
-            (0, 0, EARLY): da_words[third][:, C - C // RUN :, :].rearrange("p c t -> p (c t)").bitcast(F32),
-            (0, EARLY, C): w1_words[1].rearrange("p h k j -> p (h k j)").bitcast(F32)[:, EARLY:C],
-            (1, 0, C): g_planes[:, 0, C:S],
-        }
-
-
-        def slots_of(e):
-            return slice(e * C, (e + 1) * C)
 
         def as_words(words):
             return words.rearrange("p (c i) t -> p c t i", i=RUN)
@@ -113,252 +93,295 @@ def tile_moe_bdx_mlp_silu_kernel(tc, dyT, a, w2, w1, gate, offs, out):
         def as_planes(planes):
             return planes.rearrange("p t (c i) -> p c t i", i=RUN)
 
-        def in_runs(block):
-            return block.rearrange("p t c -> p (t c)").rearrange("p (c t i) -> p c t i", t=PACK, i=RUN)
+        def in_runs(flat):
+            return flat.rearrange("p (c t i) -> p c t i", t=PACK, i=RUN)
 
-        def last_of_runs(block):
-            return block.rearrange("p t c -> p (t c)").rearrange("p (n i) -> p n i", i=RUN)[:, :, RUN - 1]
-
+        def listed(b):
+            return offsets[:, b * B // LIST_ROWS : (b + 1) * B // LIST_ROWS]
 
         def load_a(u, t0=0, t1=PACK):
-            nc.sync.dma_start(v[u][:, t0:t1, :], a_planes[:, u[1], t0:t1, slots_of(u[0])])
+            e, h = units[u]
+            nc.sync.dma_start(v[u][:, t0:t1, :], a_planes[:, h, t0:t1, e * C : (e + 1) * C])
 
         def load_dy(t):
             nc.sync.dma_start(dy[t][:], dy_planes[:, t, :])
 
         def load_w2(u):
-            nc.sync.dma_start(w2_raw[u], w2_planes[:, u[0], :, u[1] * PASS : (u[1] + 1) * PASS])
+            e, h = units[u]
+            nc.sync.dma_start(w2_raw[u][:], w2_planes[:, e, :, h * PASS : (h + 1) * PASS])
 
         def load_w1(e):
             nc.sync.dma_start(w1_raw[e][:], w1_planes[:, e])
 
+        gate_banks = []
+
         def spread_gates(e):
-            bank = dh_banks.tile([P, C // P, P], F32, name="dh")
+            bank = side_banks.tile([P, C // P, P], F32, name="side")
             for j in range(C // P):
                 nc.tensor.transpose(bank[:, j, :], gate_columns[:, e, j : j + 1].to_broadcast([P, P]), identity[:])
-            nc.scalar.activation(
-                gates[:, slots_of(e)].rearrange("r (p j) -> r p j", j=C // P),
-                bank[:].rearrange("r j p -> r p j"),
-                IDENTITY,
-                bias=zero[:],
+            gate_banks.append(bank)
+
+        def gates_in_bank(b):
+            half = slice(b % 2 * P // 2, (b % 2 + 1) * P // 2)
+            return gate_banks[b // 2][:, :, half].rearrange("r j p -> r p j")
+
+        def copy_gates(b):
+            nc.vector.tensor_copy(gates[b][:].rearrange("r (p j) -> r p j", j=RUN), gates_in_bank(b))
+
+        def gather_gated(t, b):
+            nc.vector.tensor_tensor(g_planes[b][:, t, :], dy[t][:].indirect(listed(b)), gates[b][:], MULT)
+
+        def gather_plain(t, b):
+            nc.scalar.activation(g_planes[b][:, t, :], dy[t][:].indirect(listed(b)), COPY)
+
+        def gate_plane(t, b):
+            plane = g_planes[b][:, t, :].rearrange("r (p j) -> r p j", j=RUN)
+            nc.vector.tensor_tensor(plane, plane, gates_in_bank(b), MULT)
+
+        def gate_and_lay(b):
+            nc.vector.tensor_tensor(
+                as_words(g_words[b]),
+                as_planes(g_planes[b]),
+                gates_in_bank(b).unsqueeze(2).to_broadcast([P, B // RUN, PACK, RUN]),
+                MULT,
             )
-
-        def silu(u, t0=0, t1=PACK, bias=0.0):
-            nc.scalar.activation(
-                in_runs(m_of[u])[:, :, t0:t1, :], as_planes(v[u][:])[:, :, t0:t1, :], SILU, scale=-1.0, bias=bias
-            )
-
-        def tanh(u, t0=0, t1=PACK, bias=0.0):
-            nc.scalar.activation(
-                in_runs(th_of[u])[:, :, t0:t1, :], as_planes(v[u][:])[:, :, t0:t1, :], TANH, scale=0.5, bias=bias
-            )
-
-        def gather(t, s0=0, s1=S):
-            window = dy[t][:].indirect(offsets[:, s0 // LIST_ROWS : s1 // LIST_ROWS])
-            nc.vector.tensor_tensor(g_planes[:, t, s0:s1], window, gates[:, s0:s1], MULT)
-
-        def round_on_gpsimd(words, planes):
-            nc.gpsimd.tensor_scalar(words, planes, 1.0, 0.0, MULT, ADD)
 
         def lay_on_gpsimd(words, planes):
-            round_on_gpsimd(words, planes.rearrange("p t c -> p c t"))
+            nc.gpsimd.tensor_scalar(words, planes.rearrange("p t c -> p c t"), 1.0, 0.0, MULT, ADD)
 
-        def lay_g(e, copy, c0=0, c1=C):
-            copy(as_words(g_words[e][:, c0:c1, :]), as_planes(g_planes[:, :, e * C + c0 : e * C + c1]))
+        def quantize(codes, scales, words, fmt):
+            nc.vector.quantize_mx(out=codes.bitcast(fmt), scales=scales, in_=words)
 
-        def quantize_g(e, c0=0, c1=C):
-            nc.vector.quantize_mx(
-                out=g_codes[e][:, c0:c1].bitcast(E5M2),
-                scales=g_scales[e][:, c0:c1],
-                in_=g_words[e][:, c0:c1, :].rearrange("p c t -> p (c t)"),
+        def quantize_g(b):
+            columns = slice(b % 2 * B, (b % 2 + 1) * B)
+            quantize(g_codes[b // 2][:, columns], g_scales[b // 2][:, columns], g_words[b].rearrange("p c t -> p (c t)"), E5M2)
+
+        def lay_last_g(half):
+            lay_on_gpsimd(g_last[half], g_planes[3][:, :, half * B // 2 : (half + 1) * B // 2])
+
+        def quantize_last_g(half):
+            columns = slice(B + half * B // 2, B + (half + 1) * B // 2)
+            quantize(g_codes[1][:, columns], g_scales[1][:, columns], g_last[half].rearrange("p c t -> p (c t)"), E5M2)
+
+        def lay_w2_columns(c):
+            nc.vector.tensor_copy(
+                w2_words[0][:, :, c * P // 2 : (c + 1) * P // 2, :].rearrange("p t q j -> p q j t"),
+                w2_first[c][:].rearrange("p j (q t) -> p q j t", t=PACK),
             )
 
-        def lay_w2(u, t0=0, t1=PACK):
-            nc.scalar.copy(
+        def lay_w2(u, copy, t0, t1):
+            copy(
                 w2_words[u][:, t0:t1].rearrange("p t q j -> p q j t"),
-                w2_raw[u].rearrange("p j (q t) -> p q j t", t=PACK)[:, :, :, t0:t1],
+                w2_raw[u][:].rearrange("p j (q t) -> p q j t", t=PACK)[:, :, :, t0:t1],
             )
 
-        def quantize_w2(u, parts=PLANE_PARTS):
-            for t0, t1 in parts:
-                columns = slice(t0 * P, t1 * P)
-                nc.vector.quantize_mx(
-                    out=w2_codes[:, columns].bitcast(E4M3),
-                    scales=w2_scales[:, columns],
-                    in_=w2_words[u][:, t0:t1].rearrange("p t q j -> p (t q j)"),
-                )
+        def quantize_w2(u, t0, t1):
+            columns = slice(t0 * P, t1 * P)
+            quantize(w2_codes[u][:, columns], w2_scales[u][:, columns], w2_words[u][:, t0:t1].rearrange("p t q j -> p (t q j)"), E4M3)
 
         def lay_w1(e):
             for h in range(HALVES):
                 lay_on_gpsimd(w1_words[e][:, h], w1_raw[e][:, h])
 
         def quantize_w1(e):
-            nc.vector.quantize_mx(
-                out=w1_codes[e].bitcast(E4M3),
-                scales=w1_scales[e],
-                in_=w1_words[e].rearrange("p h k j -> p (h k j)"),
+            quantize(w1_codes[e][:], w1_scales[e][:], w1_words[e].rearrange("p h k j -> p (h k j)"), E4M3)
+
+        def runs_of(c0, c1):
+            return slice(c0 // RUN, c1 // RUN)
+
+        def silu(u, t0=0, t1=PACK, c0=0, c1=C):
+            nc.scalar.activation(
+                in_runs(m_of[u % 2])[:, runs_of(c0, c1), t0:t1, :], as_planes(v[u][:, t0:t1, c0:c1]), SILU, scale=-1.0, bias=zero[:]
             )
 
-        def make_x(u):
-            for t in range(PACK):
-                dh = dh_banks.tile([P, C], F32, name="dh")
-                columns = slice(t * P, (t + 1) * P)
-                nc.tensor.matmul_mx(
-                    out=dh[:],
-                    lhsT=w2_codes[:, columns].bitcast(E4M3),
-                    lhsT_scale=w2_scales[:, columns],
-                    rhs=g_codes[u[0]].bitcast(E5M2),
-                    rhs_scale=g_scales[u[0]][:],
-                    start=True,
-                    stop=True,
-                )
-                m = in_runs(m_of[u])[:, :, t, :]
-                nc.vector.scalar_tensor_tensor(m, m, -1.0, dh[:].rearrange("p (c i) -> p c i", i=RUN), ADD, MULT)
+        def tanh(u, c0=0, c1=C, t0=0, t1=PACK):
+            nc.scalar.activation(
+                in_runs(th_of[u % 2])[:, runs_of(c0, c1), t0:t1, :], as_planes(v[u][:, t0:t1, c0:c1]), TANH, scale=0.5
+            )
 
-        def make_da(u, parts=((0, RUN // 2), (RUN // 2, RUN))):
-            for i0, i1 in parts:
-                nc.vector.scalar_tensor_tensor(
-                    da_words[u].rearrange("p (i c) t -> p (c t) i", i=RUN)[:, :, i0:i1],
-                    th_of[u].rearrange("p t c -> p (t c)").rearrange("p (n i) -> p n i", i=RUN)[:, :, i0:i1],
-                    1.0,
-                    m_of[u].rearrange("p t c -> p (t c)").rearrange("p (n i) -> p n i", i=RUN)[:, :, i0:i1],
-                    ADD,
-                    MULT,
-                )
+        def make_x(u, t, c0=0, c1=C):
+            e = units[u][0]
+            dh = dh_banks.tile([P, c1 - c0], F32, name="dh")
+            columns = slice(t * P, (t + 1) * P)
+            nc.tensor.matmul_mx(
+                out=dh[:],
+                lhsT=w2_codes[u][:, columns].bitcast(E4M3),
+                lhsT_scale=w2_scales[u][:, columns],
+                rhs=g_codes[e][:, c0:c1].bitcast(E5M2),
+                rhs_scale=g_scales[e][:, c0:c1],
+                start=True,
+                stop=True,
+            )
+            m = in_runs(m_of[u % 2])[:, runs_of(c0, c1), t, :]
+            nc.vector.scalar_tensor_tensor(m, m, -1.0, dh[:].rearrange("p (c i) -> p c i", i=RUN), ADD, MULT)
 
-        def quantize_da(u, parts=SLOT_PARTS):
-            for c0, c1 in parts:
-                nc.vector.quantize_mx(
-                    out=da_codes[u][:, c0:c1].bitcast(E5M2),
-                    scales=da_scales[u][:, c0:c1],
-                    in_=da_words[u][:, c0:c1, :].rearrange("p c t -> p (c t)"),
-                )
+        def make_da(u, half):
+            part = slice(half * B * PACK, (half + 1) * B * PACK)
+            nc.vector.scalar_tensor_tensor(
+                da_words[u][:, half * B : (half + 1) * B, :].rearrange("p (i c) t -> p (c t) i", i=RUN),
+                th_of[u % 2][:, part].rearrange("p (n i) -> p n i", i=RUN),
+                1.0,
+                m_of[u % 2][:, part].rearrange("p (n i) -> p n i", i=RUN),
+                ADD,
+                MULT,
+            )
 
-        dx = [dx_banks.tile([P, C], F32, name="dx") for e in range(E)]
+        def quantize_da(u, half):
+            columns = slice(half * B, (half + 1) * B)
+            quantize(da_codes[u][:, columns], da_scales[u][:, columns], da_words[u][:, columns, :].rearrange("p c t -> p (c t)"), E5M2)
 
-        def add_to_dx(u):
-            e, h = u
+        def add_to_dx(dx, u, c0, c1):
+            e, h = units[u]
             columns = slice(h * K, (h + 1) * K)
             nc.tensor.matmul_mx(
-                out=dx[e][:],
+                out=dx[:],
                 lhsT=w1_codes[e][:, columns].bitcast(E4M3),
                 lhsT_scale=w1_scales[e][:, columns],
-                rhs=da_codes[u][:].bitcast(E5M2),
-                rhs_scale=da_scales[u][:],
+                rhs=da_codes[u][:, c0:c1].bitcast(E5M2),
+                rhs_scale=da_scales[u][:, c0:c1],
                 start=(h == 0),
                 stop=(h == HALVES - 1),
             )
 
-        def put_back(e, c0, c1, scale=-0.5):
-            slots = dx_slots[e, c0, c1]
-            nc.scalar.activation(
-                slots.rearrange("p (c i) -> p c i", i=RUN),
-                dx[e][:].rearrange("p (i c) -> p c i", i=RUN)[:, c0 // RUN : c1 // RUN],
-                COPY,
-                scale=scale,
-            )
-            window = result[:].indirect(offsets[:, (e * C + c0) // LIST_ROWS : (e * C + c1) // LIST_ROWS])
-            nc.vector.tensor_copy(window, slots)
-
+        def scatter_on_scalar(b):
+            nc.scalar.activation(result[:].indirect(listed(b)), dx_slots[b], COPY)
 
         nc.sync.dma_start(gate_columns[:], gate[0, :].rearrange("(e p j) -> p e j", e=E, p=P))
         load_dy(1)
         nc.sync.dma_start(offsets[:], offs)
-        load_a(first, 0, 2)
         load_dy(2)
-        load_a(first, 2, 4)
         load_dy(3)
         load_dy(0)
-        load_w2(first)
-        load_w2(second)
-        load_a(second)
-        load_w2(third)
+        for c in range(2):
+            nc.sync.dma_start(w2_first[c][:], w2_planes[:, 0, :, c * PASS // 2 : (c + 1) * PASS // 2])
+            load_a(0, 2 - 2 * c, 4 - 2 * c)
+        load_a(1)
+        load_w2(1)
         load_w1(0)
-        load_a(third)
-        load_w2(last)
+        load_w2(2)
+        load_a(2)
         load_w1(1)
-        load_a(last)
-
+        load_w2(3)
+        load_a(3)
 
         make_identity(nc, identity[:])
-        nc.scalar.activation(zero[:], identity[:, 0:1], SILU, scale=0.0)
+        nc.vector.memset(zero[:], 0.0)
+        nc.scalar.activation(zero[:], zero[:], SILU)
         for e in range(E):
             spread_gates(e)
-        nc.scalar.activation(after_gates[:], gates[:, S - 1 : S], SILU, scale=0.0)
+            copy_gates(e + 1)
         nc.vector.memset(result[:], 0.0)
-        nc.vector.memset(one[:], 1.0)
-        nc.vector.memset(m_last[:, 0, 0:1], -0.5)
 
-        low, high = SLOT_PARTS
-        for slots in EXPERT_PARTS:
-            gather(1, *slots)
-        gather(2)
-        gather(3, 0, C + C // 2)
-        gather(0, C, C + C // 2)
-        gather(0, *low)
-        gather(0, *high)
-        for planes in PLANE_PARTS:
-            silu(first, *planes, bias=after_gates[:])
-            tanh(first, *planes, bias=after_gates[:])
-        lay_g(1, nc.scalar.copy, *low)
-        lay_w2(first)
-        for slots in SLOT_PARTS:
-            lay_g(0, nc.vector.tensor_copy, *slots)
-        for slots in SLOT_PARTS:
-            quantize_g(0, *slots)
-        quantize_g(1, *low)
-        gather(0, C + C // 2, S)
-        quantize_w2(first, ((0, 1), (1, 2), (2, 4)))
-        gather(3, C + C // 2, S)
-        for c0 in range(C // 2, C, C // 4):
-            lay_on_gpsimd(g_words[1][:, c0 : c0 + C // 4, :], g_planes[:, :, C + c0 : C + c0 + C // 4])
-        make_x(first)
+        for t in (1, 2, 3):
+            gather_plain(t, 0)
+            gather_gated(t, 1)
+            gather_plain(t, 3)
+            gather_gated(t, 2)
+            gate_plane(t, 3)
+        gather_plain(0, 0)
+        gather_gated(0, 1)
+        gate_and_lay(0)
+        gather_plain(0, 3)
+        nc.scalar.copy(as_words(g_words[1]), as_planes(g_planes[1]))
+        lay_w2_columns(0)
+        quantize_g(0)
+        quantize_g(1)
+        gate_plane(0, 3)
+        lay_w2_columns(1)
+        quantize_w2(0, 2, 4)
+        gather_gated(0, 2)
+        quantize_w2(0, 0, 2)
+        lay_on_gpsimd(g_words[2], g_planes[2])
+        lay_last_g(0)
 
-        for tiles in PLANE_PARTS:
-            lay_w2(second, *tiles)
-        quantize_w2(second)
-        make_da(first)
-        quantize_g(1, *high)
-        quantize_da(first)
+        for t0 in (2, 0):
+            silu(0, t0, t0 + 2)
+            tanh(0, t0=t0, t1=t0 + 2)
+        for t in (2, 3, 0, 1):
+            make_x(0, t)
+        quantize_g(2)
+        make_da(0, 0)
+        quantize_last_g(0)
+        make_da(0, 1)
+        silu(1)
+        lay_w2(1, nc.scalar.copy, 2, 4)
+        tanh(1, 0, B)
+        tanh(1, B, C)
+        lay_w2(1, nc.vector.tensor_copy, 0, 2)
+        quantize_da(0, 0)
+        quantize_w2(1, 0, 2)
+        quantize_da(0, 1)
+        quantize_w2(1, 2, 4)
         lay_w1(0)
-        silu(second)
-        make_x(second)
+        lay_last_g(1)
 
-        for tiles in PLANE_PARTS:
-            lay_w2(third, *tiles)
-        quantize_w2(third)
-        tanh(second)
-        make_da(second)
+        lay_w2(2, nc.scalar.copy, 0, 2)
+        lay_w2(2, nc.scalar.copy, 2, 4)
+        for t in range(PACK):
+            make_x(1, t)
+        quantize_last_g(1)
+        make_da(1, 0)
+        quantize_w2(2, 0, 2)
         quantize_w1(0)
-        add_to_dx(first)
-        quantize_da(second)
+        make_da(1, 1)
+        quantize_w2(2, 2, 4)
+        quantize_da(1, 0)
+        quantize_da(1, 1)
         lay_w1(1)
-        add_to_dx(second)
-        silu(third)
-        make_x(third)
+        dx = dx_bank.tile([P, C], F32, name="dx")
+        add_to_dx(dx, 0, 0, C)
+        add_to_dx(dx, 1, 0, C)
 
-        for tiles in PLANE_PARTS:
-            lay_w2(last, *tiles)
-        quantize_w2(last)
-        tanh(third)
-        make_da(third, [(0, RUN - 1)])
-        put_back(0, 0, EARLY, m_last[:, 0, 0:1])
-        silu(last)
-        nc.scalar.activation(lifted[:], last_of_runs(th_of[third]), IDENTITY, bias=one[:])
-        nc.gpsimd.tensor_tensor(
-            da_words[third][:, C - C // RUN :, :].rearrange("p c t -> p (c t)"), lifted[:], last_of_runs(m_of[third]), MULT
-        )
-        make_x(last)
-        quantize_da(third, [(0, C)])
+        silu(2)
+        tanh(2, 0, B)
+        tanh(2, B, C)
+        lay_w2(3, nc.scalar.copy, 0, 2)
+        lay_w2(3, nc.scalar.copy, 2, 4)
+        for t in range(PACK):
+            make_x(2, t)
         quantize_w1(1)
-        tanh(last)
+        make_da(2, 0)
+        make_da(2, 1)
+        quantize_w2(3, 0, 2)
+        quantize_da(2, 0)
+        quantize_w2(3, 2, 4)
+        quantize_da(2, 1)
+        dx_late = [side_banks.tile([P, B], F32, name="side") for half in range(2)]
+        for half in range(2):
+            add_to_dx(dx_late[half], 2, half * B, (half + 1) * B)
 
-        make_da(last)
-        add_to_dx(third)
-        quantize_da(last)
-        add_to_dx(last)
-        put_back(0, EARLY, C)
-        put_back(1, 0, C)
+        nc.scalar.activation(
+            dx_first[:].rearrange("p (b c i) -> p b c i", b=2, i=RUN),
+            dx[:].rearrange("p (b i c) -> p b c i", b=2, i=RUN),
+            COPY,
+            scale=-0.5,
+        )
+        silu(3, c0=0, c1=B)
+        scatter_on_scalar(0)
+        tanh(3, 0, B)
+        silu(3, c0=B, c1=C)
+        tanh(3, B, C)
+        scatter_on_scalar(1)
+        for t in range(PACK):
+            make_x(3, t, 0, B)
+        make_x(3, 0, B, C)
+        make_da(3, 0)
+        make_x(3, 1, B, C)
+        quantize_da(3, 0)
+        add_to_dx(dx_late[0], 3, 0, B)
+        nc.scalar.activation(
+            dx_slots[2].rearrange("p (c i) -> p c i", i=RUN), dx_late[0][:].rearrange("p (i c) -> p c i", i=RUN), COPY, scale=-0.5
+        )
+        scatter_on_scalar(2)
+        make_x(3, 2, B, C)
+        make_x(3, 3, B, C)
+        make_da(3, 1)
+        quantize_da(3, 1)
+        add_to_dx(dx_late[1], 3, B, C)
+        nc.vector.tensor_scalar_mul(
+            dx_slots[3].rearrange("p (c i) -> p c i", i=RUN), dx_late[1][:].rearrange("p (i c) -> p c i", i=RUN), -0.5
+        )
+        nc.vector.tensor_copy(result[:].indirect(listed(3)), dx_slots[3])
 
         for part in range(STORES):
             columns = slice(part * T // STORES, (part + 1) * T // STORES)

@@ -27,6 +27,7 @@ LIST_ROWS = 16
 B = C // 2
 BLOCKS = S // B
 STORES = 4
+LATE = 3 * B // 4
 
 FLOPS = 2 * S * N * H + 2 * S * H * K
 BYTES = 4 * (N * T + H * S + E * N * H + E * H * K + S + K * T) + 2 * S
@@ -51,33 +52,49 @@ def tile_moe_bdx_mlp_silu_kernel(tc, dyT, a, w2, w1, gate, offs, out):
         dy = [keep.tile([P, T], F32, name=f"dy{t}") for t in range(PACK)]
         g_first = keep.tile([P, PACK, B], F32, name="g_first")
         g_fourth = keep.tile([P, PACK, B], F32, name="g_fourth")
-        room_m = keep.tile([P, 2 * PACK * C + 2 * B], F32, name="room_m")
-        room_w2 = keep.tile([P, (2 * PACK - 1) * B], F32, name="room_w2", align_bytes=64)
+        room_m = keep.tile([P, 2 * PACK * C + 2 * B], F32, name="room_m", align_bytes=64)
+        room_w2 = keep.tile([P, (2 * PACK + 1) * B], F32, name="room_w2", align_bytes=64)
 
         def planes_at(room, start):
             return room[:, start : start + PACK * B].rearrange("p (t s) -> p t s", t=PACK)
 
-        g_planes = [g_first[:], planes_at(room_m, PACK * C - B), planes_at(room_w2, (PACK - 1) * B), g_fourth[:]]
+        g_planes = [g_first[:], planes_at(room_m, PACK * C - B), planes_at(room_w2, (PACK + 1) * B), g_fourth[:]]
         gates = {b: keep.tile([P, B], F32, name=f"gates{b}") for b in (1, 2)}
-        w2_first = [keep.tile([P, PACK, PASS // 2], F32, name=f"w2_first{c}") for c in range(2)]
-        w2_raw = {u: keep.tile([P, PACK, PASS], F32, name=f"w2_raw{u}") for u in (1, 2, 3)}
+        w2_raw = {u: keep.tile([P, PACK, PASS], F32, name=f"w2_raw{u}") for u in range(4)}
         v = [keep.tile([P, PACK, C], F32, name=f"v{u}", align_bytes=64) for u in range(4)]
         m_of = [room_m[:, 0 : PACK * C], keep.tile([P, PACK * C], F32, name="m_odd")[:]]
         th_of = [room_m[:, PACK * C + 2 * B :], keep.tile([P, PACK * C], F32, name="th_odd")[:]]
         w1_raw = [keep.tile([P, HALVES, PACK, K], F32, name=f"w1_raw{e}") for e in range(E)]
 
-        w2_words = {u: keep.tile([P, PACK, P, PACK], BF16, name=f"w2_words{u}", align_bytes=64)[:] for u in (1, 2, 3)}
-        w2_words[0] = room_w2[:, 0 : PACK * B].bitcast(BF16).rearrange("p (t q j) -> p t q j", t=PACK, j=PACK)
+        w2_words = {u: keep.tile([P, PACK, P, PACK], BF16, name=f"w2_words{u}", align_bytes=64)[:] for u in (2, 3)}
+        w2_words[1] = room_w2[:, 0 : PACK * B].bitcast(BF16).rearrange("p (t q j) -> p t q j", t=PACK, j=PACK)
+        first_pairs = [
+            room[:, start : start + 2 * B].bitcast(BF16).rearrange("p (t q j) -> p t q j", t=2, j=PACK)
+            for room, start in ((room_m, PACK * C), (room_w2, PACK * B))
+        ]
+
+        def w2_tiles(u, t0, t1):
+            if u == 0:
+                return first_pairs[t0 // 2][:, t0 % 2 : t0 % 2 + t1 - t0]
+            return w2_words[u][:, t0:t1]
+
         w2_codes = [keep.tile([P, PASS], U32, name=f"w2_codes{u}", align_bytes=64) for u in range(4)]
         w2_scales = [keep.tile([P, PASS], U8, name=f"w2_scales{u}", align_bytes=64) for u in range(4)]
-        g_words = [keep.tile([P, B, PACK], BF16, name=f"g_words{b}", align_bytes=64)[:] for b in range(3)]
-        g_last = [w2_words[0][:, 0], w2_words[1][:, 3]]
+        g_words = [keep.tile([P, B, PACK], BF16, name=f"g_words{b}", align_bytes=64)[:] for b in range(2)]
+        g_words.append(first_pairs[0].rearrange("p t q j -> p (t q) j"))
+        start = PACK * B - 2 * LATE
+        g_words.append(room_w2[:, start : start + 2 * B].bitcast(BF16).rearrange("p (c t) -> p c t", t=PACK))
         g_codes = [keep.tile([P, C], U32, name=f"g_codes{e}", align_bytes=64) for e in range(E)]
         g_scales = [keep.tile([P, C], U8, name=f"g_scales{e}", align_bytes=64) for e in range(E)]
         da_words = [keep.tile([P, C, PACK], BF16, name=f"da_words{u}", align_bytes=64) for u in range(4)]
         da_codes = [keep.tile([P, C], U32, name=f"da_codes{u}", align_bytes=64) for u in range(4)]
         da_scales = [keep.tile([P, C], U8, name=f"da_scales{u}", align_bytes=64) for u in range(4)]
-        w1_words = [da_words[e][:, B:C, :].rearrange("p (h k) j -> p h k j", h=HALVES) for e in range(E)]
+        w1_words = {
+            (0, 0): da_words[0][:, C - K : C, :],
+            (0, 1): da_words[1][:, B - K : B, :],
+            (1, 0): da_words[1][:, B : B + K, :],
+            (1, 1): da_words[1][:, C - K : C, :],
+        }
         w1_codes = [keep.tile([P, HALVES * K], U32, name=f"w1_codes{e}", align_bytes=64) for e in range(E)]
         w1_scales = [keep.tile([P, HALVES * K], U8, name=f"w1_scales{e}", align_bytes=64) for e in range(E)]
         dx_first = keep.tile([P, C], F32, name="dx_first")
@@ -147,7 +164,7 @@ def tile_moe_bdx_mlp_silu_kernel(tc, dyT, a, w2, w1, gate, offs, out):
             )
 
         def lay_on_gpsimd(words, planes):
-            nc.gpsimd.tensor_scalar(words, planes.rearrange("p t c -> p c t"), 1.0, 0.0, MULT, ADD)
+            nc.gpsimd.tensor_scalar(as_words(words), as_planes(planes), 1.0, 0.0, MULT, ADD)
 
         def quantize(codes, scales, words, fmt):
             nc.vector.quantize_mx(out=codes.bitcast(fmt), scales=scales, in_=words)
@@ -156,35 +173,25 @@ def tile_moe_bdx_mlp_silu_kernel(tc, dyT, a, w2, w1, gate, offs, out):
             columns = slice(b % 2 * B, (b % 2 + 1) * B)
             quantize(g_codes[b // 2][:, columns], g_scales[b // 2][:, columns], g_words[b].rearrange("p c t -> p (c t)"), E5M2)
 
-        def lay_last_g(half):
-            lay_on_gpsimd(g_last[half], g_planes[3][:, :, half * B // 2 : (half + 1) * B // 2])
-
-        def quantize_last_g(half):
-            columns = slice(B + half * B // 2, B + (half + 1) * B // 2)
-            quantize(g_codes[1][:, columns], g_scales[1][:, columns], g_last[half].rearrange("p c t -> p (c t)"), E5M2)
-
-        def lay_w2_columns(c):
-            nc.vector.tensor_copy(
-                w2_words[0][:, :, c * P // 2 : (c + 1) * P // 2, :].rearrange("p t q j -> p q j t"),
-                w2_first[c][:].rearrange("p j (q t) -> p q j t", t=PACK),
-            )
+        def lay_last_g(c0, c1):
+            lay_on_gpsimd(g_words[3][:, c0:c1, :], g_planes[3][:, :, c0:c1])
 
         def lay_w2(u, copy, t0, t1):
             copy(
-                w2_words[u][:, t0:t1].rearrange("p t q j -> p q j t"),
+                w2_tiles(u, t0, t1).rearrange("p t q j -> p q j t"),
                 w2_raw[u][:].rearrange("p j (q t) -> p q j t", t=PACK)[:, :, :, t0:t1],
             )
 
         def quantize_w2(u, t0, t1):
             columns = slice(t0 * P, t1 * P)
-            quantize(w2_codes[u][:, columns], w2_scales[u][:, columns], w2_words[u][:, t0:t1].rearrange("p t q j -> p (t q j)"), E4M3)
+            quantize(w2_codes[u][:, columns], w2_scales[u][:, columns], w2_tiles(u, t0, t1).rearrange("p t q j -> p (t q j)"), E4M3)
 
-        def lay_w1(e):
-            for h in range(HALVES):
-                lay_on_gpsimd(w1_words[e][:, h], w1_raw[e][:, h])
+        def lay_w1(e, h):
+            lay_on_gpsimd(w1_words[e, h], w1_raw[e][:, h])
 
-        def quantize_w1(e):
-            quantize(w1_codes[e][:], w1_scales[e][:], w1_words[e].rearrange("p h k j -> p (h k j)"), E4M3)
+        def quantize_w1(e, h):
+            columns = slice(h * K, (h + 1) * K)
+            quantize(w1_codes[e][:, columns], w1_scales[e][:, columns], w1_words[e, h].rearrange("p k j -> p (k j)"), E4M3)
 
         def runs_of(c0, c1):
             return slice(c0 // RUN, c1 // RUN)
@@ -252,9 +259,9 @@ def tile_moe_bdx_mlp_silu_kernel(tc, dyT, a, w2, w1, gate, offs, out):
         load_dy(2)
         load_dy(3)
         load_dy(0)
-        for c in range(2):
-            nc.sync.dma_start(w2_first[c][:], w2_planes[:, 0, :, c * PASS // 2 : (c + 1) * PASS // 2])
-            load_a(0, 2 - 2 * c, 4 - 2 * c)
+        load_w2(0)
+        load_a(0, 2, 4)
+        load_a(0, 0, 2)
         load_a(1)
         load_w2(1)
         load_w1(0)
@@ -283,25 +290,26 @@ def tile_moe_bdx_mlp_silu_kernel(tc, dyT, a, w2, w1, gate, offs, out):
         gate_and_lay(0)
         gather_plain(0, 3)
         nc.scalar.copy(as_words(g_words[1]), as_planes(g_planes[1]))
-        lay_w2_columns(0)
+        gate_plane(0, 3)
         quantize_g(0)
         quantize_g(1)
-        gate_plane(0, 3)
-        lay_w2_columns(1)
-        quantize_w2(0, 2, 4)
+        lay_w2(0, nc.vector.tensor_copy, 2, 4)
+        lay_w2(0, nc.scalar.copy, 0, 2)
+        quantize_w2(0, 3, 4)
         gather_gated(0, 2)
+        quantize_w2(0, 2, 3)
         quantize_w2(0, 0, 2)
         lay_on_gpsimd(g_words[2], g_planes[2])
-        lay_last_g(0)
+        lay_last_g(LATE, B)
 
         for t0 in (2, 0):
             silu(0, t0, t0 + 2)
-            tanh(0, t0=t0, t1=t0 + 2)
-        for t in (2, 3, 0, 1):
+        tanh(0, 0, B)
+        tanh(0, B, C)
+        for t in (3, 2, 0, 1):
             make_x(0, t)
         quantize_g(2)
         make_da(0, 0)
-        quantize_last_g(0)
         make_da(0, 1)
         silu(1)
         lay_w2(1, nc.scalar.copy, 2, 4)
@@ -312,25 +320,26 @@ def tile_moe_bdx_mlp_silu_kernel(tc, dyT, a, w2, w1, gate, offs, out):
         quantize_w2(1, 0, 2)
         quantize_da(0, 1)
         quantize_w2(1, 2, 4)
-        lay_w1(0)
-        lay_last_g(1)
+        lay_w1(0, 0)
+        lay_last_g(0, LATE)
 
         lay_w2(2, nc.scalar.copy, 0, 2)
         lay_w2(2, nc.scalar.copy, 2, 4)
         for t in range(PACK):
             make_x(1, t)
-        quantize_last_g(1)
+        quantize_g(3)
         make_da(1, 0)
         quantize_w2(2, 0, 2)
-        quantize_w1(0)
+        quantize_w1(0, 0)
         make_da(1, 1)
         quantize_w2(2, 2, 4)
         quantize_da(1, 0)
         quantize_da(1, 1)
-        lay_w1(1)
+        lay_w1(0, 1)
+        lay_w1(1, 0)
+        lay_w1(1, 1)
         dx = dx_bank.tile([P, C], F32, name="dx")
         add_to_dx(dx, 0, 0, C)
-        add_to_dx(dx, 1, 0, C)
 
         silu(2)
         tanh(2, 0, B)
@@ -339,9 +348,12 @@ def tile_moe_bdx_mlp_silu_kernel(tc, dyT, a, w2, w1, gate, offs, out):
         lay_w2(3, nc.scalar.copy, 2, 4)
         for t in range(PACK):
             make_x(2, t)
-        quantize_w1(1)
+        quantize_w1(0, 1)
+        add_to_dx(dx, 1, 0, C)
         make_da(2, 0)
+        quantize_w1(1, 0)
         make_da(2, 1)
+        quantize_w1(1, 1)
         quantize_w2(3, 0, 2)
         quantize_da(2, 0)
         quantize_w2(3, 2, 4)
@@ -350,16 +362,16 @@ def tile_moe_bdx_mlp_silu_kernel(tc, dyT, a, w2, w1, gate, offs, out):
         for half in range(2):
             add_to_dx(dx_late[half], 2, half * B, (half + 1) * B)
 
+        silu(3, c0=0, c1=B)
         nc.scalar.activation(
             dx_first[:].rearrange("p (b c i) -> p b c i", b=2, i=RUN),
             dx[:].rearrange("p (b i c) -> p b c i", b=2, i=RUN),
             COPY,
             scale=-0.5,
         )
-        silu(3, c0=0, c1=B)
-        scatter_on_scalar(0)
         tanh(3, 0, B)
         silu(3, c0=B, c1=C)
+        scatter_on_scalar(0)
         tanh(3, B, C)
         scatter_on_scalar(1)
         for t in range(PACK):

@@ -27,6 +27,7 @@ LIST_ROWS = 16
 B = C // 2
 BLOCKS = S // B
 STORES = 4
+LAST = C - B // 2
 LATE = 3 * B // 4
 
 FLOPS = 2 * S * N * H + 2 * S * H * K
@@ -76,6 +77,8 @@ def tile_moe_bdx_mlp_silu_kernel(tc, dyT, a, w2, w1, gate, offs, out):
         def w2_tiles(u, t0, t1):
             if u == 0:
                 return first_pairs[t0 // 2][:, t0 % 2 : t0 % 2 + t1 - t0]
+            if u >= 2 and t0 == 0:
+                return da_words[u - 2][:, B:C, :].rearrange("p (t q) j -> p t q j", t=2)
             return w2_words[u][:, t0:t1]
 
         w2_codes = [keep.tile([P, PASS], U32, name=f"w2_codes{u}", align_bytes=64) for u in range(4)]
@@ -86,14 +89,12 @@ def tile_moe_bdx_mlp_silu_kernel(tc, dyT, a, w2, w1, gate, offs, out):
         g_words.append(room_w2[:, start : start + 2 * B].bitcast(BF16).rearrange("p (c t) -> p c t", t=PACK))
         g_codes = [keep.tile([P, C], U32, name=f"g_codes{e}", align_bytes=64) for e in range(E)]
         g_scales = [keep.tile([P, C], U8, name=f"g_scales{e}", align_bytes=64) for e in range(E)]
-        da_words = [keep.tile([P, C, PACK], BF16, name=f"da_words{u}", align_bytes=64) for u in range(4)]
+        da_words = [keep.tile([P, C, PACK], BF16, name=f"da_words{u}", align_bytes=64) for u in range(3)]
+        da_words.append(da_words[2])
         da_codes = [keep.tile([P, C], U32, name=f"da_codes{u}", align_bytes=64) for u in range(4)]
         da_scales = [keep.tile([P, C], U8, name=f"da_scales{u}", align_bytes=64) for u in range(4)]
         w1_words = {
-            (0, 0): da_words[0][:, C - K : C, :],
-            (0, 1): da_words[1][:, B - K : B, :],
-            (1, 0): da_words[1][:, B : B + K, :],
-            (1, 1): da_words[1][:, C - K : C, :],
+            (e, h): da_words[1 + e][:, e * B + h * K : e * B + (h + 1) * K, :] for e in range(E) for h in range(HALVES)
         }
         w1_codes = [keep.tile([P, HALVES * K], U32, name=f"w1_codes{e}", align_bytes=64) for e in range(E)]
         w1_scales = [keep.tile([P, HALVES * K], U8, name=f"w1_scales{e}", align_bytes=64) for e in range(E)]
@@ -176,11 +177,14 @@ def tile_moe_bdx_mlp_silu_kernel(tc, dyT, a, w2, w1, gate, offs, out):
         def lay_last_g(c0, c1):
             lay_on_gpsimd(g_words[3][:, c0:c1, :], g_planes[3][:, :, c0:c1])
 
-        def lay_w2(u, copy, t0, t1):
+        def lay_w2(u, copy, t0, t1, q0=0, q1=P):
             copy(
-                w2_tiles(u, t0, t1).rearrange("p t q j -> p q j t"),
-                w2_raw[u][:].rearrange("p j (q t) -> p q j t", t=PACK)[:, :, :, t0:t1],
+                w2_tiles(u, t0, t1).rearrange("p t q j -> p q j t")[:, q0:q1],
+                w2_raw[u][:].rearrange("p j (q t) -> p q j t", t=PACK)[:, q0:q1, :, t0:t1],
             )
+
+        def round_on_gpsimd(words, values):
+            nc.gpsimd.tensor_scalar(words, values, 1.0, 0.0, MULT, ADD)
 
         def quantize_w2(u, t0, t1):
             columns = slice(t0 * P, t1 * P)
@@ -189,9 +193,8 @@ def tile_moe_bdx_mlp_silu_kernel(tc, dyT, a, w2, w1, gate, offs, out):
         def lay_w1(e, h):
             lay_on_gpsimd(w1_words[e, h], w1_raw[e][:, h])
 
-        def quantize_w1(e, h):
-            columns = slice(h * K, (h + 1) * K)
-            quantize(w1_codes[e][:, columns], w1_scales[e][:, columns], w1_words[e, h].rearrange("p k j -> p (k j)"), E4M3)
+        def quantize_w1(e):
+            quantize(w1_codes[e][:], w1_scales[e][:], da_words[1 + e][:, e * B : (e + 1) * B, :].rearrange("p k j -> p (k j)"), E4M3)
 
         def runs_of(c0, c1):
             return slice(c0 // RUN, c1 // RUN)
@@ -222,10 +225,10 @@ def tile_moe_bdx_mlp_silu_kernel(tc, dyT, a, w2, w1, gate, offs, out):
             m = in_runs(m_of[u % 2])[:, runs_of(c0, c1), t, :]
             nc.vector.scalar_tensor_tensor(m, m, -1.0, dh[:].rearrange("p (c i) -> p c i", i=RUN), ADD, MULT)
 
-        def make_da(u, half):
-            part = slice(half * B * PACK, (half + 1) * B * PACK)
+        def make_da(u, c0, c1):
+            part = slice(c0 * PACK, c1 * PACK)
             nc.vector.scalar_tensor_tensor(
-                da_words[u][:, half * B : (half + 1) * B, :].rearrange("p (i c) t -> p (c t) i", i=RUN),
+                da_words[u][:, c0:c1, :].rearrange("p (i c) t -> p (c t) i", i=RUN),
                 th_of[u % 2][:, part].rearrange("p (n i) -> p n i", i=RUN),
                 1.0,
                 m_of[u % 2][:, part].rearrange("p (n i) -> p n i", i=RUN),
@@ -233,8 +236,8 @@ def tile_moe_bdx_mlp_silu_kernel(tc, dyT, a, w2, w1, gate, offs, out):
                 MULT,
             )
 
-        def quantize_da(u, half):
-            columns = slice(half * B, (half + 1) * B)
+        def quantize_da(u, c0, c1):
+            columns = slice(c0, c1)
             quantize(da_codes[u][:, columns], da_scales[u][:, columns], da_words[u][:, columns, :].rearrange("p c t -> p (c t)"), E5M2)
 
         def add_to_dx(dx, u, c0, c1):
@@ -264,12 +267,12 @@ def tile_moe_bdx_mlp_silu_kernel(tc, dyT, a, w2, w1, gate, offs, out):
         load_a(0, 0, 2)
         load_a(1)
         load_w2(1)
-        load_w1(0)
         load_w2(2)
         load_a(2)
-        load_w1(1)
+        load_w1(0)
         load_w2(3)
         load_a(3)
+        load_w1(1)
 
         make_identity(nc, identity[:])
         nc.vector.memset(zero[:], 0.0)
@@ -309,58 +312,55 @@ def tile_moe_bdx_mlp_silu_kernel(tc, dyT, a, w2, w1, gate, offs, out):
         for t in (3, 2, 0, 1):
             make_x(0, t)
         quantize_g(2)
-        make_da(0, 0)
-        make_da(0, 1)
+        make_da(0, 0, B)
+        make_da(0, B, C)
         silu(1)
         lay_w2(1, nc.scalar.copy, 2, 4)
         tanh(1, 0, B)
         tanh(1, B, C)
         lay_w2(1, nc.vector.tensor_copy, 0, 2)
-        quantize_da(0, 0)
+        quantize_da(0, 0, B)
         quantize_w2(1, 0, 2)
-        quantize_da(0, 1)
         quantize_w2(1, 2, 4)
-        lay_w1(0, 0)
+        quantize_da(0, B, C)
         lay_last_g(0, LATE)
+        lay_w2(2, round_on_gpsimd, 0, 2, 0, P // 2)
 
-        lay_w2(2, nc.scalar.copy, 0, 2)
         lay_w2(2, nc.scalar.copy, 2, 4)
+        lay_w2(2, nc.scalar.copy, 0, 2, P // 2, P)
         for t in range(PACK):
             make_x(1, t)
         quantize_g(3)
-        make_da(1, 0)
-        quantize_w2(2, 0, 2)
-        quantize_w1(0, 0)
-        make_da(1, 1)
+        make_da(1, 0, B)
         quantize_w2(2, 2, 4)
-        quantize_da(1, 0)
-        quantize_da(1, 1)
+        make_da(1, B, C)
+        quantize_w2(2, 0, 2)
+        quantize_da(1, 0, B)
+        quantize_da(1, B, C)
+        lay_w1(0, 0)
         lay_w1(0, 1)
-        lay_w1(1, 0)
-        lay_w1(1, 1)
-        dx = dx_bank.tile([P, C], F32, name="dx")
-        add_to_dx(dx, 0, 0, C)
+        lay_w2(3, round_on_gpsimd, 0, 2, 0, P // 2)
 
         silu(2)
         tanh(2, 0, B)
         tanh(2, B, C)
-        lay_w2(3, nc.scalar.copy, 0, 2)
+        lay_w2(3, nc.scalar.copy, 0, 2, P // 2, P)
         lay_w2(3, nc.scalar.copy, 2, 4)
-        for t in range(PACK):
+        for t in (2, 3, 0, 1):
             make_x(2, t)
-        quantize_w1(0, 1)
+        quantize_w1(0)
+        dx = dx_bank.tile([P, C], F32, name="dx")
+        add_to_dx(dx, 0, 0, C)
         add_to_dx(dx, 1, 0, C)
-        make_da(2, 0)
-        quantize_w1(1, 0)
-        make_da(2, 1)
-        quantize_w1(1, 1)
+        make_da(2, 0, B)
+        make_da(2, B, LAST)
+        make_da(2, LAST, C)
         quantize_w2(3, 0, 2)
-        quantize_da(2, 0)
+        quantize_da(2, 0, B)
         quantize_w2(3, 2, 4)
-        quantize_da(2, 1)
-        dx_late = [side_banks.tile([P, B], F32, name="side") for half in range(2)]
-        for half in range(2):
-            add_to_dx(dx_late[half], 2, half * B, (half + 1) * B)
+        quantize_da(2, B, C)
+        lay_w1(1, 0)
+        lay_w1(1, 1)
 
         silu(3, c0=0, c1=B)
         nc.scalar.activation(
@@ -377,22 +377,35 @@ def tile_moe_bdx_mlp_silu_kernel(tc, dyT, a, w2, w1, gate, offs, out):
         for t in range(PACK):
             make_x(3, t, 0, B)
         make_x(3, 0, B, C)
-        make_da(3, 0)
         make_x(3, 1, B, C)
-        quantize_da(3, 0)
+        make_da(3, 0, B)
+        quantize_w1(1)
+        pieces = ((0, B), (B, LAST), (LAST, C))
+        dx_late = [pool.tile([P, c1 - c0], F32, name=name) for (c0, c1), pool, name in zip(pieces, (side_banks, side_banks, dx_bank), ("side", "side", "dx"))]
+        add_to_dx(dx_late[0], 2, 0, B)
+        make_x(3, 2, B, C)
+        quantize_da(3, 0, B)
         add_to_dx(dx_late[0], 3, 0, B)
+        for piece in (1, 2):
+            add_to_dx(dx_late[piece], 2, *pieces[piece])
         nc.scalar.activation(
             dx_slots[2].rearrange("p (c i) -> p c i", i=RUN), dx_late[0][:].rearrange("p (i c) -> p c i", i=RUN), COPY, scale=-0.5
         )
         scatter_on_scalar(2)
-        make_x(3, 2, B, C)
         make_x(3, 3, B, C)
-        make_da(3, 1)
-        quantize_da(3, 1)
-        add_to_dx(dx_late[1], 3, B, C)
-        nc.vector.tensor_scalar_mul(
-            dx_slots[3].rearrange("p (c i) -> p c i", i=RUN), dx_late[1][:].rearrange("p (i c) -> p c i", i=RUN), -0.5
-        )
+        for c0, c1 in pieces[1:]:
+            make_da(3, c0, c1)
+        for piece in (1, 2):
+            c0, c1 = pieces[piece]
+            quantize_da(3, c0, c1)
+            add_to_dx(dx_late[piece], 3, c0, c1)
+        for piece in (1, 2):
+            c0, c1 = pieces[piece]
+            nc.vector.tensor_scalar_mul(
+                dx_slots[3][:, c0 - B : c1 - B].rearrange("p (c i) -> p c i", i=RUN),
+                dx_late[piece][:].rearrange("p (i c) -> p c i", i=RUN),
+                -0.5,
+            )
         nc.vector.tensor_copy(result[:].indirect(listed(3)), dx_slots[3])
 
         for part in range(STORES):

@@ -295,8 +295,8 @@ def tile_moe_bdx_mlp_silu_kernel(tc, dyT, a, w2, w1, gate, offs, out):
         nc.scalar.copy(as_words(g_words[1]), as_planes(g_planes[1]))
         gate_plane(0, 3)
         quantize_g(0)
-        quantize_g(1)
         lay_w2(0, nc.vector.tensor_copy, 2, 4)
+        quantize_g(1)
         lay_w2(0, nc.scalar.copy, 0, 2)
         quantize_w2(0, 3, 4)
         gather_gated(0, 2)
@@ -378,12 +378,13 @@ def tile_moe_bdx_mlp_silu_kernel(tc, dyT, a, w2, w1, gate, offs, out):
             make_x(3, t, 0, B)
         make_x(3, 0, B, C)
         make_x(3, 1, B, C)
-        make_da(3, 0, B)
+        make_x(3, 2, B, C)
         quantize_w1(1)
+        make_da(3, 0, B)
+        make_x(3, 3, B, C)
         pieces = ((0, B), (B, LAST), (LAST, C))
         dx_late = [pool.tile([P, c1 - c0], F32, name=name) for (c0, c1), pool, name in zip(pieces, (side_banks, side_banks, dx_bank), ("side", "side", "dx"))]
         add_to_dx(dx_late[0], 2, 0, B)
-        make_x(3, 2, B, C)
         quantize_da(3, 0, B)
         add_to_dx(dx_late[0], 3, 0, B)
         for piece in (1, 2):
@@ -392,7 +393,6 @@ def tile_moe_bdx_mlp_silu_kernel(tc, dyT, a, w2, w1, gate, offs, out):
             dx_slots[2].rearrange("p (c i) -> p c i", i=RUN), dx_late[0][:].rearrange("p (i c) -> p c i", i=RUN), COPY, scale=-0.5
         )
         scatter_on_scalar(2)
-        make_x(3, 3, B, C)
         for c0, c1 in pieces[1:]:
             make_da(3, c0, c1)
         for piece in (1, 2):

@@ -209,6 +209,11 @@ def tile_moe_bdx_mlp_silu_kernel(tc, dyT, a, w2, w1, gate, offs, out):
                 in_runs(th_of[u % 2])[:, runs_of(c0, c1), t0:t1, :], as_planes(v[u][:, t0:t1, c0:c1]), TANH, scale=0.5
             )
 
+        def x_bytes(u, c0, c1):
+            if (u, c0) == (3, LAST):
+                return th_of[1][:, 0 : (c1 - c0) * PACK]
+            return m_of[u % 2][:, c0 * PACK : c1 * PACK]
+
         def make_x(u, t, c0=0, c1=C):
             e = units[u][0]
             dh = dh_banks.tile([P, c1 - c0], F32, name="dh")
@@ -223,7 +228,8 @@ def tile_moe_bdx_mlp_silu_kernel(tc, dyT, a, w2, w1, gate, offs, out):
                 stop=True,
             )
             m = in_runs(m_of[u % 2])[:, runs_of(c0, c1), t, :]
-            nc.vector.scalar_tensor_tensor(m, m, -1.0, dh[:].rearrange("p (c i) -> p c i", i=RUN), ADD, MULT)
+            x = in_runs(x_bytes(u, c0, c1))[:, :, t, :]
+            nc.vector.scalar_tensor_tensor(x, m, -1.0, dh[:].rearrange("p (c i) -> p c i", i=RUN), ADD, MULT)
 
         def make_da(u, c0, c1):
             part = slice(c0 * PACK, c1 * PACK)
@@ -231,7 +237,7 @@ def tile_moe_bdx_mlp_silu_kernel(tc, dyT, a, w2, w1, gate, offs, out):
                 da_words[u][:, c0:c1, :].rearrange("p (i c) t -> p (c t) i", i=RUN),
                 th_of[u % 2][:, part].rearrange("p (n i) -> p n i", i=RUN),
                 1.0,
-                m_of[u % 2][:, part].rearrange("p (n i) -> p n i", i=RUN),
+                x_bytes(u, c0, c1).rearrange("p (n i) -> p n i", i=RUN),
                 ADD,
                 MULT,
             )
@@ -376,12 +382,11 @@ def tile_moe_bdx_mlp_silu_kernel(tc, dyT, a, w2, w1, gate, offs, out):
         scatter_on_scalar(1)
         for t in range(PACK):
             make_x(3, t, 0, B)
-        make_x(3, 0, B, C)
-        make_x(3, 1, B, C)
-        make_x(3, 2, B, C)
+        for t in range(PACK - 1):
+            make_x(3, t, B, LAST)
         quantize_w1(1)
         make_da(3, 0, B)
-        make_x(3, 3, B, C)
+        make_x(3, PACK - 1, B, LAST)
         pieces = ((0, B), (B, LAST), (LAST, C))
         dx_late = [pool.tile([P, c1 - c0], F32, name=name) for (c0, c1), pool, name in zip(pieces, (side_banks, side_banks, dx_bank), ("side", "side", "dx"))]
         add_to_dx(dx_late[0], 2, 0, B)
@@ -393,6 +398,8 @@ def tile_moe_bdx_mlp_silu_kernel(tc, dyT, a, w2, w1, gate, offs, out):
             dx_slots[2].rearrange("p (c i) -> p c i", i=RUN), dx_late[0][:].rearrange("p (i c) -> p c i", i=RUN), COPY, scale=-0.5
         )
         scatter_on_scalar(2)
+        for t in range(PACK):
+            make_x(3, t, LAST, C)
         for c0, c1 in pieces[1:]:
             make_da(3, c0, c1)
         for piece in (1, 2):

@@ -52,7 +52,7 @@ def tile_moe_bdx_mlp_silu_kernel(tc, dyT, a, w2, w1, gate, offs, out):
         offsets = lists.tile([P, S // LIST_ROWS], U16, name="offsets")
         dy = [keep.tile([P, T], F32, name=f"dy{t}") for t in range(PACK)]
         g_first = keep.tile([P, PACK, B], F32, name="g_first")
-        g_fourth = keep.tile([P, PACK, B], F32, name="g_fourth")
+        g_fourth = keep.tile([P, PACK, B], F32, name="g_fourth", align_bytes=64)
         room_m = keep.tile([P, 2 * PACK * C + 2 * B], F32, name="room_m", align_bytes=64)
         room_w2 = keep.tile([P, (2 * PACK + 1) * B], F32, name="room_w2", align_bytes=64)
 
@@ -67,8 +67,7 @@ def tile_moe_bdx_mlp_silu_kernel(tc, dyT, a, w2, w1, gate, offs, out):
         th_of = [room_m[:, PACK * C + 2 * B :], keep.tile([P, PACK * C], F32, name="th_odd")[:]]
         w1_raw = [keep.tile([P, HALVES, PACK, K], F32, name=f"w1_raw{e}") for e in range(E)]
 
-        w2_words = {u: keep.tile([P, PACK, P, PACK], BF16, name=f"w2_words{u}", align_bytes=64)[:] for u in (2, 3)}
-        w2_words[1] = room_w2[:, 0 : PACK * B].bitcast(BF16).rearrange("p (t q j) -> p t q j", t=PACK, j=PACK)
+        w2_words = {u: keep.tile([P, PACK, P, PACK], BF16, name=f"w2_words{u}", align_bytes=64)[:] for u in (1, 2, 3)}
         first_pairs = [
             room[:, start : start + 2 * B].bitcast(BF16).rearrange("p (t q j) -> p t q j", t=2, j=PACK)
             for room, start in ((room_m, PACK * C), (room_w2, PACK * B))
@@ -77,8 +76,12 @@ def tile_moe_bdx_mlp_silu_kernel(tc, dyT, a, w2, w1, gate, offs, out):
         def w2_tiles(u, t0, t1):
             if u == 0:
                 return first_pairs[t0 // 2][:, t0 % 2 : t0 % 2 + t1 - t0]
-            if u >= 2 and t0 == 0:
-                return da_words[u - 2][:, B:C, :].rearrange("p (t q) j -> p t q j", t=2)
+            if u == 1 and t0 == 0:
+                return first_pairs[0][:, 0 : t1 - t0]
+            if u == 2 and t0 == 0:
+                return g_fourth[:, 0:2, :].rearrange("p a b -> p (a b)").bitcast(BF16).rearrange("p (t q j) -> p t q j", t=2, j=PACK)
+            if u == 3 and t0 == 0:
+                return da_words[1][:, B:C, :].rearrange("p (t q) j -> p t q j", t=2)
             return w2_words[u][:, t0:t1]
 
         w2_codes = [keep.tile([P, PASS], U32, name=f"w2_codes{u}", align_bytes=64) for u in range(4)]
@@ -89,8 +92,8 @@ def tile_moe_bdx_mlp_silu_kernel(tc, dyT, a, w2, w1, gate, offs, out):
         g_words.append(room_w2[:, start : start + 2 * B].bitcast(BF16).rearrange("p (c t) -> p c t", t=PACK))
         g_codes = [keep.tile([P, C], U32, name=f"g_codes{e}", align_bytes=64) for e in range(E)]
         g_scales = [keep.tile([P, C], U8, name=f"g_scales{e}", align_bytes=64) for e in range(E)]
-        da_words = [keep.tile([P, C, PACK], BF16, name=f"da_words{u}", align_bytes=64) for u in range(3)]
-        da_words.append(da_words[2])
+        da_words = [keep.tile([P, C, PACK], BF16, name=f"da_words{u}", align_bytes=64)[:] for u in (1, 2)]
+        da_words = [room_w2[:, 0 : PACK * B].bitcast(BF16).rearrange("p (c t) -> p c t", t=PACK)] + da_words + da_words[1:]
         da_codes = [keep.tile([P, C], U32, name=f"da_codes{u}", align_bytes=64) for u in range(4)]
         da_scales = [keep.tile([P, C], U8, name=f"da_scales{u}", align_bytes=64) for u in range(4)]
         w1_words = {
@@ -271,8 +274,9 @@ def tile_moe_bdx_mlp_silu_kernel(tc, dyT, a, w2, w1, gate, offs, out):
         load_w2(0)
         load_a(0, 2, 4)
         load_a(0, 0, 2)
-        load_a(1)
         load_w2(1)
+        load_a(1, 0, 2)
+        load_a(1, 2, 4)
         load_w2(2)
         load_a(2)
         load_w1(0)
@@ -319,14 +323,15 @@ def tile_moe_bdx_mlp_silu_kernel(tc, dyT, a, w2, w1, gate, offs, out):
             make_x(0, t)
         quantize_g(2)
         make_da(0, 0, B)
-        make_da(0, B, C)
-        silu(1)
-        lay_w2(1, nc.scalar.copy, 2, 4)
-        tanh(1, 0, B)
-        tanh(1, B, C)
         lay_w2(1, nc.vector.tensor_copy, 0, 2)
         quantize_da(0, 0, B)
         quantize_w2(1, 0, 2)
+        make_da(0, B, C)
+        lay_w2(1, nc.scalar.copy, 2, 4)
+        silu(1, 0, 2)
+        silu(1, 2, 4)
+        tanh(1, 0, B)
+        tanh(1, B, C)
         quantize_w2(1, 2, 4)
         quantize_da(0, B, C)
         lay_last_g(0, LATE)
@@ -347,7 +352,8 @@ def tile_moe_bdx_mlp_silu_kernel(tc, dyT, a, w2, w1, gate, offs, out):
         lay_w1(0, 1)
         lay_w2(3, round_on_gpsimd, 0, 2, 0, P // 2)
 
-        silu(2)
+        silu(2, 2, 4)
+        silu(2, 0, 2)
         tanh(2, 0, B)
         tanh(2, B, C)
         lay_w2(3, nc.scalar.copy, 0, 2, P // 2, P)
@@ -369,11 +375,8 @@ def tile_moe_bdx_mlp_silu_kernel(tc, dyT, a, w2, w1, gate, offs, out):
         lay_w1(1, 1)
 
         silu(3, c0=0, c1=B)
-        nc.scalar.activation(
-            dx_first[:].rearrange("p (b c i) -> p b c i", b=2, i=RUN),
-            dx[:].rearrange("p (b i c) -> p b c i", b=2, i=RUN),
-            COPY,
-            scale=-0.5,
+        nc.vector.tensor_scalar_mul(
+            dx_first[:].rearrange("p (b c i) -> p b c i", b=2, i=RUN), dx[:].rearrange("p (b i c) -> p b c i", b=2, i=RUN), -0.5
         )
         tanh(3, 0, B)
         silu(3, c0=B, c1=C)

@@ -26,6 +26,7 @@ RUN = 4
 LIST_ROWS = 16
 B = C // 2
 BLOCKS = S // B
+LOAD_ALIGN = 256
 STORES = 4
 LAST = C - B // 2
 LATE = 3 * B // 4
@@ -50,7 +51,7 @@ def tile_moe_bdx_mlp_silu_kernel(tc, dyT, a, w2, w1, gate, offs, out):
         dx_bank = ctx.enter_context(tc.psum_pool(name="dx_bank", bufs=1))
 
         offsets = lists.tile([P, S // LIST_ROWS], U16, name="offsets")
-        dy = [keep.tile([P, T], F32, name=f"dy{t}") for t in range(PACK)]
+        dy = [keep.tile([P, T], F32, name=f"dy{t}", align_bytes=LOAD_ALIGN) for t in range(PACK)]
         g_first = keep.tile([P, PACK, B], F32, name="g_first")
         g_fourth = keep.tile([P, PACK, B], F32, name="g_fourth", align_bytes=64)
         room_m = keep.tile([P, 2 * PACK * C + 2 * B], F32, name="room_m", align_bytes=64)
@@ -61,11 +62,11 @@ def tile_moe_bdx_mlp_silu_kernel(tc, dyT, a, w2, w1, gate, offs, out):
 
         g_planes = [g_first[:], planes_at(room_m, PACK * C - B), planes_at(room_w2, (PACK + 1) * B), g_fourth[:]]
         gates = {b: keep.tile([P, B], F32, name=f"gates{b}") for b in (1, 2)}
-        w2_raw = {u: keep.tile([P, PACK, PASS], F32, name=f"w2_raw{u}") for u in range(4)}
-        v = [keep.tile([P, PACK, C], F32, name=f"v{u}", align_bytes=64) for u in range(4)]
+        w2_raw = {u: keep.tile([P, PACK, PASS], F32, name=f"w2_raw{u}", align_bytes=LOAD_ALIGN) for u in range(4)}
+        v = [keep.tile([P, PACK, C], F32, name=f"v{u}", align_bytes=LOAD_ALIGN) for u in range(4)]
         m_of = [room_m[:, 0 : PACK * C], keep.tile([P, PACK * C], F32, name="m_odd")[:]]
         th_of = [room_m[:, PACK * C + 2 * B :], keep.tile([P, PACK * C], F32, name="th_odd")[:]]
-        w1_raw = [keep.tile([P, HALVES, PACK, K], F32, name=f"w1_raw{e}") for e in range(E)]
+        w1_raw = [keep.tile([P, HALVES, PACK, K], F32, name=f"w1_raw{e}", align_bytes=LOAD_ALIGN) for e in range(E)]
 
         w2_words = {u: keep.tile([P, PACK, P, PACK], BF16, name=f"w2_words{u}", align_bytes=64)[:] for u in (1, 2, 3)}
         first_pairs = [
@@ -103,7 +104,7 @@ def tile_moe_bdx_mlp_silu_kernel(tc, dyT, a, w2, w1, gate, offs, out):
         w1_scales = [keep.tile([P, HALVES * K], U8, name=f"w1_scales{e}", align_bytes=64) for e in range(E)]
         dx_first = keep.tile([P, C], F32, name="dx_first")
         dx_slots = [dx_first[:, 0:B], dx_first[:, B:C]] + [keep.tile([P, B], F32, name=f"dx_slots{b}")[:] for b in (2, 3)]
-        result = keep.tile([P, T], F32, name="result")
+        result = keep.tile([P, T], F32, name="result", align_bytes=LOAD_ALIGN)
         gate_columns = keep.tile([P, E, C // P], F32, name="gate_columns")
         zero = keep.tile([P, 1], F32, name="zero")
         identity = keep.tile([P, P], F32, name="identity")

@@ -279,10 +279,12 @@ def tile_moe_bdx_mlp_silu_kernel(tc, dyT, a, w2, w1, gate, offs, out):
         load_a(1, 0, 2)
         load_a(1, 2, 4)
         load_w2(2)
-        load_a(2)
+        load_a(2, 2, 4)
+        load_a(2, 0, 2)
         load_w1(0)
         load_w2(3)
-        load_a(3)
+        load_a(3, 0, 2)
+        load_a(3, 2, 4)
         load_w1(1)
 
         make_identity(nc, identity[:])
@@ -375,12 +377,12 @@ def tile_moe_bdx_mlp_silu_kernel(tc, dyT, a, w2, w1, gate, offs, out):
         lay_w1(1, 0)
         lay_w1(1, 1)
 
-        silu(3, c0=0, c1=B)
+        silu(3, 0, 2)
+        silu(3, 2, 4)
         nc.vector.tensor_scalar_mul(
             dx_first[:].rearrange("p (b c i) -> p b c i", b=2, i=RUN), dx[:].rearrange("p (b i c) -> p b c i", b=2, i=RUN), -0.5
         )
         tanh(3, 0, B)
-        silu(3, c0=B, c1=C)
         scatter_on_scalar(0)
         tanh(3, B, C)
         scatter_on_scalar(1)

@@ -79,8 +79,6 @@ def tile_moe_bdx_mlp_silu_kernel(tc, dyT, a, w2, w1, gate, offs, out):
                 return first_pairs[t0 // 2][:, t0 % 2 : t0 % 2 + t1 - t0]
             if u == 1 and t0 == 0:
                 return first_pairs[0][:, 0 : t1 - t0]
-            if u == 2 and t0 == 0:
-                return g_fourth[:, 0:2, :].rearrange("p a b -> p (a b)").bitcast(BF16).rearrange("p (t q j) -> p t q j", t=2, j=PACK)
             if u == 3 and t0 == 0:
                 return da_words[1][:, B:C, :].rearrange("p (t q) j -> p t q j", t=2)
             return w2_words[u][:, t0:t1]

@@ -27,6 +27,7 @@ LIST_ROWS = 16
 B = C // 2
 BLOCKS = S // B
 LOAD_ALIGN = 256
+CUT = C + B // 2
 STORES = 4
 LAST = C - B // 2
 LATE = 3 * B // 4
@@ -53,15 +54,12 @@ def tile_moe_bdx_mlp_silu_kernel(tc, dyT, a, w2, w1, gate, offs, out):
         offsets = lists.tile([P, S // LIST_ROWS], U16, name="offsets")
         dy = [keep.tile([P, T], F32, name=f"dy{t}", align_bytes=LOAD_ALIGN) for t in range(PACK)]
         g_first = keep.tile([P, PACK, B], F32, name="g_first")
-        g_fourth = keep.tile([P, PACK, B], F32, name="g_fourth", align_bytes=64)
         room_m = keep.tile([P, 2 * PACK * C + 2 * B], F32, name="room_m", align_bytes=64)
-        room_w2 = keep.tile([P, (2 * PACK + 1) * B], F32, name="room_w2", align_bytes=64)
+        room_w2 = keep.tile([P, (PACK + 3 * PACK) * B], F32, name="room_w2", align_bytes=64)
 
-        def planes_at(room, start):
-            return room[:, start : start + PACK * B].rearrange("p (t s) -> p t s", t=PACK)
-
-        g_planes = [g_first[:], planes_at(room_m, PACK * C - B), planes_at(room_w2, (PACK + 1) * B), g_fourth[:]]
-        gates = {b: keep.tile([P, B], F32, name=f"gates{b}") for b in (1, 2)}
+        g_later = room_w2[:, PACK * B :].rearrange("p (t s) -> p t s", t=PACK)
+        g_planes = [g_first[:]] + [g_later[:, :, b * B : (b + 1) * B] for b in range(3)]
+        gates = keep.tile([P, 2 * B], F32, name="gates")
         w2_raw = {u: keep.tile([P, PACK, PASS], F32, name=f"w2_raw{u}", align_bytes=LOAD_ALIGN) for u in range(4)}
         v = [keep.tile([P, PACK, C], F32, name=f"v{u}", align_bytes=LOAD_ALIGN) for u in range(4)]
         m_of = [room_m[:, 0 : PACK * C], keep.tile([P, PACK * C], F32, name="m_odd")[:]]
@@ -146,17 +144,21 @@ def tile_moe_bdx_mlp_silu_kernel(tc, dyT, a, w2, w1, gate, offs, out):
             return gate_banks[b // 2][:, :, half].rearrange("r j p -> r p j")
 
         def copy_gates(b):
-            nc.vector.tensor_copy(gates[b][:].rearrange("r (p j) -> r p j", j=RUN), gates_in_bank(b))
+            nc.vector.tensor_copy(gates[:, (b - 1) * B : b * B].rearrange("r (p j) -> r p j", j=RUN), gates_in_bank(b))
 
-        def gather_gated(t, b):
-            nc.vector.tensor_tensor(g_planes[b][:, t, :], dy[t][:].indirect(listed(b)), gates[b][:], MULT)
+        def between(s0, s1):
+            return offsets[:, s0 // LIST_ROWS : s1 // LIST_ROWS]
 
-        def gather_plain(t, b):
-            nc.scalar.activation(g_planes[b][:, t, :], dy[t][:].indirect(listed(b)), COPY)
+        def gather_gated(t, s0, s1):
+            nc.vector.tensor_tensor(g_later[:, t, s0 - B : s1 - B], dy[t][:].indirect(between(s0, s1)), gates[:, s0 - B : s1 - B], MULT)
 
-        def gate_plane(t, b):
-            plane = g_planes[b][:, t, :].rearrange("r (p j) -> r p j", j=RUN)
-            nc.vector.tensor_tensor(plane, plane, gates_in_bank(b), MULT)
+        def gather_plain(t, s0, s1):
+            plane = g_first[:, t, :] if s0 == 0 else g_later[:, t, s0 - B : s1 - B]
+            nc.scalar.activation(plane, dy[t][:].indirect(between(s0, s1)), COPY)
+
+        def gate_plane(t, s0):
+            plane = g_later[:, t, s0 - B :].rearrange("r (p j) -> r p j", j=RUN)
+            nc.vector.tensor_tensor(plane, plane, gate_banks[1][:, :, (s0 - C) // RUN :].rearrange("r j p -> r p j"), MULT)
 
         def gate_and_lay(b):
             nc.vector.tensor_tensor(
@@ -294,23 +296,26 @@ def tile_moe_bdx_mlp_silu_kernel(tc, dyT, a, w2, w1, gate, offs, out):
         nc.vector.memset(result[:], 0.0)
 
         for t in (1, 2, 3):
-            gather_plain(t, 0)
-            gather_gated(t, 1)
-            gather_plain(t, 3)
-            gather_gated(t, 2)
-            gate_plane(t, 3)
-        gather_plain(0, 0)
-        gather_gated(0, 1)
+            gather_plain(t, CUT, S)
+            gather_plain(t, 0, B)
+            if t == 1:
+                gather_gated(t, B, C)
+                gather_gated(t, C, CUT)
+            else:
+                gather_gated(t, B, CUT)
+            gate_plane(t, CUT)
+        gather_plain(0, 0, B)
+        gather_gated(0, B, C)
         gate_and_lay(0)
-        gather_plain(0, 3)
+        gather_plain(0, S - B, S)
         nc.scalar.copy(as_words(g_words[1]), as_planes(g_planes[1]))
-        gate_plane(0, 3)
+        gate_plane(0, S - B)
         quantize_g(0)
         lay_w2(0, nc.vector.tensor_copy, 2, 4)
         quantize_g(1)
         lay_w2(0, nc.scalar.copy, 0, 2)
         quantize_w2(0, 3, 4)
-        gather_gated(0, 2)
+        gather_gated(0, C, S - B)
         quantize_w2(0, 2, 3)
         quantize_w2(0, 0, 2)
         lay_on_gpsimd(g_words[2], g_planes[2])

from contextlib import ExitStack

import concourse.mybir as mybir
from concourse.masks import make_identity

F32 = mybir.dt.float32
BF16 = mybir.dt.bfloat16
U32 = mybir.dt.uint32
U16 = mybir.dt.uint16
U8 = mybir.dt.uint8
E4M3 = mybir.dt.float8_e4m3fn_x4
E5M2 = mybir.dt.float8_e5m2_x4
ADD = mybir.AluOpType.add
MULT = mybir.AluOpType.mult
COPY = mybir.ActivationFunctionType.Copy
TANH = mybir.ActivationFunctionType.Tanh
SILU = mybir.ActivationFunctionType.Silu

P = 128
K, T, E, C, H, N = 128, 1536, 2, 512, 1024, 512
S = E * C
PACK = 4
PASS = P * PACK
HALVES = H // PASS
RUN = 4
LIST_ROWS = 16
B = C // 2
BLOCKS = S // B
LOAD_ALIGN = 256
CUT = C + B // 2
STORES = 4
LAST = C - B // 2
LATE = 3 * B // 4

FLOPS = 2 * S * N * H + 2 * S * H * K
BYTES = 4 * (N * T + H * S + E * N * H + E * H * K + S + K * T) + 2 * S


def tile_moe_bdx_mlp_silu_kernel(tc, dyT, a, w2, w1, gate, offs, out):
    nc = tc.nc
    dy_planes = dyT.rearrange("(p t) s -> p t s", t=PACK)
    a_planes = a.rearrange("(h p t) s -> p h t s", h=HALVES, t=PACK)
    w2_planes = w2.rearrange("e (p j) i -> p e j i", j=PACK)
    w1_planes = w1.rearrange("e (h p j) k -> p e h j k", h=HALVES, j=PACK)
    units = [(e, h) for e in range(E) for h in range(HALVES)]

    with ExitStack() as ctx:
        lists = ctx.enter_context(tc.tile_pool(name="lists", bufs=1))
        keep = ctx.enter_context(tc.tile_pool(name="keep", bufs=1))
        dh_banks = ctx.enter_context(tc.psum_pool(name="dh_banks", bufs=5))
        side_banks = ctx.enter_context(tc.psum_pool(name="side_banks", bufs=2))
        dx_bank = ctx.enter_context(tc.psum_pool(name="dx_bank", bufs=1))

        offsets = lists.tile([P, S // LIST_ROWS], U16, name="offsets")
        dy = [keep.tile([P, T], F32, name=f"dy{t}", align_bytes=LOAD_ALIGN) for t in range(PACK)]
        g_first = keep.tile([P, PACK, B], F32, name="g_first")
        room_m = keep.tile([P, 2 * PACK * C + 2 * B], F32, name="room_m", align_bytes=64)
        room_w2 = keep.tile([P, (PACK + 3 * PACK) * B], F32, name="room_w2", align_bytes=64)

        g_later = room_w2[:, PACK * B :].rearrange("p (t s) -> p t s", t=PACK)
        g_planes = [g_first[:]] + [g_later[:, :, b * B : (b + 1) * B] for b in range(3)]
        gates = keep.tile([P, 2 * B], F32, name="gates")
        w2_raw = {u: keep.tile([P, PACK, PASS], F32, name=f"w2_raw{u}", align_bytes=LOAD_ALIGN) for u in range(4)}
        v = [keep.tile([P, PACK, C], F32, name=f"v{u}", align_bytes=LOAD_ALIGN) for u in range(4)]
        m_of = [room_m[:, 0 : PACK * C], keep.tile([P, PACK * C], F32, name="m_odd")[:]]
        th_of = [room_m[:, PACK * C + 2 * B :], keep.tile([P, PACK * C], F32, name="th_odd")[:]]
        w1_raw = [keep.tile([P, HALVES, PACK, K], F32, name=f"w1_raw{e}", align_bytes=LOAD_ALIGN) for e in range(E)]

        w2_words = {u: keep.tile([P, PACK, P, PACK], BF16, name=f"w2_words{u}", align_bytes=64)[:] for u in (1, 2, 3)}
        first_pairs = [
            room[:, start : start + 2 * B].bitcast(BF16).rearrange("p (t q j) -> p t q j", t=2, j=PACK)
            for room, start in ((room_m, PACK * C), (room_w2, PACK * B))
        ]

        def w2_tiles(u, t0, t1):
            if u == 0:
                return first_pairs[t0 // 2][:, t0 % 2 : t0 % 2 + t1 - t0]
            if u == 1 and t0 == 0:
                return first_pairs[0][:, 0 : t1 - t0]
            if u == 3 and t0 == 0:
                return da_words[1][:, B:C, :].rearrange("p (t q) j -> p t q j", t=2)
            return w2_words[u][:, t0:t1]

        w2_codes = [keep.tile([P, PASS], U32, name=f"w2_codes{u}", align_bytes=64) for u in range(4)]
        w2_scales = [keep.tile([P, PASS], U8, name=f"w2_scales{u}", align_bytes=64) for u in range(4)]
        g_words = [keep.tile([P, B, PACK], BF16, name=f"g_words{b}", align_bytes=64)[:] for b in range(2)]
        g_words.append(first_pairs[0].rearrange("p t q j -> p (t q) j"))
        start = PACK * B - 2 * LATE
        g_words.append(room_w2[:, start : start + 2 * B].bitcast(BF16).rearrange("p (c t) -> p c t", t=PACK))
        g_codes = [keep.tile([P, C], U32, name=f"g_codes{e}", align_bytes=64) for e in range(E)]
        g_scales = [keep.tile([P, C], U8, name=f"g_scales{e}", align_bytes=64) for e in range(E)]
        da_words = [keep.tile([P, C, PACK], BF16, name=f"da_words{u}", align_bytes=64)[:] for u in (1, 2)]
        da_words = [room_w2[:, 0 : PACK * B].bitcast(BF16).rearrange("p (c t) -> p c t", t=PACK)] + da_words + da_words[1:]
        da_codes = [keep.tile([P, C], U32, name=f"da_codes{u}", align_bytes=64) for u in range(4)]
        da_scales = [keep.tile([P, C], U8, name=f"da_scales{u}", align_bytes=64) for u in range(4)]
        w1_words = {
            (e, h): da_words[1 + e][:, e * B + h * K : e * B + (h + 1) * K, :] for e in range(E) for h in range(HALVES)
        }
        w1_codes = [keep.tile([P, HALVES * K], U32, name=f"w1_codes{e}", align_bytes=64) for e in range(E)]
        w1_scales = [keep.tile([P, HALVES * K], U8, name=f"w1_scales{e}", align_bytes=64) for e in range(E)]
        dx_first = keep.tile([P, C], F32, name="dx_first")
        dx_slots = [dx_first[:, 0:B], dx_first[:, B:C]] + [keep.tile([P, B], F32, name=f"dx_slots{b}")[:] for b in (2, 3)]
        result = keep.tile([P, T], F32, name="result", align_bytes=LOAD_ALIGN)
        gate_columns = keep.tile([P, E, C // P], F32, name="gate_columns")
        zero = keep.tile([P, 1], F32, name="zero")
        identity = keep.tile([P, P], F32, name="identity")

        def as_words(words):
            return words.rearrange("p (c i) t -> p c t i", i=RUN)

        def as_planes(planes):
            return planes.rearrange("p t (c i) -> p c t i", i=RUN)

        def in_runs(flat):
            return flat.rearrange("p (c t i) -> p c t i", t=PACK, i=RUN)

        def listed(b):
            return offsets[:, b * B // LIST_ROWS : (b + 1) * B // LIST_ROWS]

        def load_a(u, t0=0, t1=PACK):
            e, h = units[u]
            nc.sync.dma_start(v[u][:, t0:t1, :], a_planes[:, h, t0:t1, e * C : (e + 1) * C])

        def load_dy(t):
            nc.sync.dma_start(dy[t][:], dy_planes[:, t, :])

        def load_w2(u):
            e, h = units[u]
            nc.sync.dma_start(w2_raw[u][:], w2_planes[:, e, :, h * PASS : (h + 1) * PASS])

        def load_w1(e):
            nc.sync.dma_start(w1_raw[e][:], w1_planes[:, e])

        gate_banks = []

        def spread_gates(e):
            bank = side_banks.tile([P, C // P, P], F32, name="side")
            for j in range(C // P):
                nc.tensor.transpose(bank[:, j, :], gate_columns[:, e, j : j + 1].to_broadcast([P, P]), identity[:])
            gate_banks.append(bank)

        def gates_in_bank(b):
            half = slice(b % 2 * P // 2, (b % 2 + 1) * P // 2)
            return gate_banks[b // 2][:, :, half].rearrange("r j p -> r p j")

        def copy_gates(b):
            nc.vector.tensor_copy(gates[:, (b - 1) * B : b * B].rearrange("r (p j) -> r p j", j=RUN), gates_in_bank(b))

        def between(s0, s1):
            return offsets[:, s0 // LIST_ROWS : s1 // LIST_ROWS]

        def gather_gated(t, s0, s1):
            nc.vector.tensor_tensor(g_later[:, t, s0 - B : s1 - B], dy[t][:].indirect(between(s0, s1)), gates[:, s0 - B : s1 - B], MULT)

        def gather_plain(t, s0, s1):
            plane = g_first[:, t, :] if s0 == 0 else g_later[:, t, s0 - B : s1 - B]
            nc.scalar.activation(plane, dy[t][:].indirect(between(s0, s1)), COPY)

        def gate_plane(t, s0):
            plane = g_later[:, t, s0 - B :].rearrange("r (p j) -> r p j", j=RUN)
            nc.vector.tensor_tensor(plane, plane, gate_banks[1][:, :, (s0 - C) // RUN :].rearrange("r j p -> r p j"), MULT)

        def gate_and_lay(b):
            nc.vector.tensor_tensor(
                as_words(g_words[b]),
                as_planes(g_planes[b]),
                gates_in_bank(b).unsqueeze(2).to_broadcast([P, B // RUN, PACK, RUN]),
                MULT,
            )

        def lay_on_gpsimd(words, planes):
            nc.gpsimd.tensor_scalar(as_words(words), as_planes(planes), 1.0, 0.0, MULT, ADD)

        def quantize(codes, scales, words, fmt):
            nc.vector.quantize_mx(out=codes.bitcast(fmt), scales=scales, in_=words)

        def quantize_g(b):
            columns = slice(b % 2 * B, (b % 2 + 1) * B)
            quantize(g_codes[b // 2][:, columns], g_scales[b // 2][:, columns], g_words[b].rearrange("p c t -> p (c t)"), E5M2)

        def lay_last_g(c0, c1):
            lay_on_gpsimd(g_words[3][:, c0:c1, :], g_planes[3][:, :, c0:c1])

        def lay_w2(u, copy, t0, t1, q0=0, q1=P):
            copy(
                w2_tiles(u, t0, t1).rearrange("p t q j -> p q j t")[:, q0:q1],
                w2_raw[u][:].rearrange("p j (q t) -> p q j t", t=PACK)[:, q0:q1, :, t0:t1],
            )

        def round_on_gpsimd(words, values):
            nc.gpsimd.tensor_scalar(words, values, 1.0, 0.0, MULT, ADD)

        def quantize_w2(u, t0, t1):
            columns = slice(t0 * P, t1 * P)
            quantize(w2_codes[u][:, columns], w2_scales[u][:, columns], w2_tiles(u, t0, t1).rearrange("p t q j -> p (t q j)"), E4M3)

        def lay_w1(e, h):
            lay_on_gpsimd(w1_words[e, h], w1_raw[e][:, h])

        def quantize_w1(e):
            quantize(w1_codes[e][:], w1_scales[e][:], da_words[1 + e][:, e * B : (e + 1) * B, :].rearrange("p k j -> p (k j)"), E4M3)

        def runs_of(c0, c1):
            return slice(c0 // RUN, c1 // RUN)

        def silu(u, t0=0, t1=PACK, c0=0, c1=C):
            nc.scalar.activation(
                in_runs(m_of[u % 2])[:, runs_of(c0, c1), t0:t1, :], as_planes(v[u][:, t0:t1, c0:c1]), SILU, scale=-1.0, bias=zero[:]
            )

        def tanh(u, c0=0, c1=C, t0=0, t1=PACK):
            nc.scalar.activation(
                in_runs(th_of[u % 2])[:, runs_of(c0, c1), t0:t1, :], as_planes(v[u][:, t0:t1, c0:c1]), TANH, scale=0.5
            )

        def x_bytes(u, c0, c1):
            if (u, c0) == (3, LAST):
                return th_of[1][:, 0 : (c1 - c0) * PACK]
            return m_of[u % 2][:, c0 * PACK : c1 * PACK]

        def make_x(u, t, c0=0, c1=C):
            e = units[u][0]
            dh = dh_banks.tile([P, c1 - c0], F32, name="dh")
            columns = slice(t * P, (t + 1) * P)
            nc.tensor.matmul_mx(
                out=dh[:],
                lhsT=w2_codes[u][:, columns].bitcast(E4M3),
                lhsT_scale=w2_scales[u][:, columns],
                rhs=g_codes[e][:, c0:c1].bitcast(E5M2),
                rhs_scale=g_scales[e][:, c0:c1],
                start=True,
                stop=True,
            )
            m = in_runs(m_of[u % 2])[:, runs_of(c0, c1), t, :]
            x = in_runs(x_bytes(u, c0, c1))[:, :, t, :]
            nc.vector.scalar_tensor_tensor(x, m, -1.0, dh[:].rearrange("p (c i) -> p c i", i=RUN), ADD, MULT)

        def make_da(u, c0, c1):
            part = slice(c0 * PACK, c1 * PACK)
            nc.vector.scalar_tensor_tensor(
                da_words[u][:, c0:c1, :].rearrange("p (i c) t -> p (c t) i", i=RUN),
                th_of[u % 2][:, part].rearrange("p (n i) -> p n i", i=RUN),
                1.0,
                x_bytes(u, c0, c1).rearrange("p (n i) -> p n i", i=RUN),
                ADD,
                MULT,
            )

        def quantize_da(u, c0, c1):
            columns = slice(c0, c1)
            quantize(da_codes[u][:, columns], da_scales[u][:, columns], da_words[u][:, columns, :].rearrange("p c t -> p (c t)"), E5M2)

        def add_to_dx(dx, u, c0, c1):
            e, h = units[u]
            columns = slice(h * K, (h + 1) * K)
            nc.tensor.matmul_mx(
                out=dx[:],
                lhsT=w1_codes[e][:, columns].bitcast(E4M3),
                lhsT_scale=w1_scales[e][:, columns],
                rhs=da_codes[u][:, c0:c1].bitcast(E5M2),
                rhs_scale=da_scales[u][:, c0:c1],
                start=(h == 0),
                stop=(h == HALVES - 1),
            )

        def scatter_on_scalar(b):
            nc.scalar.activation(result[:].indirect(listed(b)), dx_slots[b], COPY)

        nc.sync.dma_start(gate_columns[:], gate[0, :].rearrange("(e p j) -> p e j", e=E, p=P))
        load_dy(1)
        nc.sync.dma_start(offsets[:], offs)
        load_dy(2)
        load_dy(3)
        load_dy(0)
        load_w2(0)
        load_a(0, 2, 4)
        load_a(0, 0, 2)
        load_w2(1)
        load_a(1, 0, 2)
        load_a(1, 2, 4)
        load_w2(2)
        load_a(2, 2, 4)
        load_a(2, 0, 2)
        load_w1(0)
        load_w2(3)
        load_a(3, 0, 2)
        load_a(3, 2, 4)
        load_w1(1)

        make_identity(nc, identity[:])
        nc.vector.memset(zero[:], 0.0)
        nc.scalar.activation(zero[:], zero[:], SILU)
        for e in range(E):
            spread_gates(e)
            copy_gates(e + 1)
        nc.vector.memset(result[:], 0.0)

        for t in (1, 2, 3):
            gather_plain(t, CUT, S)
            gather_plain(t, 0, B)
            if t == 1:
                gather_gated(t, B, C)
                gather_gated(t, C, CUT)
            else:
                gather_gated(t, B, CUT)
            gate_plane(t, CUT)
        gather_plain(0, 0, B)
        gather_gated(0, B, C)
        gate_and_lay(0)
        gather_plain(0, S - B, S)
        nc.scalar.copy(as_words(g_words[1]), as_planes(g_planes[1]))
        gate_plane(0, S - B)
        quantize_g(0)
        lay_w2(0, nc.vector.tensor_copy, 2, 4)
        quantize_g(1)
        lay_w2(0, nc.scalar.copy, 0, 2)
        quantize_w2(0, 3, 4)
        gather_gated(0, C, S - B)
        quantize_w2(0, 2, 3)
        quantize_w2(0, 0, 2)
        lay_on_gpsimd(g_words[2], g_planes[2])
        lay_last_g(LATE, B)

        for t0 in (2, 0):
            silu(0, t0, t0 + 2)
        tanh(0, 0, B)
        tanh(0, B, C)
        for t in (3, 2, 0, 1):
            make_x(0, t)
        quantize_g(2)
        make_da(0, 0, B)
        lay_w2(1, nc.vector.tensor_copy, 0, 2)
        quantize_da(0, 0, B)
        quantize_w2(1, 0, 2)
        make_da(0, B, C)
        lay_w2(1, nc.scalar.copy, 2, 4)
        silu(1, 0, 2)
        silu(1, 2, 4)
        tanh(1, 0, B)
        tanh(1, B, C)
        quantize_w2(1, 2, 4)
        quantize_da(0, B, C)
        lay_last_g(0, LATE)
        lay_w2(2, round_on_gpsimd, 0, 2, 0, P // 2)

        lay_w2(2, nc.scalar.copy, 2, 4)
        lay_w2(2, nc.scalar.copy, 0, 2, P // 2, P)
        for t in range(PACK):
            make_x(1, t)
        quantize_g(3)
        make_da(1, 0, B)
        quantize_w2(2, 2, 4)
        make_da(1, B, C)
        quantize_w2(2, 0, 2)
        quantize_da(1, 0, B)
        quantize_da(1, B, C)
        lay_w1(0, 0)
        lay_w1(0, 1)
        lay_w2(3, round_on_gpsimd, 0, 2, 0, P // 2)

        silu(2, 2, 4)
        silu(2, 0, 2)
        tanh(2, 0, B)
        tanh(2, B, C)
        lay_w2(3, nc.scalar.copy, 0, 2, P // 2, P)
        lay_w2(3, nc.scalar.copy, 2, 4)
        for t in (2, 3, 0, 1):
            make_x(2, t)
        quantize_w1(0)
        dx = dx_bank.tile([P, C], F32, name="dx")
        add_to_dx(dx, 0, 0, C)
        add_to_dx(dx, 1, 0, C)
        make_da(2, 0, B)
        make_da(2, B, LAST)
        make_da(2, LAST, C)
        quantize_w2(3, 0, 2)
        quantize_da(2, 0, B)
        quantize_w2(3, 2, 4)
        quantize_da(2, B, C)
        lay_w1(1, 0)
        lay_w1(1, 1)

        silu(3, 0, 2)
        silu(3, 2, 4)
        nc.vector.tensor_scalar_mul(
            dx_first[:].rearrange("p (b c i) -> p b c i", b=2, i=RUN), dx[:].rearrange("p (b i c) -> p b c i", b=2, i=RUN), -0.5
        )
        tanh(3, 0, B)
        scatter_on_scalar(0)
        tanh(3, B, C)
        scatter_on_scalar(1)
        for t in range(PACK):
            make_x(3, t, 0, B)
        for t in range(PACK - 1):
            make_x(3, t, B, LAST)
        quantize_w1(1)
        make_da(3, 0, B)
        make_x(3, PACK - 1, B, LAST)
        pieces = ((0, B), (B, LAST), (LAST, C))
        dx_late = [pool.tile([P, c1 - c0], F32, name=name) for (c0, c1), pool, name in zip(pieces, (side_banks, side_banks, dx_bank), ("side", "side", "dx"))]
        add_to_dx(dx_late[0], 2, 0, B)
        quantize_da(3, 0, B)
        add_to_dx(dx_late[0], 3, 0, B)
        for piece in (1, 2):
            add_to_dx(dx_late[piece], 2, *pieces[piece])
        nc.scalar.activation(
            dx_slots[2].rearrange("p (c i) -> p c i", i=RUN), dx_late[0][:].rearrange("p (i c) -> p c i", i=RUN), COPY, scale=-0.5
        )
        scatter_on_scalar(2)
        for t in range(PACK):
            make_x(3, t, LAST, C)
        for c0, c1 in pieces[1:]:
            make_da(3, c0, c1)
        for piece in (1, 2):
            c0, c1 = pieces[piece]
            quantize_da(3, c0, c1)
            add_to_dx(dx_late[piece], 3, c0, c1)
        for piece in (1, 2):
            c0, c1 = pieces[piece]
            nc.vector.tensor_scalar_mul(
                dx_slots[3][:, c0 - B : c1 - B].rearrange("p (c i) -> p c i", i=RUN),
                dx_late[piece][:].rearrange("p (i c) -> p c i", i=RUN),
                -0.5,
            )
        nc.vector.tensor_copy(result[:].indirect(listed(3)), dx_slots[3])

        for part in range(STORES):
            columns = slice(part * T // STORES, (part + 1) * T // STORES)
            (nc.sync, nc.scalar)[part % 2].dma_start(out[:, columns], result[:, columns])
